import numpy as np, ml_dtypes
CORES = [40,64,80,88,96,104,120,144]
N = 8
BF = ml_dtypes.bfloat16
def gentries(a):
    return np.ascontiguousarray(a.reshape(8, 16, -1).transpose(0, 2, 1)).reshape(8, -1)
def gtable(e):
    e = np.asarray(e); return np.ascontiguousarray(e.reshape(8, -1, 16).transpose(0, 2, 1)).reshape(128, -1).astype(np.int32)
V, H, K, Q, PO, HP = 1024, 1024, 4, 256, 3, 3
W = V + 2 * H
ALL = (N, 8, 16, V)
def bases(rng):
    return rng.integers(32, 65, (1, 1, 16, 1)) * (1 - 2 * rng.integers(0, 2, (1, 1, 16, 1)))
def sky(rng, base, c):
    main = rng.choice(np.array([0, 1, 2]), (N, 8, 1, V), p=np.array([0.45, 0.35, 0.2]))
    camp = np.where(rng.random(ALL) < 0.3, rng.integers(0, 3, ALL), main)
    t = base + np.array([-90, 0, 90])[camp] + np.rint(c * rng.integers(-40, 41, ALL)).astype(np.int64)
    d = np.clip(np.rint(c * rng.integers(32, 129, ALL)), 32, 128).astype(np.int64)
    return t, d, drifts(rng)
def drifts(rng):
    return rng.integers(-256, 257, ALL) * np.where(rng.random((N, 8, 1, V)) < 0.5, 4, 1)
def agree(rng, base, ms):
    m = rng.choice(np.array(ms), (N, 8, 1, V)); off = np.argsort(rng.random(ALL), axis=2) >= m
    far = rng.integers(150, 181, ALL) * (1 - 2 * rng.integers(0, 2, ALL))
    return base + rng.integers(-8, 9, ALL) + np.where(off, far, 0), rng.integers(112, 129, ALL)
def nets(rng):
    o = np.argsort(rng.random((N, 8, V)), axis=-1); place = np.argsort(o, axis=-1)
    mate = np.take_along_axis(o[:, :, None], ((place >> 3) << 3)[:, :, None] + rng.integers(0, 8, (N, 8, K, V)), 3)
    u = rng.random((N, 8, K, V))
    s = np.where(u < 0.55, mate, np.where(u < 0.75, rng.integers(0, V, u.shape), rng.integers(V, W, u.shape)))
    j = rng.integers(0, K, (N, 8, 1, V))
    r = np.where(rng.random((N, 8, V)) < 0.8, np.take_along_axis(s, j, 2)[:, :, 0], rng.integers(0, W, (N, 8, V)))
    return s, r
def ring(rng):
    n = rng.integers(1, HP + 4, V); last = np.add.accumulate(n); i = np.arange(V)
    c = np.searchsorted(last, i, side="right"); first = last[c] - n[c]
    nx = np.where(i + 1 < np.minimum(last[c], V), i + 1, first); o = rng.permutation(V)
    y = np.zeros(V, np.int64); y[o] = o[nx]
    return y
def pack(t, d, f, s, r):
    e = np.ascontiguousarray(s.reshape(N, 8, K, 4, Q).transpose(0, 1, 3, 2, 4)).reshape(N, 8, K * V)
    return {"th": (t * 0.015625).astype(np.float32).astype(BF).reshape(N, 128, V), "dl": (d * 0.0078125).astype(np.float32).astype(BF).reshape(N, 128, V),
            "dr": (f * 0.0000152587890625).astype(np.float32).astype(BF).reshape(N, 128, V), "sl": np.stack([gtable(a) for a in e]), "rf": np.stack([gtable(a) for a in r])}
def setup_inputs(rng):
    t, d, f = sky(rng, bases(rng), 1.0); s, r = nets(rng)
    return pack(t, d, f, s, r)
def setup_inputs_corners(rng):
    base = bases(rng); t, d = agree(rng, base, [16, 16, 16, 15, 9, 9, 8, 8, 1, 0]); tc, dc = agree(rng, base, [16]); f = drifts(rng); s, r = nets(rng)
    calm = ((np.arange(N)[:, None] + np.arange(8)) & 1) == 0
    t = np.where(calm[:, :, None, None], tc, t); d = np.where(calm[:, :, None, None], dc, d)
    pts = np.array([0, V - 1, V, V + H - 1, V + H, W - 1])
    s = np.where(rng.random(s.shape) < 0.2, rng.choice(pts, s.shape), s); u = rng.random(r.shape)
    r = np.where(u < 0.5, rng.choice(pts, r.shape), np.where(u < 0.65, np.arange(V), r))
    for q in range(N):
        for g in range(8):
            if calm[q, g]:
                y = ring(rng); s[q, g, 0] = y; r[q, g] = y
    return pack(t, d, f, s, r)
def setup_inputs_crowd(rng):
    base = bases(rng); t, d, f = sky(rng, base, 1.0); s, r = nets(rng); tc, dc = agree(rng, base, [16, 15])
    kind = (np.arange(N)[:, None] + np.arange(8) + rng.integers(0, 4)) & 3; k = kind[:, :, None, None]
    t = np.where(k < 3, tc, t); d = np.where(k < 3, dc, d)
    one = rng.integers(0, W, (N, 8, 1, 1)); one[N - 1] = V - 1; one[:, 7] = W - 1
    few = rng.integers(0, W, (N, 8, 3)); three = np.take_along_axis(few, rng.integers(0, 3, (N, 8, K * V)), 2).reshape(N, 8, K, V)
    spare = np.arange(K)[:, None] == rng.integers(0, K, (N, 8, 1, V))
    s = np.where(k == 0, one, np.where(k == 1, np.where(spare, s, one), np.where(k == 2, three, s)))
    r = np.where(kind[:, :, None] < 2, one[:, :, 0], r)
    return pack(t, d, f, s, r)
def setup_inputs_ends(rng):
    t, d, f = sky(rng, bases(rng), 1.0); s, r = nets(rng); one = (N, 8, 1, V)
    flip = np.where(rng.random(ALL) < 0.25, -1, 1)
    t = np.where(rng.random(one) < 0.8, 256 * (1 - 2 * rng.integers(0, 2, one)) * flip, t)
    d = np.where(rng.random(one) < 0.8, rng.choice(np.array([32, 128]), ALL), d)
    f = np.where(rng.random(one) < 0.8, 1024 * (1 - 2 * rng.integers(0, 2, ALL)), f)
    s = np.where(rng.random(s.shape) < 0.7, rng.choice(np.array([0, W - 1]), s.shape), s)
    r = np.where(rng.random(r.shape) < 0.7, rng.choice(np.array([0, W - 1]), r.shape), r)
    v = np.arange(V); ix = v[(v % Q < 4) | (v % Q >= Q - 4)]; odd = (ix & 1) == 1; n = (N, 8, len(ix))
    t[..., ix] = np.where(odd, -256, 256); d[..., ix] = 128; f[..., ix] = np.where((ix & 2) == 2, -1024, 1024)
    for j in range(K):
        a, b = rng.choice(ix[odd], n), rng.choice(ix[~odd], n)
        s[:, :, j, ix] = np.where(odd, a, b) if j < K - 1 else np.where(odd, b, a)
    return pack(t, d, f, s, r)
def setup_inputs_spread(rng):
    c = np.exp2(rng.integers(-1, 2, (N, 8, 1, V)).astype(np.float64)); t, d, f = sky(rng, bases(rng), c); s, r = nets(rng)
    f = rng.integers(-256, 257, ALL) * (1 << rng.integers(0, 3, (N, 8, 1, V)))
    s = np.where(rng.random((N, 8, 1, V)) < 0.4, (W * rng.random(s.shape) ** 3).astype(np.int64), s)
    return pack(t, d, f, s, r)
def setup_inputs_ties(rng):
    base = rng.choice(np.array([-64, -32, 32, 64]), (1, 1, 16, 1)); s, r = nets(rng)
    main = rng.integers(-3, 4, (N, 8, 1, V)); t = base + 32 * np.where(rng.random(ALL) < 0.3, rng.integers(-3, 4, ALL), main)
    d = rng.choice(np.array([32, 64, 128]), ALL)
    f = rng.choice(np.array([0, 0, 0, 0, 0, 0, 0, 1, -1, 1024, -1024]), (N, 8, 1, V)) * rng.integers(0, 2, ALL)
    return pack(t, d, f, s, r)
def check_ranges(d):
    bad = []
    for k, lo, hi, u in (("th", -4.0, 4.0, 64.0), ("dl", 0.25, 1.0, 128.0), ("dr", -0.015625, 0.015625, 65536.0)):
        v = np.asarray(d[k]).astype(np.float64)
        if not (np.min(v) >= lo and np.max(v) <= hi): bad.append("range of " + k)
        elif np.any(np.rint(v * u) != v * u): bad.append("multiples of " + k)
    for k in ("sl", "rf"):
        if np.min(d[k]) < 0 or np.max(d[k]) > W - 1: bad.append("range of " + k)
    return bad
def view(a):
    return np.concatenate([a, np.roll(a, -1, axis=0)[..., :H], np.roll(a, -1, axis=1)[..., :H]], axis=3)
def reference(th, dl, dr, sl, rf):
    x, e, f = [a.astype(np.float64).reshape(N, 8, 16, V) for a in (th, dl, dr)]
    S = np.stack([gentries(a) for a in sl]).astype(np.int64).reshape(N, 8, 4, K, Q).transpose(0, 1, 3, 2, 4).reshape(N, 8, K, V)
    R = np.stack([gentries(a) for a in rf]).astype(np.int64)
    away = np.broadcast_to(np.arange(V, W), (N, 8, 2 * H))
    for poll in range(PO):
        ids = np.concatenate([np.arange(Q) + (poll & 1) * Q, np.arange(Q) + (2 + (poll & 1)) * Q])
        xw, ew, Sw = view(x), view(e), view(S); Sp = S[..., ids]; xo, eo = x[..., ids], e[..., ids]
        lo, hi = [], []
        for j in range(K):
            ix = Sp[:, :, j][:, :, None, :]; a = np.take_along_axis(xw, ix, 3); b = np.take_along_axis(ew, ix, 3)
            lo.append(a - b); hi.append(a + b)
        lo.append(xo - eo); hi.append(xo + eo)
        cnt = []
        for a in lo:
            c = np.zeros(a.shape, np.int64)
            for b, h in zip(lo, hi): c += (b <= a) & (a <= h)
            cnt.append(c)
        best = np.maximum.reduce(cnt)
        A = np.maximum.reduce([np.where(c == best, a, -64.0) for c, a in zip(cnt, lo)])
        hold = [(b <= A) & (A <= h) for b, h in zip(lo, hi)]
        B = np.minimum.reduce([np.where(m, h, 64.0) for m, h in zip(hold, hi)])
        n = np.stack([np.add.reduce(m.astype(np.int64), axis=2) for m in hold[:K]], axis=2)
        stay = n >= 9; score = np.where(stay, n, 0); top = np.argmax(score, axis=2); some = np.max(score, axis=2) > 0
        cand = np.take_along_axis(Sp, top[:, :, None], 2)[:, :, 0]
        Rw = np.concatenate([R, away], axis=2); h = cand; meet = h == ids
        for hop in range(HP):
            h = np.take_along_axis(Rw, h, 2); meet = meet | (h == ids)
        veto = some & meet
        fall = ~stay | (veto[:, :, None] & (np.arange(K)[:, None] == top[:, :, None]))
        w = np.where(some & ~meet, cand, R[..., ids]); ww = w[:, :, None]
        nm = np.take_along_axis(Sw, ww, 3)
        new = np.where(ww < V, nm, np.where(ww < V + H, V, V + H) + nm)
        Sn = np.where(fall & ((ww < V) | (nm < H)), new, Sp)
        x = x + f; e = e + 0.0625
        x[..., ids] = A + 0.5 * (B - A); e[..., ids] = 0.5 * (B - A) + 0.0625
        S = np.array(S); S[..., ids] = Sn; R = np.array(R); R[..., ids] = w
    xw, ew = view(x), view(e); y = 0.5 * e
    for j in range(K):
        ix = S[:, :, j][:, :, None, :]; z = np.take_along_axis(xw, ix, 3) - x
        y = y + np.take_along_axis(ew, ix, 3) * np.reciprocal(1.0 + np.exp(-z))
    return {"yt": x.reshape(N, 128, V).astype(np.float32), "yq": y.reshape(N, 128, V).astype(np.float32), "yr": np.asarray(R, np.float32)}

def check_inputs(d):
    bad = list(check_ranges(d))
    if not bad:
        for name, y in reference(**d).items():
            for q in range(N):
                v = np.abs(np.asarray(y[q], np.float64)); s = np.sqrt(np.mean(v * v))
                if v.max() > 11 * s or s < 2.0 ** -2: bad.append('%s of rank %d is uneven or too small' % (name, q))
    return bad

@@ -1,0 +1,811 @@
+from concourse.bass import DstId, RemoteDMATransfer
+from concourse.mybir import AluOpType as Op, ActivationFunctionType as Fn
+
+C = 256
+PART = 2048
+SENT = 3 * PART
+KEY = 8192.0
+f32, b16, i32, u16 = "float32", "bfloat16", "int32", "uint16"
+
+
+def _s(shape, d):
+    return ("sbuf", [128] + shape, d)
+
+
+SCRATCH = {
+    "TH": _s([3072], b16), "DL": _s([3072], b16), "DR": _s([1024], b16),
+    "W1": _s([3 * PART], f32), "W2": _s([3 * PART], f32), "W3": _s([3 * PART], f32),
+    "M0": _s([SENT + 32], b16), "M1": _s([SENT + 32], b16), "M2": _s([SENT + 32], b16),
+    "SLI": _s([2, 2, 64], i32), "RFI": _s([2, 2, 16], i32), "SLB": _s([2, 2, 64], i32), "RFB": _s([2, 2, 16], i32),
+    "XI": _s([144], f32), "PI": _s([8], i32), "PJ": _s([8], i32), "COL": _s([8], f32),
+    "E16": _s([16], f32), "KM": _s([8], f32),
+    "IP": _s([128], b16), "IM": _s([128], b16), "IP16": _s([128], b16), "IM16": _s([128], b16),
+    "I34": _s([128], b16), "IVE": _s([128], b16), "IF": _s([128], f32), "IQ": _s([128], f32),
+    "TN": _s([144], f32), "TNP": _s([144], b16), "TNM": _s([144], b16), "TJ": _s([5, 144], b16),
+    "PV": _s([2, 96], f32),
+    "SP": _s([2, 4, 2, 16], f32), "R2": _s([2, 2, 32], f32),
+    "OF0": _s([2, 64], u16), "OFW": _s([2, 2, 64], u16), "OFH": _s([4, 32], u16),
+    "IA": _s([64], i32), "IB": _s([64], i32),
+    "DRP": _s([512], f32), "DR2": _s([512], f32), "T0": _s([512], f32),
+    "LO0": _s([5 * C], f32), "LO1": _s([5 * C], f32), "HI0": _s([5 * C], f32), "HI1": _s([5 * C], f32),
+    "TG": _s([2, 4 * C], b16), "DG": _s([2, 4 * C], b16),
+    "LL": _s([10 * C], b16), "LH": _s([20 * C], b16), "CH": _s([5 * C], b16), "CL": _s([4 * C], b16),
+    "E1": _s([2 * C], f32), "E2": _s([2 * C], f32), "MM": _s([C], f32), "AB": _s([2 * C], f32),
+    "GH": _s([4, 512], b16),
+    "SC": _s([4, 2, 16], f32), "KS": _s([4, 2, 16], f32), "K2": _s([2, 32], f32),
+    "MXI": _s([32], i32), "CI": _s([32], i32), "C2": _s([2, 32], f32),
+    "U1": _s([64], f32), "U2": _s([64], f32), "FC": _s([32], f32), "SM": _s([32], f32), "NV": _s([32], f32),
+    "EQ": _s([4, 32], f32), "OK": _s([32], f32), "UU": _s([32], f32),
+    "ST": _s([128], b16), "VE": _s([128], b16), "F1": _s([32], b16), "F2": _s([32], b16),
+    "S2": _s([128], f32), "TK": _s([128], f32), "DD": _s([128], f32),
+    "SH": _s([4, 32], b16), "SO": _s([4, 32], b16), "RH": _s([32], b16), "RO": _s([32], b16), "RS": _s([32], f32),
+    "TI": _s([2, 2, 16, 32], b16),
+    "P0": _s([4 * C], f32), "P1": _s([4 * C], f32),
+    "SV": _s([1024], f32), "YT": _s([1024], f32), "YQ": _s([1024], f32), "RN": _s([64], f32), "YR": _s([128], f32),
+    "PL": ("psum", [128, 1536], f32), "PH": ("psum", [128, 1536], f32),
+    "PA": ("psum", [128, 512], f32), "PN": ("psum", [128, 512], f32),
+}
+NCALL = 16
+SEMAPHORES = (["V", "A", "P", "G", "sent", "out", "cp1", "cp2", "aT", "aW1", "aW2", "aW3", "aM0", "aM1", "aM2",
+               "lt0", "lt1", "ld0", "ld1", "ldr", "lsl", "lrf"] + ["r%d" % k for k in range(NCALL)])
+
+
+def pieces():
+    def two(sem, buf, a, b, n):
+        return (sem, [(buf, a, n), (buf, b, n)])
+    out = [("aT", [("TH", h * 512, 512), ("DL", h * 512, 512)]) for h in range(2)]
+    out += [two("aM0", "M0", 0, 1024, 1024), two("aW1", "W1", 512, 1536, 512)]
+    for t in range(3):
+        w, p = "W%d" % (t + 1), t & 1
+        x, y = p * 512, (2 + p) * 512
+        out.append(two("a" + w, w, x, x + C, C))
+        if t:
+            out.append(two("aM%d" % t, "M%d" % t, (1 - p) * 512, (3 - p) * 512, 512))
+        if t == 2:
+            out.append(two("a" + w, w, y, y + C, C))
+            break
+        out.append(two("a" + w, w, y, y + C // 2, C // 2))
+        out.append(two("a" + w, w, y + C, y + C + C // 2, C // 2))
+        out.append(two("aW%d" % (t + 2), "W%d" % (t + 2), x, y, 512))
+    return out
+
+
+def part_width(buf):
+    return 1024 if buf in ("TH", "DL") else PART
+
+
+def route(T, topo, r):
+    src, dst = T.cores[r], T.cores[(r - 1) % len(T.cores)]
+    able = [c for c in topo.cores_of(src) if c != src and T.rank_of(c) is None and topo.may_write(c, dst)]
+    far = [c for c in able if topo.die(c) != topo.die(src)][0]
+    if topo.may_write(src, dst):
+        out = topo.engines(src, dst)
+        return dst, [(dst, out), (far, [e for e in topo.engines(src, far) if e not in out])]
+    near = [c for c in able if topo.die(c) == topo.die(src)][0]
+    eng = topo.engines(src, near)
+    return dst, [(near, eng[:len(eng) // 2]), (far, eng[len(eng) // 2:])]
+
+
+def bits(engines):
+    return sum(1 << e for e in engines)
+
+
+def share(engines, k):
+    n = len(engines) // 2
+    return engines[k * n:(k + 1) * n] if k < 2 else engines
+
+
+def relay_program(g, core, T, topo, r, h):
+    dst, halves = route(T, topo, r)
+    rid, pid = topo.addr(dst, core)
+    sent = 0
+    for k, (sem, two) in enumerate(pieces()):
+        buf, a, n = two[h]
+        a += part_width(buf)
+        eng = share(topo.engines(core, dst), k)
+        g.wait_ge(T.sem["r%d" % k], len(halves[h][1]))
+        g.remote_dma(T[buf][:, a:a + n], T[buf][:, a:a + n], T.sem[sem], T.sem.sent, pid, rid, bits(eng))
+        sent += len(eng)
+    g.wait_ge(T.sem.sent, sent)
+
+
+def rank_program(g, core, T, topo):
+    rank = T.rank_of(core)
+    n_ranks = len(T.cores)
+    if rank is None:
+        for r in range(n_ranks):
+            for h, (c, _) in enumerate(route(T, topo, r)[1]):
+                if c == core:
+                    relay_program(g, core, T, topo, r, h)
+        return
+    ops = []
+    total = {}
+
+    def op(q, fn, rd=(), wr=(), bk=(), dma=None, whole=()):
+        ops.append([q, fn, list(rd), list(wr), list(bk), dma, list(whole)])
+        if dma:
+            total[dma[0]] = total.get(dma[0], 0) + dma[1]
+
+    def tt(out, a, b, o, rd, wr, bk=(), whole=()):
+        op("V", lambda: g.vector.tensor_tensor(out, a, b, o), rd, wr, bk, None, whole)
+
+    def ts(out, a, s1, o0, rd, wr, s2=None, o1=None, bk=(), whole=()):
+        if s2 is None:
+            op("V", lambda: g.vector.tensor_scalar(out, a, s1, None, o0), rd, wr, bk, None, whole)
+        else:
+            op("V", lambda: g.vector.tensor_scalar(out, a, s1, s2, o0, o1), rd, wr, bk, None, whole)
+
+    def cp(out, a, rd, wr, bk=(), whole=()):
+        op("V", lambda: g.vector.tensor_copy(out, a), rd, wr, bk, None, whole)
+
+    def act(out, a, rd, wr, bk=(), bias=0.0, scale=1.0, fn=Fn.Identity, whole=()):
+        op("A", lambda: g.scalar.activation(out, a, fn, bias=bias, scale=scale), rd, wr, bk, None, whole)
+
+    def mm(lst, rd, bk):
+        def emit():
+            for m in lst:
+                last = g.tensor.matmul(*m)
+            return last
+        op("P", emit, rd, (), bk)
+
+    def dma(q, out, a, sem, rd, wr=(), whole=()):
+        e = g.sync if q == "S" else g.scalar
+        op(q, lambda: e.dma_start(out, a).then_inc(T.sem[sem], 16), rd, wr, (), (sem, 16), whole)
+
+    dst, halves = route(T, topo, rank)
+    plan = pieces()
+    for k, (sem, two) in enumerate(plan):
+        for c, e in route(T, topo, (rank + 1) % n_ranks)[1]:
+            total[sem] = total.get(sem, 0) + len(e if c == core else share(topo.engines(c, core), k))
+    called = [0]
+
+    def send(rd, shift=True, after=()):
+        k = called[0]
+        called[0] += 1
+        sem, two = plan[k]
+        trs = []
+        for (buf, a, n), (to, eng) in zip(two, halves):
+            rid, pid = topo.addr(to, core)
+            b = a + part_width(buf)
+            trs.append(RemoteDMATransfer(dst_ids=[DstId(rid=rid, pnc=pid)], dma_engine_mask=bits(eng),
+                                         remote_sem=T.sem[sem if to == dst else "r%d" % k],
+                                         src=T[buf][:, a:a + n], dst=T[buf][:, b:b + n]))
+        op("G", lambda: g.remote_dma_fused(trs, local_sem=T.sem.sent), rd, (), (), ("sent", sum(len(e) for _, e in halves)), after)
+        if shift:
+            (buf, a, n), (_, a2, n2) = two
+            for s, m in ([(a, n + n2)] if a + n == a2 else [(a, n), (a2, n2)]):
+                b = s + 2 * PART
+                dma("S", T[buf][0:112, b:b + m], T[buf][16:128, s:s + m], sem, rd, (), after)
+                dma("S", T[buf][112:128, b:b + m], T[buf][0:16, s:s + m], sem, rd)
+
+    W = [None, T.W1, T.W2, T.W3]
+    M = [T.M0, T.M1, T.M2]
+    LO, HI = [T.LO0, T.LO1], [T.HI0, T.HI1]
+    PL, PH, PA, PN = T.PL, T.PH, T.PA, T.PN
+    THK, DLK = ["TH0", "TH1"], ["DL0", "DL1"]
+
+    for h in range(2):
+        v = slice(h * 512, (h + 1) * 512)
+        dma("S", T.TH[:, v], T.th[:, v], "lt%d" % h, (), [THK[h]])
+        dma("A", T.DL[:, v], T.dl[:, v], "ld%d" % h, (), [DLK[h]])
+    op("G", lambda: g.iota(T.PI[:], [[0, 8]], 0, 1), (), ["PI"])
+    op("G", lambda: g.iota(T.XI[:], [[1, 144]], 0, 0, allow_small_or_imprecise_dtypes=True), (), ["XI"])
+    for h in range(2):
+        send([THK[h], DLK[h]], shift=False)
+    for par in range(2):
+        op("G", lambda par=par: g.iota(T.PV[:, par, :], [[0, 3], [1024, 2], [32, 16]], 512 * par, 0,
+                                       allow_small_or_imprecise_dtypes=True), (), ["PV%d" % par])
+    dma("S", T.SLI[:], T.sl[:], "lsl", (), ["SLI"])
+    dma("S", T.RFI[:], T.rf[:], "lrf", (), ["RFI"])
+    for buf, src in ((T.TH, T.th), (T.DL, T.dl)):
+        dma("S", buf[0:112, 2048:3072], src[16:128, :], "aT", ())
+        dma("S", buf[112:128, 2048:3072], src[0:16, :], "aT", ())
+    dma("S", T.DR[:], T.dr[:], "ldr", (), ["DR"])
+    op("V", lambda: g.vector.memset(T.TI[:], 0.0), (), ["TI0", "TI1"])
+    for t in range(3):
+        op("V", lambda t=t: g.vector.memset(M[t][:, SENT:SENT + 32], float(SENT // 2)), (), ["Ms%d" % t])
+    for k, m in ((0, 127), (1, 15), (2, 31), (3, 16), (4, 112)):
+        ts(T.PJ[:, k:k + 1], T.PI[:, k:k + 1], m, Op.bitwise_and, ["PI"], ["PJ%d" % k])
+    cp(T.COL[:, 0:5], T.PJ[:, 0:5], ["PJ%d" % k for k in range(5)], ["C0"])
+    ts(T.COL[:, 5:6], T.COL[:, 3:4], -2.0, Op.mult, ["C0"], ["C5"], 16.0, Op.add)
+    ts(T.COL[:, 4:5], T.COL[:, 4:5], 15.0, Op.add, ["C0"], ["C4"])
+    act(T.COL[:, 6:7], T.COL[:, 0:1], ["C0"], ["C6"], scale=0.0, fn=Fn.Sigmoid)
+    act(T.COL[:, 7:8], T.COL[:, 6:7], ["C6"], ["C7"], scale=0.5)
+    for buf, key, v in ((T.IP, "IP", 1.0), (T.IM, "IM", -1.0), (T.IP16, "IP16", 16.0), (T.IM16, "IM16", -16.0), (T.IF, "IF", 1.0)):
+        ts(buf[:], T.XI[:, 0:128], T.COL[:, 0:1], Op.is_equal, ["XI", "C0"], [key], v, Op.mult)
+    ts(T.TN[:], T.XI[:], T.COL[:, 4:5], Op.is_equal, ["XI", "C4"], ["TN"])
+    ts(T.E16[:], T.XI[:, 0:16], T.COL[:, 1:2], Op.is_equal, ["XI", "C0"], ["E16"])
+    tt(T.KM[:, 0:4], T.E16[:, 0:4], T.E16[:, 4:8], Op.add, ["E16"], ["KM"])
+    tt(T.KM[:, 4:5], T.E16[:, 8:9], T.E16[:, 9:10], Op.add, ["E16"], ["KM4"])
+
+    def constants():
+        act(T.TNP[:], T.TN[:], ["TN"], ["TNP"], scale=4 * KEY)
+        act(T.TNM[:], T.TN[:], ["TN"], ["TNM"], scale=-4 * KEY)
+        for k in range(5):
+            act(T.TJ[:, k, :], T.TN[:], ["TN", "KM", "KM4"], ["TJ%d" % k], scale=T.KM[:, k:k + 1])
+        act(T.IQ[:], T.IF[:], ["IF", "C7"], ["IQ"], scale=T.COL[:, 7:8])
+        act(T.I34[:], T.IF[:], ["IF"], ["I34"], scale=0.75)
+        act(T.IVE[:], T.IF[:], ["IF"], ["IVE"], scale=-2 * KEY)
+    constants()
+
+    def drifts():
+        for x in range(2):
+            act(T.DRP[:, x * C:(x + 1) * C], T.DR[:, 2 * x * C:(2 * x + 1) * C], ["DR"], ["DRP%d" % x], bias=0.125)
+            act(T.DR2[:, x * C:(x + 1) * C], T.DR[:, (2 * x + 1) * C:(2 * x + 2) * C], ["DR"], ["DR2%d" % x], bias=0.125, scale=2.0)
+
+    def offsets(par):
+        for x in range(2):
+            cp(T.OFW[:, par, x, :], T.SP[:, par, :, x, :], ["SP%d" % par], ["OFW%d%d" % (par, x)])
+
+    def place(out, off_i, off_f, rd, wr):
+        ts(T.IB[:, 0:32], off_i, 240, Op.bitwise_and, rd, ["IB"])
+        ts(T.U1[:, 0:32], off_f, 2.0 * PART, Op.is_ge, rd, ["U1"], T.COL[:, 5:6], Op.mult)
+        tt(T.U1[:, 32:64], T.IB[:, 0:32], off_f, Op.add, rd + ["IB"], ["U1b"])
+        tt(T.U2[:, 0:32], T.U1[:, 0:32], T.U1[:, 32:64], Op.add, ["U1", "U1b"], ["U2"])
+        ts(out, T.U2[:, 0:32], T.COL[:, 3:4], Op.add, ["U2", "C0"], wr)
+
+    def flags(par):
+        ts(T.F1[:], T.R2[:, par, 0, :], float(PART), Op.is_ge, ["R2%d" % par], ["F1"], KEY, Op.mult)
+        ts(T.F2[:], T.R2[:, par, 0, :], 2.0 * PART, Op.is_ge, ["R2%d" % par], ["F2"], float(PART), Op.mult)
+
+    def names_high(par):
+        act(T.SH[:], T.SP[:, par], ["SP%d" % par], ["SH"])
+        tt(T.U2[:, 0:32], T.F1[:], T.R2[:, par, 1, :], Op.add, ["F1", "R2%d" % par], ["U2"])
+        ts(T.RS[:], T.U2[:, 0:32], float(SENT), Op.min, ["U2"], ["RS"])
+        act(T.RH[:], T.RS[:], ["RS"], ["RH"])
+
+    def names_low(par):
+        tt(T.SO[:], T.SP[:, par], T.SH[:], Op.subtract, ["SP%d" % par, "SH"], ["SO"])
+        tt(T.RO[:], T.RS[:], T.RH[:], Op.subtract, ["RS", "RH"], ["RO"])
+        ti = "TI%d" % par
+        keys = [ti + "_%d" % k for k in range(10)]
+        for j in range(4):
+            act(T.TI[:, par, :, :, j], T.SH[:, j, :], ["SH", ti], [keys[j]])
+        act(T.TI[:, par, :, :, 8], T.RH[:], ["RH", ti], [keys[8]])
+        for j in range(4):
+            act(T.TI[:, par, :, :, 4 + j], T.SO[:, j, :], ["SO", ti], [keys[4 + j]])
+        act(T.TI[:, par, :, :, 9], T.RO[:], ["RO", ti], [keys[9]])
+        act(T.TI[:, par, :, :, 16:26], T.TI[:, par, :, :, 0:10], keys + [ti], [ti + "d"])
+
+    def names_out(par, t):
+        ti = "TI%d" % par
+        for x in range(2):
+            a = 2 * x + par
+            op("V", lambda x=x, a=a: g.vector.transpose(M[t][:, a * 512:(a + 1) * 512], T.TI[:, par, x]),
+               [ti, ti + "d"] + [ti + "_%d" % k for k in range(10)], ["M%d_%d" % (t, a)])
+        if t:
+            send(["M%d_%d" % (t, par), "M%d_%d" % (t, 2 + par)])
+
+    def carry(t, par):
+        for part in range(3):
+            for x in range(2):
+                a = part * PART + (2 * x + par) * 512
+                dma("S", M[t][:, a:a + 512], M[t - 1][:, a:a + 512], "cp%d" % t,
+                    ["M%d_%d" % (t - 1, 2 * x + par)], (), ["aM%d" % (t - 1)])
+
+    cp(T.OF0[:], T.SLI[:, :, 0, :], ["SLI"], ["OF0"])
+    ts(T.SLB[:], T.SLI[:], 3840, Op.bitwise_and, ["SLI"], ["SLB"])
+    ts(T.RFB[:], T.RFI[:], 3840, Op.bitwise_and, ["RFI"], ["RFB"])
+    for par in range(2):
+        for x in range(2):
+            tt(T.SP[:, par, :, x, :], T.SLI[:, x, par, :], T.SLB[:, x, par, :], Op.add, ["SLI", "SLB"], ["SP%d" % par])
+        tt(T.R2[:, par, 0, :], T.RFI[:, :, par, :], T.RFB[:, :, par, :], Op.add, ["RFI", "RFB"], ["R2%d" % par])
+        cp(T.IA[:, 0:32], T.R2[:, par, 0, :], ["R2%d" % par], ["IA"])
+        place(T.R2[:, par, 1, :], T.IA[:, 0:32], T.IA[:, 0:32], ["IA", "C5"], ["R2%d" % par])
+        flags(par)
+        names_high(par)
+        offsets(par)
+        names_low(par)
+    ts(T.PV[:], T.PV[:], T.COL[:, 2:3], Op.add, ["PV0", "PV1", "C0"], ["PV"])
+    names_out(0, 0)
+    names_out(1, 0)
+    send(["M0_%d" % a for a in range(4)], after=["aT"])
+    for ps, sign, b in ((PA, T.IM, 6), (PN, T.IP, 7)):
+        for x in range(2):
+            v, u = slice((2 * x + 1) * C, (2 * x + 2) * C), slice(x * C, (x + 1) * C)
+            mm([(ps[:, u], T.IP[:], T.TH[:, v], True, False), (ps[:, u], sign[:], T.DL[:, v], False, False),
+                (ps[:, u], T.IP[:], T.DR[:, v], False, True)], THK + DLK + ["DR", "IP", "IM"], [b])
+
+    def first_drift():
+        for k, (ps, b) in enumerate(((PA, 6), (PN, 7))):
+            for x in range(2):
+                a = 2 * x + 1
+                act(T.W1[:, a * 512 + k * C:a * 512 + (k + 1) * C], ps[:, x * C:(x + 1) * C], (), ["W1_%d%s" % (a, "lh"[k])], [b])
+        send(["W1_1l", "W1_1h", "W1_3l", "W1_3h"], after=["aT"])
+
+    def wkeys(t):
+        return ["W%d_%d%s" % (t, a, s) for a in range(4) for s in "lh"]
+
+    BANKS = [(0, 2), (2, 4), (4, 5)]
+
+    def fetch(t, x):
+        par = t & 1
+        lo, lk = LO[x], "LO%d" % x
+        if t == 0:
+            off = T.OF0[:, x, :]
+            if x == 0:
+                for b in range(2):
+                    v, off = slice(b * 512, (b + 1) * 512), T.OF0[:, x, 32 * b:32 * b + 32]
+                    cp(T.TG[:, x, v], T.TH[:].indirect(off), THK + ["OF0"], ["TG0%d" % b], whole=["aT"])
+                    act(T.DG[:, x, v], T.DL[:].indirect(off), DLK + ["OF0"], ["DG0%d" % b], whole=["aT"])
+            else:
+                act(T.TG[:, x, :], T.TH[:].indirect(off), THK + ["OF0"], ["TG10", "TG11"], whole=["aT"])
+                act(T.DG[:, x, :], T.DL[:].indirect(off), DLK + ["OF0"], ["DG10", "DG11"], whole=["aT"])
+            return
+        rd, wh, ok = wkeys(t), ["aW%d" % t], "OFW%d%d" % (par, x)
+        wl, whi = W[t][:, 0:3 * PART], W[t][:, C:3 * PART]
+        if x == 0:
+            cp(lo[:, 0:2 * C], wl.indirect(T.OFW[:, par, x, 0:32]), rd + [ok], [lk + "0"], whole=wh)
+            act(lo[:, 2 * C:4 * C], wl.indirect(T.OFW[:, par, x, 32:64]), rd + [ok], [lk + "1"], whole=wh)
+            lay_lo(t, x, [0, 1])
+            base(t, x, 0, [0, 1])
+        else:
+            act(lo[:, 0:4 * C], wl.indirect(T.OFW[:, par, x, :]), rd + [ok], [lk + "0", lk + "1"], whole=wh)
+        act(HI[x][:, 0:4 * C], whi.indirect(T.OFW[:, par, x, :]), rd + [ok], ["HI%d0" % x, "HI%d1" % x], bias=0.125, whole=wh)
+
+    def own(t, x):
+        a = 2 * x + (t & 1)
+        act(LO[x][:, 4 * C:5 * C], W[t][:, a * 512:a * 512 + C], ["W%d_%dl" % (t, a)], ["LO%d2" % x])
+        act(HI[x][:, 4 * C:5 * C], W[t][:, a * 512 + C:a * 512 + 512], ["W%d_%dh" % (t, a)], ["HI%d2" % x], bias=0.125)
+
+    def region(x, k):
+        return (PL, 0) if (x + k) & 1 == 0 else (PH, 3)
+
+    def from_pair(x, out, bank, b, sign, stop):
+        a, v = 2 * x, slice(BANKS[b][0] * C, BANKS[b][1] * C)
+        if b < 2:
+            th, dl, rd = T.TG[:, x, v], T.DG[:, x, v], ["TG%d%d" % (x, b), "DG%d%d" % (x, b)]
+        else:
+            th, dl, rd = T.TH[:, a * C:(a + 1) * C], T.DL[:, a * C:(a + 1) * C], THK + DLK
+        mm([(out, T.IP[:], th, True, False), (out, sign[:], dl, False, stop)], rd + ["IP", "IM"], [bank])
+
+    def lay_lo(t, x, banks):
+        lo, lk = LO[x], "LO%d" % x
+        ps, b0 = region(x, 0)
+        for b in banks:
+            v = slice(BANKS[b][0] * C, BANKS[b][1] * C)
+            if t == 0:
+                from_pair(x, ps[:, v], b0 + b, b, T.IM, True)
+                if x == 0 and b == 0:
+                    cp(lo[:, v], ps[:, v], (), [lk + str(b)], [b0 + b])
+                else:
+                    act(lo[:, v], ps[:, v], (), [lk + str(b)], [b0 + b])
+            elif x == 0 and b == 0:
+                cp(ps[:, v], lo[:, v], [lk + str(b)], ["L0"], [b0 + b])
+            else:
+                act(ps[:, v], lo[:, v], [lk + str(b)], (), [b0 + b])
+
+    def first_hi(x, banks):
+        for b in banks:
+            v = slice(BANKS[b][0] * C, BANKS[b][1] * C)
+            out, bank = ((PA[:], 6), (PN[:], 7), (PA[:, 0:C], 6))[b]
+            from_pair(x, out, bank, b, T.IP, True)
+            act(HI[x][:, v], out, (), ["HI%d%d" % (x, b)], [bank])
+
+    def base(t, x, high, banks):
+        ps, b0 = region(x, 1 - high)
+        for b in banks:
+            v = slice(BANKS[b][0] * C, BANKS[b][1] * C)
+            if t == 0:
+                from_pair(x, ps[:, v], b0 + b, b, T.IP if high else T.IM, False)
+            else:
+                src, key = (HI[x], "HI%d%d" % (x, b)) if high else (LO[x], "LO%d%d" % (x, b))
+                mm([(ps[:, v], T.IF[:], src[:, v], True, False)], [key, "IF"], [b0 + b])
+
+    def spans(first, count):
+        return [(max(first, p), min(first + count, q), b) for b, (p, q) in enumerate(BANKS) if max(first, p) < min(first + count, q)]
+
+    def banks_of(first, count, b0):
+        return [b0 + b for _, _, b in spans(first, count)]
+
+    def chunk(t, x, hook):
+        par = t & 1
+        a = 2 * x + par
+        lo, lks = LO[x], ["LO%d%d" % (x, b) for b in range(3)]
+        hi, hks = HI[x], ["HI%d%d" % (x, b) for b in range(3)]
+        (PO, ob), (PS, sb) = region(x, 0), region(x, 1)
+        steps = [("D", s) for s in range(1, 5)] + [("U", s) for s in range(1, 5)]
+        last = {0: ("U", 1), 1: ("U", 3), 2: ("U", 4)}
+
+        def add(src, p, first, n, wt, key, step):
+            for lo_, hi_, b in spans(first, n):
+                mm([(PS[:, lo_ * C:hi_ * C], wt[:], src[:, (p + lo_ - first) * C:(p + hi_ - first) * C], False, last[b] == step)],
+                   [key, "IP16", "IM16"], [sb + b])
+        pos = 0
+        for s in range(1, 5):
+            n = 5 - s
+            tt(T.LL[:, pos * C:(pos + n) * C], PO[:, 0:n * C], lo[:, s * C:5 * C], Op.is_le, lks + ["L0"], ["LL%d" % s], banks_of(0, n, ob))
+            add(T.LL, pos, 0, n, T.IM16, "LL%d" % s, None)
+            add(T.LL, pos, s, n, T.IP16, "LL%d" % s, None)
+            pos += n
+        hook("ll")
+        pos = 0
+        for kind, s in steps:
+            n, key = 5 - s, "LH%s%d" % (kind, s)
+            out = T.LH[:, pos * C:(pos + n) * C]
+            if kind == "D":
+                tt(out, PO[:, 0:n * C], hi[:, s * C:5 * C], Op.is_le, hks, [key], banks_of(0, n, ob))
+                add(T.LH, pos, 0, n, T.IP16, key, (kind, s))
+            else:
+                tt(out, PO[:, s * C:5 * C], hi[:, 0:n * C], Op.is_gt, hks, [key], banks_of(s, n, ob))
+                add(T.LH, pos, s, n, T.IM16, key, (kind, s))
+            pos += n
+            if (kind, s) == ("U", 1):
+                act(T.E1[:], PS[:, 0:2 * C], (), ["E1"], [sb])
+            hook(kind + str(s))
+        base(t, x, 1, [0, 1, 2])
+        spare = PS[:, 5 * C:6 * C]
+        tt(T.E2[:], PS[:, 2 * C:4 * C], T.E1[:], Op.max, ["E1"], ["E2"], [sb + 1])
+        hook("m")
+        tt(spare, PS[:, 4 * C:5 * C], T.E2[:, 0:C], Op.max, ["E2"], ["sp"], [sb + 2])
+        hook("m")
+        tt(T.MM[:], spare, T.E2[:, C:2 * C], Op.max, ["E2", "sp"], ["MM"], [sb + 2])
+        hook("m")
+        big = 1.5 * 2.0 ** 27
+        ts(spare, T.MM[:], big, Op.add, ["MM"], ["sp"], -big, Op.add, [sb + 2])
+        hook("m")
+        if t < 2:
+            A, B = W[t + 1][:, a * 512:a * 512 + C], W[t + 1][:, a * 512 + C:a * 512 + 512]
+            ak, bk_ = "W%d_%dl" % (t + 1, a), "W%d_%dh" % (t + 1, a)
+        else:
+            B, bk_ = T.AB[:, C:2 * C], "ABb"
+        pa = PA[:, x * C:(x + 1) * C]
+        tt(pa, T.MM[:], spare, Op.subtract, ["MM", "sp"], ["pa"], [sb + 2, 6])
+        if x == 1 and t < 2:
+            tt(A, T.MM[:], spare, Op.subtract, ["MM", "sp"], [ak], [sb + 2])
+            send([ak])
+        hook("A")
+        for b, (p, q) in enumerate(BANKS):
+            for r in range(p, q):
+                tt(T.CH[:, r * C:(r + 1) * C], pa, hi[:, r * C:(r + 1) * C], Op.is_gt, hks + ["pa"], ["CH%d" % r], [6])
+            mm([(PO[:, p * C:q * C], T.IP16[:], T.CH[:, p * C:q * C], False, True)], ["CH%d" % r for r in range(p, q)] + ["IP16"], [ob + b])
+            if b == 0:
+                act(T.E1[:], PO[:, 0:2 * C], (), ["E1"], [ob])
+        hook("pen")
+        n_ps = PN[:, x * 64:(x + 1) * 64]
+        mm([(n_ps, T.TNM[:, 15 - i:143 - i], T.CH[:, i:4 * C:16], i == 0, False) for i in range(16)],
+           ["CH%d" % r for r in range(4)] + ["TNM"], [7])
+
+        def low(r):
+            tt(T.CL[:, r * C:(r + 1) * C], pa, lo[:, r * C:(r + 1) * C], Op.is_ge, lks + ["pa"], ["CL%d" % r], [6])
+        hook("C")
+        spare = PO[:, 5 * C:6 * C]
+        low(0)
+        tt(T.E2[:], PO[:, 2 * C:4 * C], T.E1[:], Op.min, ["E1"], ["E2"], [ob + 1])
+        low(1)
+        tt(spare, PO[:, 4 * C:5 * C], T.E2[:, 0:C], Op.min, ["E2"], ["sq"], [ob + 2])
+        low(2)
+        tt(B, spare, T.E2[:, C:2 * C], Op.min, ["E2", "sq"], [bk_], [ob + 2])
+        if x == 1 and t < 2:
+            send([bk_])
+        low(3)
+        mm([(n_ps, T.TNP[:, 15 - i:143 - i], T.CL[:, i:4 * C:16], False, i == 15) for i in range(16)],
+           ["CL%d" % r for r in range(4)] + ["TNP"], [7])
+        if t == 2:
+            tt(T.W3[:, a * 512:a * 512 + C], pa, B, Op.add, [bk_], ["W3_%dl" % a], [6])
+            tt(T.W3[:, a * 512 + C:a * 512 + 512], B, pa, Op.subtract, [bk_], ["W3_%dh" % a], [6])
+            send(["W3_%dl" % a, "W3_%dh" % a])
+        elif x == 0:
+            act(A, pa, (), [ak], [6])
+            send([ak, bk_])
+
+    def ask(t, m):
+        act(T.GH[:, m, :], M[t][:].indirect(T.OFH[:, m, :]), ["M%d_%d" % (t, a) for a in range(4)] + ["Ms%d" % t, "OFH%d" % m],
+            ["GH%d" % m], whole=["aM%d" % t] + (["cp%d" % t] if t else []))
+
+    def to_list(m, table, out, start, stop):
+        return [(out, T.TJ[:, table, 15 - i:143 - i], T.GH[:, m, i:512:16], start and i == 0, stop and i == 15) for i in range(16)]
+
+    def hop(t, m):
+        ask(t, m)
+        mm(to_list(m, 4, PN[:, 384 + 32 * m:416 + 32 * m], True, True), ["GH%d" % m, "TJ4"], [7])
+
+    def hop_on(m):
+        cp(T.OFH[:, m + 1, :], PN[:, 384 + 32 * m:416 + 32 * m], (), ["OFH%d" % (m + 1)], [7])
+
+    def keys_under(t):
+        for j in range(4):
+            act(T.SC[:, j], T.SP[:, t & 1, j], ["SP%d" % (t & 1)], ["SC%d" % j], bias=KEY * (3 - j))
+
+    def elect(t):
+        for x in range(2):
+            tt(T.KS[:, :, x, :], PN[:, x * 64:(x + 1) * 64], T.SC[:, :, x, :], Op.add, ["SC%d" % j for j in range(4)], ["KS%d" % x], [7])
+        tt(T.K2[:], T.KS[:, 0:2], T.KS[:, 2:4], Op.max, ["KS0", "KS1"], ["K2"])
+        tt(T.MXI[:], T.K2[:, 0, :], T.K2[:, 1, :], Op.max, ["K2"], ["MXI"])
+        ts(T.CI[:], T.MXI[:], int(KEY) - 1, Op.bitwise_and, ["MXI"], ["CI"])
+        place(T.C2[:, 1, :], T.CI[:], T.CI[:], ["CI", "C5"], ["PC"])
+        cp(T.OFH[:, 0, :], T.C2[:, 1, :], ["PC"], ["OFH0"])
+        hop(t, 0)
+
+    def beside(t):
+        par = t & 1
+        cp(T.C2[:, 0, :], T.CI[:], ["CI"], ["C20"])
+        ts(T.ST[:], T.KS[:], 36 * KEY, Op.is_ge, ["KS0", "KS1"], ["ST"], 2 * KEY, Op.mult)
+        ts(T.SM[:], T.MXI[:], 36 * KEY, Op.is_ge, ["MXI"], ["SM"])
+        ts(T.U1[:, 0:32], T.MXI[:], 36 * KEY, Op.is_lt, ["MXI"], ["U1"], 8.0, Op.mult)
+        ts(T.U1[:, 32:64], T.CI[:], float(PART), Op.is_ge, ["CI"], ["U1b"], 8.0, Op.mult)
+        tt(T.EQ[:, 3, :], T.C2[:, 1, :], T.PV[:, par, 0:32], Op.is_equal, ["PC", "PV"], ["EQ3"])
+        tt(T.FC[:], T.U1[:, 0:32], T.U1[:, 32:64], Op.add, ["U1", "U1b"], ["FC"])
+        tt(T.C2[:], T.C2[:], T.R2[:, par], Op.subtract, ["C20", "PC", "R2%d" % par], ["C2", "PC"])
+
+    def veto(t):
+        par = t & 1
+        r2 = "R2%d" % par
+        tt(T.EQ[:, 0:3, :], PN[:, 384:480], T.PV[:, par, :], Op.is_equal, ["PV"], ["EQ"], [7])
+        tt(T.U1[:], T.EQ[:, 0:2, :], T.EQ[:, 2:4, :], Op.add, ["EQ", "EQ3"], ["U1", "U1b"])
+        tt(T.U2[:, 0:32], T.U1[:, 0:32], T.U1[:, 32:64], Op.add, ["U1"], ["U2"])
+        tt(T.NV[:], T.U2[:, 0:32], T.FC[:], Op.is_le, ["U2", "FC"], ["NV"])
+        tt(T.OK[:], T.NV[:], T.SM[:], Op.mult, ["NV", "SM"], ["OK"])
+        ts(T.U1[:, 0:32], T.NV[:], 2.0 ** 22, Op.mult, ["NV"], ["U1"])
+        for k in range(2):
+            tt(T.C2[:, k, :], T.C2[:, k, :], T.OK[:], Op.mult, ["C2", "OK"], ["C2%d" % k])
+        tt(T.UU[:], T.U1[:, 0:32], T.MXI[:], Op.add, ["U1", "MXI"], ["UU"])
+        tt(T.R2[:, par], T.R2[:, par], T.C2[:], Op.add, [r2, "C20", "C21"], [r2])
+        cp(T.OFH[:, 3, :], T.R2[:, par, 1, :], [r2], ["OFH3"])
+        ask(t, 3)
+        flags(par)
+        for j in range(4):
+            tt(T.VE[:, 32 * j:32 * j + 32], T.KS[:, j], T.UU[:], Op.is_ge, ["KS0", "KS1", "UU"], ["VE%d" % j])
+
+    def rows_in(t):
+        par = t & 1
+        lst = [(PN[:, 256:384], T.IF[:], T.SP[:, par], True, False)]
+        for j in range(4):
+            out = PN[:, 256 + 32 * j:288 + 32 * j]
+            lst += [(out, T.I34[:], T.F1[:], False, False), (out, T.IM[:], T.F2[:], False, j == 3)]
+        mm(lst, ["SP%d" % par, "IF", "I34", "IM", "F1", "F2"], [7])
+        act(T.S2[:], PN[:, 256:384], (), ["S2"], [7])
+        lst = [(PN[:, 128:256], T.IP[:], T.ST[:], True, False), (PN[:, 128:256], T.IVE[:], T.VE[:], False, False)]
+        for j in range(4):
+            out = PN[:, 128 + 32 * j:160 + 32 * j]
+            lst += [(out, T.IP[:], T.F1[:], False, False)] + to_list(3, j, out, False, j == 3)
+        mm(lst, ["ST", "IP", "IVE", "F1", "GH3"] + ["VE%d" % j for j in range(4)] + ["TJ%d" % j for j in range(4)], [7])
+
+    def rows_out(t):
+        par = t & 1
+        sp = "SP%d" % par
+        ts(T.TK[:], PN[:, 128:256], KEY + PART, Op.is_lt, (), ["TK"], bk=[7])
+        tt(T.DD[:], PN[:, 128:256], T.S2[:], Op.subtract, ["S2"], ["DD"], [7])
+        tt(T.DD[:], T.DD[:], T.TK[:], Op.mult, ["DD", "TK"], ["DD"])
+        tt(T.SP[:, par], T.SP[:, par], T.DD[:], Op.add, [sp, "DD"], [sp])
+        offsets(par)
+
+    def drift(t):
+        par, keys = t & 1, []
+        for x in range(2):
+            a = 2 * x + par
+            pa, B, bk_ = PA[:, x * C:(x + 1) * C], W[t + 1][:, a * 512 + C:a * 512 + 512], "W%d_%dh" % (t + 1, a)
+            lo_, hi_ = W[t + 2][:, a * 512:a * 512 + C], W[t + 2][:, a * 512 + C:a * 512 + 512]
+            kl, kh = "W%d_%dl" % (t + 2, a), "W%d_%dh" % (t + 2, a)
+            u = slice(x * C, (x + 1) * C)
+            if t == 0:
+                tt(lo_, pa, T.DR[:, a * C:(a + 1) * C], Op.add, ["DR"], [kl], [6])
+                drip(2 * x)
+                tt(hi_, B, T.DRP[:, u], Op.add, [bk_, "DRP%d" % x], [kh])
+                drip(3)
+            else:
+                tt(T.AB[:, u], B, pa, Op.subtract, [bk_], ["AB" + "ab"[x]], [6])
+                drip(x)
+                tt(T.T0[:, u], pa, B, Op.add, [bk_], ["T0%d" % x], [6])
+                drip(3 - 2 * x)
+                act(hi_, T.AB[:, u], ["AB" + "ab"[x]], [kh], bias=0.125)
+                tt(lo_, T.T0[:, u], T.DR2[:, u], Op.add, ["T0%d" % x, "DR2%d" % x], [kl])
+                drip(1)
+            keys += [kl, kh]
+        send(keys, after=["aW%d" % (t + 1)])
+
+    def theta_out(par):
+        for x in range(2):
+            a = 2 * x + par
+            act(T.YT[:, a * C:(a + 1) * C], T.W3[:, a * 512:a * 512 + C], ["W3_%dl" % a], ["YT%d" % a], bias=-0.125, scale=0.5)
+            act(T.SV[:, a * C:(a + 1) * C], T.W3[:, a * 512:a * 512 + C], ["W3_%dl" % a], ["SV%d" % a])
+            dma("S", T.yt[:, a * C:(a + 1) * C], T.YT[:, a * C:(a + 1) * C], "out", ["YT%d" % a])
+
+    held = []
+
+    def later(fn):
+        n = len(ops)
+        fn()
+        held.extend(ops[n:])
+        del ops[n:]
+
+    def drip(n):
+        while held and (n > 0 or held[0][0] != "V"):
+            n -= held[0][0] == "V"
+            ops.append(held.pop(0))
+
+    for t in range(3):
+        par = t & 1
+        if t == 0:
+            first_drift()
+            lay_lo(0, 0, [2])
+            first_hi(0, [2])
+            first_hi(1, [2])
+            base(0, 0, 0, [2])
+            fetch(0, 0)
+            lay_lo(0, 0, [0, 1])
+            first_hi(0, [0, 1])
+            base(0, 0, 0, [0, 1])
+            fetch(0, 1)
+        else:
+            fetch(t, 0)
+
+        def hook_x(at, t=t, par=par):
+            if t and at == "ll":
+                carry(t, par)
+                hop_on(1)
+                hop(t - 1, 2)
+                own(t, 1)
+                fetch(t, 1)
+            if t == 0 and at == "D3":
+                first_hi(1, [0, 1])
+            if t and at == "D2":
+                later(lambda: veto(t - 1))
+            if at[0] in "DU":
+                drip(2)
+            if at == "m":
+                drip(1)
+            if t and at == "pen":
+                rows_in(t - 1)
+            if at == "A":
+                drip(99)
+                lay_lo(t, 1, [0, 1, 2])
+
+        def hook_y(at, t=t, par=par):
+            if at == "ll":
+                keys_under(t)
+                if t:
+                    later(lambda: [rows_out(t - 1), names_high(1 - par), names_low(1 - par)])
+                else:
+                    drifts()
+            if at == "ll" or at[0] == "D":
+                drip(2)
+            if at == "U2" and t:
+                names_out(1 - par, t)
+            if at == "pen" and t == 2:
+                theta_out(1)
+        chunk(t, 0, hook_x)
+        base(t, 1, 0, [0, 1, 2])
+        chunk(t, 1, hook_y)
+        if t < 2:
+            own(t + 1, 0)
+            lay_lo(t + 1, 0, [2])
+            base(t + 1, 0, 0, [2])
+            later(lambda: elect(t))
+            drift(t)
+            drip(99)
+        else:
+            elect(t)
+        beside(t)
+        hop_on(0)
+        hop(t, 1)
+    hop_on(1)
+    hop(2, 2)
+    theta_out(0)
+
+    Z, D, P = LO, HI, [T.P0, T.P1]
+    w3 = wkeys(3)
+
+    def diffs(n, a, hs=(0, 1)):
+        par, x = a & 1, a >> 1
+        ok = "OFW%d%d" % (par, x)
+        if 0 in hs:
+            act(D[n & 1][:, 0:4 * C], T.W3[:, C:3 * PART].indirect(T.OFW[:, par, x, :]), w3 + [ok],
+                ["D%d" % (n & 1), "HI%d0" % (n & 1), "HI%d1" % (n & 1)], bias=0.0625, scale=0.5, whole=["aW3"])
+        for j in range(2 * hs[0], 2 * hs[-1] + 2):
+            tt(Z[n & 1][:, j * C:(j + 1) * C], T.W3[:].indirect(T.OFW[:, par, x, 16 * j:16 * j + 16]), T.SV[:, a * C:(a + 1) * C],
+               Op.subtract, w3 + [ok, "SV%d" % a], ["Z%d%d" % (n & 1, j)] + (["LO%d0" % n, "LO%d1" % n] if n < 2 and j == 0 else []), whole=["aW3"])
+
+    def sig(n, hs=(0, 1)):
+        ps, b = region(n & 1, 0)
+        for h in hs:
+            act(ps[:, h * 512:(h + 1) * 512], Z[n & 1][:, h * 512:(h + 1) * 512], ["Z%d%d" % (n & 1, j) for j in (2 * h, 2 * h + 1)], (),
+                [b + h], scale=0.5, fn=Fn.Sigmoid)
+
+    def weigh(n, a, hs=(0, 1)):
+        ps, b = region(n & 1, 0)
+        y = ps[:, 4 * C:5 * C]
+        if 0 in hs:
+            mm([(y, T.IQ[:], T.W3[:, a * 512 + C:a * 512 + 512], True, False)], ["IQ", "W3_%dh" % a], [b + 2])
+        for h in hs:
+            v = slice(h * 512, (h + 1) * 512)
+            tt(P[n & 1][:, v], ps[:, v], D[n & 1][:, v], Op.mult, ["D%d" % (n & 1)], ["P%d%d" % (n & 1, h)], [b + h])
+            mm([(y, T.IF[:], P[n & 1][:, j * C:(j + 1) * C], False, j == 3) for j in (2 * h, 2 * h + 1)],
+               ["IF", "P%d%d" % (n & 1, h)], [b + 2])
+
+    def y_out(n, a):
+        ps, b = region(n & 1, 0)
+        act(T.YQ[:, a * C:(a + 1) * C], ps[:, 4 * C:5 * C], (), ["YQ%d" % a], [b + 2], bias=0.03125)
+        dma("S", T.yq[:, a * C:(a + 1) * C], T.YQ[:, a * C:(a + 1) * C], "out", ["YQ%d" % a])
+
+    veto(2)
+    rows_in(2)
+    cp(T.IA[:], T.R2[:, :, 0, :], ["R20", "R21"], ["IA"])
+    ts(T.IB[:], T.IA[:], 7680, Op.bitwise_and, ["IA"], ["IB"])
+    ts(T.U1[:], T.IB[:], -0.5, Op.mult, ["IB"], ["U1", "U1b"])
+    for a in range(4):
+        v = slice((a & 1) * 32 + (a >> 1) * 16, (a & 1) * 32 + (a >> 1) * 16 + 16)
+        tt(T.RN[:, a * 16:(a + 1) * 16], T.U1[:, v], T.IA[:, v], Op.add, ["U1", "IA"], ["RN%d" % a])
+    mm([(PA[0:64, 0:128], T.RN[:], T.IF[:], True, True)], ["IF"] + ["RN%d" % a for a in range(4)], [6])
+    diffs(0, 1)
+    sig(0)
+    rows_out(2)
+    cp(T.YR[0:64, :], PA[0:64, 0:128], (), ["YR"], [6])
+    for q in range(8):
+        dma("S", T.yr[q, :], T.YR[0:64, 16 * q:16 * q + 16], "out", ["YR"])
+    diffs(1, 3)
+    sig(1)
+    weigh(0, 1)
+    diffs(2, 0)
+    weigh(1, 3)
+    sig(2)
+    y_out(0, 1)
+    diffs(3, 2, (0,))
+    weigh(2, 0, (0,))
+    y_out(1, 3)
+    sig(3, (0,))
+    diffs(3, 2, (1,))
+    sig(3, (1,))
+    weigh(2, 0, (1,))
+    weigh(3, 2)
+    y_out(2, 0)
+    y_out(3, 2)
+
+    writer, readers, bank = {}, {}, {}
+    deps = []
+    for i, (q, fn, rd, wr, bk, dm, whole) in enumerate(ops):
+        d = set()
+        for k in rd:
+            if k in writer:
+                d.add(writer[k])
+        for k in wr:
+            for j in readers.get(k, []) + ([writer[k]] if k in writer else []):
+                d.add(j)
+        for b in bk:
+            for q2, j in bank.get(b, {}).items():
+                if q2 != q or q == "A":
+                    d.add(j)
+            bank.setdefault(b, {})[q] = i
+        for k in rd:
+            readers.setdefault(k, []).append(i)
+        for k in wr:
+            writer[k] = i
+            readers[k] = []
+        deps.append(d)
+    seen = {q: {} for q in "VAPGS"}
+    need = []
+    for i, d in enumerate(deps):
+        mine, lst = seen[ops[i][0]], []
+        newest = {}
+        for j in d:
+            if ops[j][5]:
+                lst.append(ops[j][5][0])
+            else:
+                newest[ops[j][0]] = max(newest.get(ops[j][0], -1), j)
+        keep = []
+        for s in sorted(lst) + ops[i][6]:
+            if s not in mine:
+                mine[s] = 1
+                keep.append(s)
+        for q2, j in newest.items():
+            if mine.get(q2, -1) < j:
+                mine[q2] = j
+                keep.append(j)
+        need.append(keep)
+    marked = sorted(set(k for keep in need for k in keep if isinstance(k, int)))
+    count, value = {}, {}
+    for j in marked:
+        count[ops[j][0]] = count.get(ops[j][0], 0) + 1
+        value[j] = count[ops[j][0]]
+    queue = {"V": g.vector, "A": g.scalar, "P": g.tensor, "G": g, "S": g.sync}
+    for i, o in enumerate(ops):
+        for k in need[i]:
+            if isinstance(k, int):
+                queue[o[0]].wait_ge(T.sem[ops[k][0]], value[k])
+            else:
+                queue[o[0]].wait_ge(T.sem[k], total[k])
+        ins = o[1]()
+        if i in value:
+            ins.then_inc(T.sem[o[0]], 1)
+    g.sync.wait_ge(T.sem.out, total["out"])
+    g.wait_ge(T.sem.sent, total["sent"])

@@ -2,9 +2,10 @@ from concourse.bass import DstId, RemoteDMATransfer
 from concourse.mybir import AluOpType as Op, ActivationFunctionType as Fn
 
 C = 256
-PART = 2048
-SENT = 3 * PART
+SENT = 2048
+M1, M2 = SENT + 32, SENT + 32 + 2048
 KEY = 8192.0
+BIG16, BIG32 = 1.5 * 2.0 ** 27, 1.5 * 2.0 ** 28
 f32, b16, i32, u16 = "float32", "bfloat16", "int32", "uint16"
 
 
@@ -12,66 +13,69 @@ def _s(shape, d):
     return ("sbuf", [128] + shape, d)
 
 
+DIAG = {"IP": 1.0, "IM": -1.0, "IP16": 16.0, "I2": 2.0, "IM16": -16.0, "I8": 8.0, "I8K": 8192.0, "I4K": 4096.0, "I35": 3584.0,
+        "IM5": -512.0, "IVE": -16384.0}
+EARLY = 4
 SCRATCH = {
     "TH": _s([3072], b16), "DL": _s([3072], b16), "DR": _s([1024], b16),
-    "W1": _s([3 * PART], f32), "W2": _s([3 * PART], f32), "W3": _s([3 * PART], f32),
-    "M0": _s([SENT + 32], b16), "M1": _s([SENT + 32], b16), "M2": _s([SENT + 32], b16),
-    "SLI": _s([2, 2, 64], i32), "RFI": _s([2, 2, 16], i32), "SLB": _s([2, 2, 64], i32), "RFB": _s([2, 2, 16], i32),
+    "W1": _s([2, 3072], f32), "W2": _s([2, 3072], f32), "W3": _s([2, 3072], f32),
+    "M0": _s([M2 + 2048], b16), "M1": _s([M2 + 2048], b16), "M2": _s([M2 + 2048], b16),
+    "SLI": _s([2, 2, 4, 16], i32), "RFI": _s([64], i32),
     "XI": _s([144], f32), "PI": _s([8], i32), "PJ": _s([8], i32), "COL": _s([8], f32),
-    "E16": _s([16], f32), "KM": _s([8], f32),
-    "IP": _s([128], b16), "IM": _s([128], b16), "IP16": _s([128], b16), "IM16": _s([128], b16),
-    "I34": _s([128], b16), "IVE": _s([128], b16), "IF": _s([128], f32), "IQ": _s([128], f32),
-    "TN": _s([144], f32), "TNP": _s([144], b16), "TNM": _s([144], b16), "TJ": _s([5, 144], b16),
-    "PV": _s([2, 96], f32),
-    "SP": _s([2, 4, 2, 16], f32), "R2": _s([2, 2, 32], f32),
-    "OF0": _s([2, 64], u16), "OFW": _s([2, 2, 64], u16), "OFH": _s([4, 32], u16),
-    "IA": _s([64], i32), "IB": _s([64], i32),
-    "DRP": _s([512], f32), "DR2": _s([512], f32), "T0": _s([512], f32),
+    "E16": _s([16], f32), "KM": _s([8], f32), "IC": _s([128], b16),
+    "IF": _s([128], f32), "RO": _s([2, 2, 16], b16), "UV": _s([2, 16], f32), "DH": _s([1024], f32),
+    "TN": _s([144], b16), "TNP": _s([144], b16), "TNM": _s([144], b16), "TJ": _s([5, 144], b16),
+    "PV": _s([2, 2, 16], f32), "PVN": _s([2, 2, 3, 16], f32), "KC": _s([2, 4, 16], b16),
+    "SP": _s([2, 2, 4, 16], f32), "RF": _s([64], f32), "R": _s([2, 2, 16], f32),
+    "OFW": _s([2, 2, 64], u16), "OFH": _s([4, 32], u16),
+    "RD": _s([2, 3, 4, 16], f32), "FL": _s([2, 3, 4, 16], b16), "SO": _s([2, 3, 4, 16], b16),
+    "S1": _s([2, 3, 4, 16], b16), "S2": _s([2, 3, 4, 16], b16),
     "LO0": _s([5 * C], f32), "LO1": _s([5 * C], f32), "HI0": _s([5 * C], f32), "HI1": _s([5 * C], f32),
     "TG": _s([2, 4 * C], b16), "DG": _s([2, 4 * C], b16),
-    "LL": _s([10 * C], b16), "LH": _s([20 * C], b16), "CH": _s([5 * C], b16), "CL": _s([4 * C], b16),
-    "E1": _s([2 * C], f32), "E2": _s([2 * C], f32), "MM": _s([C], f32), "AB": _s([2 * C], f32),
+    "LL": _s([10 * C], b16), "LH": _s([20 * C], b16), "CH": _s([2, 5 * C], b16), "CL": _s([2, 4 * C], b16),
+    "E1": _s([2 * C], f32), "E2": _s([2 * C], f32), "MM": _s([C], f32), "AB": _s([C], f32),
     "GH": _s([4, 512], b16),
-    "SC": _s([4, 2, 16], f32), "KS": _s([4, 2, 16], f32), "K2": _s([2, 32], f32),
-    "MXI": _s([32], i32), "CI": _s([32], i32), "C2": _s([2, 32], f32),
-    "U1": _s([64], f32), "U2": _s([64], f32), "FC": _s([32], f32), "SM": _s([32], f32), "NV": _s([32], f32),
-    "EQ": _s([4, 32], f32), "OK": _s([32], f32), "UU": _s([32], f32),
-    "ST": _s([128], b16), "VE": _s([128], b16), "F1": _s([32], b16), "F2": _s([32], b16),
-    "S2": _s([128], f32), "TK": _s([128], f32), "DD": _s([128], f32),
-    "SH": _s([4, 32], b16), "SO": _s([4, 32], b16), "RH": _s([32], b16), "RO": _s([32], b16), "RS": _s([32], f32),
+    "KS": _s([2, 4, 16], f32), "K2": _s([2, 2, 16], f32), "MXI": _s([32], i32), "MXF": _s([32], f32), "CI": _s([32], i32),
+    "EQ": _s([2, 4, 16], b16), "U1": _s([32], f32), "U2": _s([32], f32),
+    "ST": _s([2, 4, 16], b16), "VE": _s([2, 4, 16], b16),
+    "NS": _s([32], b16), "F1": _s([32], b16), "F2": _s([32], b16),
+    "SB": _s([128], f32), "TK": _s([128], f32), "DD": _s([128], f32),
+    "RH": _s([2, 2, 16], b16), "RS": _s([2, 2, 16], f32),
     "TI": _s([2, 2, 16, 32], b16),
     "P0": _s([4 * C], f32), "P1": _s([4 * C], f32),
-    "SV": _s([1024], f32), "YT": _s([1024], f32), "YQ": _s([1024], f32), "RN": _s([64], f32), "YR": _s([128], f32),
+    "SV": _s([1024], f32), "YT": _s([1024], f32), "YQ": _s([1024], f32), "YR": _s([128], f32),
     "PL": ("psum", [128, 1536], f32), "PH": ("psum", [128, 1536], f32),
-    "PA": ("psum", [128, 512], f32), "PN": ("psum", [128, 512], f32),
+    "PA": ("psum", [128, 512], f32), "PN": ("psum", [128, 8, 4, 16], f32),
 }
-NCALL = 16
-SEMAPHORES = (["V", "A", "P", "G", "sent", "out", "cp1", "cp2", "aT", "aW1", "aW2", "aW3", "aM0", "aM1", "aM2",
-               "lt0", "lt1", "ld0", "ld1", "ldr", "lsl", "lrf"] + ["r%d" % k for k in range(NCALL)])
+SCRATCH.update({k: _s([128], b16) for k in DIAG})
 
 
 def pieces():
-    def two(sem, buf, a, b, n):
-        return (sem, [(buf, a, n), (buf, b, n)])
-    out = [("aT", [("TH", h * 512, 512), ("DL", h * 512, 512)]) for h in range(2)]
-    out += [two("aM0", "M0", 0, 1024, 1024), two("aW1", "W1", 512, 1536, 512)]
-    for t in range(3):
-        w, p = "W%d" % (t + 1), t & 1
-        x, y = p * 512, (2 + p) * 512
-        out.append(two("a" + w, w, x, x + C, C))
-        if t:
-            out.append(two("aM%d" % t, "M%d" % t, (1 - p) * 512, (3 - p) * 512, 512))
-        if t == 2:
-            out.append(two("a" + w, w, y, y + C, C))
-            break
-        out.append(two("a" + w, w, y, y + C // 2, C // 2))
-        out.append(two("a" + w, w, y + C, y + C + C // 2, C // 2))
-        out.append(two("aW%d" % (t + 2), "W%d" % (t + 2), x, y, 512))
+    def ends(w, a):
+        return ("%s_%d" % (w, a), "a" + w, [(w, 0, a * C, C), (w, 1, a * C, C)])
+
+    def end(w, a, k):
+        return ("%s_%d%s" % (w, a, "lh"[k]), "a" + w, [(w, k, a * C, C // 2), (w, k, a * C + C // 2, C // 2)])
+
+    def names(t, a, b, n):
+        return ("M%d" % t, "aM%d" % t, [("M%d" % t, None, a, n), ("M%d" % t, None, b, n)])
+    out = [("T%d" % h, "aT", [("TH", None, h * 512, 512), ("DL", None, h * 512, 512)]) for h in range(2)]
+    out += [ends("W1", 1), ends("W1", 3), names(0, 0, 1024, 1024)]
+    out += [ends("W1", 0), end("W1", 2, 0), end("W1", 2, 1), ends("W2", 0), ends("W2", 2)]
+    out += [ends("W2", 1), names(1, 0, 1024, 512), end("W2", 3, 0), end("W2", 3, 1), ends("W3", 1), ends("W3", 3)]
+    out += [ends("W3", 0), names(2, 512, 1536, 512), ends("W3", 2)]
     return out
 
 
-def part_width(buf):
-    return 1024 if buf in ("TH", "DL") else PART
+SEMAPHORES = (["V", "A", "P", "G", "sent", "out", "cp1", "cp2", "aT", "aW1", "aW2", "aW3", "aM0", "aM1", "aM2",
+               "lt0", "lt1", "ld0", "ld1", "ldr", "lsl", "lrf", "sv"] + ["r%d" % k for k in range(len(pieces()))]
+              + ["gd%d" % k for k in range(6)])
+
+
+def view(T, piece, part, rows=slice(0, 128)):
+    buf, k, a, n = piece
+    a += (0, M1, M2)[part] if buf[0] == "M" else 1024 * part
+    return T[buf][rows, a:a + n] if k is None else T[buf][rows, k, a:a + n]
 
 
 def route(T, topo, r):
@@ -99,12 +103,11 @@ def relay_program(g, core, T, topo, r, h):
     dst, halves = route(T, topo, r)
     rid, pid = topo.addr(dst, core)
     sent = 0
-    for k, (sem, two) in enumerate(pieces()):
-        buf, a, n = two[h]
-        a += part_width(buf)
+    for k, (_, sem, two) in enumerate(pieces()):
+        ap = view(T, two[h], 1)
         eng = share(topo.engines(core, dst), k)
         g.wait_ge(T.sem["r%d" % k], len(halves[h][1]))
-        g.remote_dma(T[buf][:, a:a + n], T[buf][:, a:a + n], T.sem[sem], T.sem.sent, pid, rid, bits(eng))
+        g.remote_dma(ap, ap, T.sem[sem], T.sem.sent, pid, rid, bits(eng))
         sent += len(eng)
     g.wait_ge(T.sem.sent, sent)
 
@@ -148,41 +151,64 @@ def rank_program(g, core, T, topo):
             return last
         op("P", emit, rd, (), bk)
 
+    def group(terms, rd, bk):
+        mm([(o, w, x, i == 0, i == len(terms) - 1) for i, (o, w, x) in enumerate(terms)], rd, bk)
+
     def dma(q, out, a, sem, rd, wr=(), whole=()):
         e = g.sync if q == "S" else g.scalar
         op(q, lambda: e.dma_start(out, a).then_inc(T.sem[sem], 16), rd, wr, (), (sem, 16), whole)
 
+    added = [0]
+
+    def add_dma(out, a, rd, wr, whole=()):
+        sem = "gd%d" % added[0]
+        added[0] += 1
+        op("G", lambda: g.dma_start(out, a, accum_op=Op.add).then_inc(T.sem[sem], 16), rd, wr, (), (sem, 16), whole)
+
     dst, halves = route(T, topo, rank)
     plan = pieces()
-    for k, (sem, two) in enumerate(plan):
+    for k, (_, sem, two) in enumerate(plan):
         for c, e in route(T, topo, (rank + 1) % n_ranks)[1]:
             total[sem] = total.get(sem, 0) + len(e if c == core else share(topo.engines(c, core), k))
     called = [0]
 
-    def send(rd, shift=True, after=()):
+    def send(name, rd, shift=True, after=()):
         k = called[0]
         called[0] += 1
-        sem, two = plan[k]
+        what, sem, two = plan[k]
+        assert what == name
         trs = []
-        for (buf, a, n), (to, eng) in zip(two, halves):
+        for piece, (to, eng) in zip(two, halves):
             rid, pid = topo.addr(to, core)
-            b = a + part_width(buf)
             trs.append(RemoteDMATransfer(dst_ids=[DstId(rid=rid, pnc=pid)], dma_engine_mask=bits(eng),
                                          remote_sem=T.sem[sem if to == dst else "r%d" % k],
-                                         src=T[buf][:, a:a + n], dst=T[buf][:, b:b + n]))
+                                         src=view(T, piece, 0), dst=view(T, piece, 1)))
         op("G", lambda: g.remote_dma_fused(trs, local_sem=T.sem.sent), rd, (), (), ("sent", sum(len(e) for _, e in halves)), after)
         if shift:
-            (buf, a, n), (_, a2, n2) = two
-            for s, m in ([(a, n + n2)] if a + n == a2 else [(a, n), (a2, n2)]):
-                b = s + 2 * PART
-                dma("S", T[buf][0:112, b:b + m], T[buf][16:128, s:s + m], sem, rd, (), after)
-                dma("S", T[buf][112:128, b:b + m], T[buf][0:16, s:s + m], sem, rd)
+            (buf, k0, a, n), (_, k1, a2, _) = two
+            if k0 != k1:
+                two = [(buf, slice(0, 2), a, n)]
+            elif a + n == a2:
+                two = [(buf, k0, a, 2 * n)]
+            for piece in two:
+                dma("S", view(T, piece, 2, slice(0, 112)), view(T, piece, 0, slice(16, 128)), sem, rd, (), after)
+                dma("S", view(T, piece, 2, slice(112, 128)), view(T, piece, 0, slice(0, 16)), sem, rd)
 
     W = [None, T.W1, T.W2, T.W3]
     M = [T.M0, T.M1, T.M2]
     LO, HI = [T.LO0, T.LO1], [T.HI0, T.HI1]
     PL, PH, PA, PN = T.PL, T.PH, T.PA, T.PN
     THK, DLK = ["TH0", "TH1"], ["DL0", "DL1"]
+    PKEY, PROW, PAUX, PHOP = PN[:, 0:2], PN[:, 2:4], PN[:, 4:6], PN[:, 6:8, 3, :]
+
+    def wq(t, k, a):
+        return W[t][:, k, a * C:(a + 1) * C]
+
+    def wk(t, a, s="lh"):
+        return ["W%d_%d%s" % (t, a, c) for c in s]
+
+    def wkeys(t):
+        return [k for a in range(4) for k in wk(t, a)]
 
     for h in range(2):
         v = slice(h * 512, (h + 1) * 512)
@@ -191,206 +217,211 @@ def rank_program(g, core, T, topo):
     op("G", lambda: g.iota(T.PI[:], [[0, 8]], 0, 1), (), ["PI"])
     op("G", lambda: g.iota(T.XI[:], [[1, 144]], 0, 0, allow_small_or_imprecise_dtypes=True), (), ["XI"])
     for h in range(2):
-        send([THK[h], DLK[h]], shift=False)
-    for par in range(2):
-        op("G", lambda par=par: g.iota(T.PV[:, par, :], [[0, 3], [1024, 2], [32, 16]], 512 * par, 0,
-                                       allow_small_or_imprecise_dtypes=True), (), ["PV%d" % par])
+        send("T%d" % h, [THK[h], DLK[h]], shift=False)
+    op("G", lambda: g.iota(T.PV[:], [[512, 2], [1024, 2], [32, 16]], 0, 0, allow_small_or_imprecise_dtypes=True), (), ["PV"])
+    op("G", lambda: g.iota(T.KC[:], [[0, 2], [-int(KEY), 4], [0, 16]], 3 * int(KEY), 0, allow_small_or_imprecise_dtypes=True), (), ["KC"])
+    dma("S", T.DR[:], T.dr[:], "ldr", (), ["DR"])
     dma("S", T.SLI[:], T.sl[:], "lsl", (), ["SLI"])
     dma("S", T.RFI[:], T.rf[:], "lrf", (), ["RFI"])
     for buf, src in ((T.TH, T.th), (T.DL, T.dl)):
         dma("S", buf[0:112, 2048:3072], src[16:128, :], "aT", ())
         dma("S", buf[112:128, 2048:3072], src[0:16, :], "aT", ())
-    dma("S", T.DR[:], T.dr[:], "ldr", (), ["DR"])
     op("V", lambda: g.vector.memset(T.TI[:], 0.0), (), ["TI0", "TI1"])
     for t in range(3):
-        op("V", lambda t=t: g.vector.memset(M[t][:, SENT:SENT + 32], float(SENT // 2)), (), ["Ms%d" % t])
+        op("V", lambda t=t: g.vector.memset(M[t][:, SENT:M1], 0.0), (), ["Ms%d" % t])
     for k, m in ((0, 127), (1, 15), (2, 31), (3, 16), (4, 112)):
         ts(T.PJ[:, k:k + 1], T.PI[:, k:k + 1], m, Op.bitwise_and, ["PI"], ["PJ%d" % k])
     cp(T.COL[:, 0:5], T.PJ[:, 0:5], ["PJ%d" % k for k in range(5)], ["C0"])
-    ts(T.COL[:, 5:6], T.COL[:, 3:4], -2.0, Op.mult, ["C0"], ["C5"], 16.0, Op.add)
+    ts(T.IP[:], T.XI[:, 0:128], T.COL[:, 0:1], Op.is_equal, ["XI", "C0"], ["IP"])
+    ts(T.COL[:, 5:6], T.COL[:, 3:4], -1.0, Op.mult, ["C0"], ["C5"], 8.0, Op.add)
     ts(T.COL[:, 4:5], T.COL[:, 4:5], 15.0, Op.add, ["C0"], ["C4"])
+    for key, v in list(DIAG.items())[1:EARLY]:
+        ts(T[key][:], T.IP[:], v, Op.mult, ["IP"], [key])
+    ts(T.IC[:], T.IP[:], T.COL[:, 5:6], Op.mult, ["IP", "C5"], ["IC"])
     act(T.COL[:, 6:7], T.COL[:, 0:1], ["C0"], ["C6"], scale=0.0, fn=Fn.Sigmoid)
     act(T.COL[:, 7:8], T.COL[:, 6:7], ["C6"], ["C7"], scale=0.5)
-    for buf, key, v in ((T.IP, "IP", 1.0), (T.IM, "IM", -1.0), (T.IP16, "IP16", 16.0), (T.IM16, "IM16", -16.0), (T.IF, "IF", 1.0)):
-        ts(buf[:], T.XI[:, 0:128], T.COL[:, 0:1], Op.is_equal, ["XI", "C0"], [key], v, Op.mult)
-    ts(T.TN[:], T.XI[:], T.COL[:, 4:5], Op.is_equal, ["XI", "C4"], ["TN"])
-    ts(T.E16[:], T.XI[:, 0:16], T.COL[:, 1:2], Op.is_equal, ["XI", "C0"], ["E16"])
-    tt(T.KM[:, 0:4], T.E16[:, 0:4], T.E16[:, 4:8], Op.add, ["E16"], ["KM"])
-    tt(T.KM[:, 4:5], T.E16[:, 8:9], T.E16[:, 9:10], Op.add, ["E16"], ["KM4"])
+    cp(T.RF[:], T.RFI[:], ["RFI"], ["RF"])
+    cp(T.SP[:], T.SLI[:], ["SLI"], ["SP0", "SP1"])
+    cp(T.OFW[:], T.SLI[:], ["SLI"], ["OFW0", "OFW1"])
 
-    def constants():
-        act(T.TNP[:], T.TN[:], ["TN"], ["TNP"], scale=4 * KEY)
-        act(T.TNM[:], T.TN[:], ["TN"], ["TNM"], scale=-4 * KEY)
-        for k in range(5):
-            act(T.TJ[:, k, :], T.TN[:], ["TN", "KM", "KM4"], ["TJ%d" % k], scale=T.KM[:, k:k + 1])
-        act(T.IQ[:], T.IF[:], ["IF", "C7"], ["IQ"], scale=T.COL[:, 7:8])
-        act(T.I34[:], T.IF[:], ["IF"], ["I34"], scale=0.75)
-        act(T.IVE[:], T.IF[:], ["IF"], ["IVE"], scale=-2 * KEY)
-    constants()
+    def first_drift():
+        for x, ps in enumerate((PL, PH)):
+            a = 2 * x + 1
+            v = slice(a * C, (a + 1) * C)
+            for k, sign in enumerate((T.IM, T.IP)):
+                out = ps[:, k * C:(k + 1) * C]
+                group([(out, T.IP[:], T.TH[:, v]), (out, sign[:], T.DL[:, v]), (out, T.IP[:], T.DR[:, v])],
+                      THK + DLK + ["DR", "IP", "IM"], [3 * x])
+            act(W[1][:, :, v], ps[:, 0:2 * C], (), wk(1, a), [3 * x])
+        for a in (1, 3):
+            send("W1_%d" % a, wk(1, a), after=["aT"])
 
-    def drifts():
-        for x in range(2):
-            act(T.DRP[:, x * C:(x + 1) * C], T.DR[:, 2 * x * C:(2 * x + 1) * C], ["DR"], ["DRP%d" % x], bias=0.125)
-            act(T.DR2[:, x * C:(x + 1) * C], T.DR[:, (2 * x + 1) * C:(2 * x + 2) * C], ["DR"], ["DR2%d" % x], bias=0.125, scale=2.0)
+    def cut(b, ks):
+        return b[:, 0, 2] if ks == [2] else b[:, :, ks[0] if len(ks) == 1 else slice(0, 2)]
 
-    def offsets(par):
-        for x in range(2):
-            cp(T.OFW[:, par, x, :], T.SP[:, par, :, x, :], ["SP%d" % par], ["OFW%d%d" % (par, x)])
+    def placing(src, keys, ks):
+        def named(b):
+            return [b + str(k) for k in ks]
+        ts(cut(T.RD, ks), src, -7.5, Op.add, keys, named("RD"), BIG16, Op.add)
+        act(cut(T.FL, ks), cut(T.RD, ks), named("RD"), named("FL"), bias=-BIG16)
+        act(cut(T.S1, ks), src, keys, named("S1"), bias=-1023.5, fn=Fn.Sign)
+        act(cut(T.S2, ks), src, keys, named("S2"), bias=-2047.5, fn=Fn.Sign)
+        tt(cut(T.SO, ks), src, cut(T.FL, ks), Op.subtract, keys + named("FL"), named("SO"))
 
-    def place(out, off_i, off_f, rd, wr):
-        ts(T.IB[:, 0:32], off_i, 240, Op.bitwise_and, rd, ["IB"])
-        ts(T.U1[:, 0:32], off_f, 2.0 * PART, Op.is_ge, rd, ["U1"], T.COL[:, 5:6], Op.mult)
-        tt(T.U1[:, 32:64], T.IB[:, 0:32], off_f, Op.add, rd + ["IB"], ["U1b"])
-        tt(T.U2[:, 0:32], T.U1[:, 0:32], T.U1[:, 32:64], Op.add, ["U1", "U1b"], ["U2"])
-        ts(out, T.U2[:, 0:32], T.COL[:, 3:4], Op.add, ["U2", "C0"], wr)
+    def placed(out, k):
+        return ([(out, w[:], cut(b, [k])) for w, b in ((T.IP, T.SO), (T.I2, T.FL), (T.IP16, T.S1), (T.IC, T.S2))],
+                [b + str(k) for b in ("FL", "SO", "S1", "S2")] + ["IP", "I2", "IP16", "IC"])
 
-    def flags(par):
-        ts(T.F1[:], T.R2[:, par, 0, :], float(PART), Op.is_ge, ["R2%d" % par], ["F1"], KEY, Op.mult)
-        ts(T.F2[:], T.R2[:, par, 0, :], 2.0 * PART, Op.is_ge, ["R2%d" % par], ["F2"], float(PART), Op.mult)
+    def first_refs():
+        placing(T.RF[:], ["RF"], [2])
+        group(*placed(PN[:, 0], 2), [7])
+        act(T.R[:], PN[:, 0], (), ["R0", "R1"], [7], bias=24.0)
 
-    def names_high(par):
-        act(T.SH[:], T.SP[:, par], ["SP%d" % par], ["SH"])
-        tt(T.U2[:, 0:32], T.F1[:], T.R2[:, par, 1, :], Op.add, ["F1", "R2%d" % par], ["U2"])
-        ts(T.RS[:], T.U2[:, 0:32], float(SENT), Op.min, ["U2"], ["RS"])
-        act(T.RH[:], T.RS[:], ["RS"], ["RH"])
-
-    def names_low(par):
-        tt(T.SO[:], T.SP[:, par], T.SH[:], Op.subtract, ["SP%d" % par, "SH"], ["SO"])
-        tt(T.RO[:], T.RS[:], T.RH[:], Op.subtract, ["RS", "RH"], ["RO"])
-        ti = "TI%d" % par
-        keys = [ti + "_%d" % k for k in range(10)]
-        for j in range(4):
-            act(T.TI[:, par, :, :, j], T.SH[:, j, :], ["SH", ti], [keys[j]])
-        act(T.TI[:, par, :, :, 8], T.RH[:], ["RH", ti], [keys[8]])
-        for j in range(4):
-            act(T.TI[:, par, :, :, 4 + j], T.SO[:, j, :], ["SO", ti], [keys[4 + j]])
-        act(T.TI[:, par, :, :, 9], T.RO[:], ["RO", ti], [keys[9]])
-        act(T.TI[:, par, :, :, 16:26], T.TI[:, par, :, :, 0:10], keys + [ti], [ti + "d"])
+    def names(ks):
+        v = ks[0] if len(ks) == 1 else slice(0, 2)
+        act(T.RS[:, :, v], T.R[:, :, v], ["R%d" % k for k in ks], ["RS"], bias=float(SENT), scale=-1.0, fn=Fn.Relu)
+        act(T.RH[:, :, v], T.RS[:, :, v], ["RS"], ["RH"])
+        placing(T.SP[:, :, v], ["SP%d" % k for k in ks], ks)
+        tt(T.RO[:, :, v], T.RS[:, :, v], T.RH[:, :, v], Op.subtract, ["RS", "RH"], ["RO"])
+        for k in ks:
+            parts = [b[:, :, k, j, :] for b in (T.FL, T.SO) for j in range(4)] + [T.RH[:, :, k], T.RO[:, :, k]]
+            mm([(PN[:, :, :, s], T.IP[:], p, True, True) for s, p in enumerate(parts)], ["FL%d" % k, "SO%d" % k, "RH", "RO", "IP"], [7])
+            for s in (0, 16):
+                act(T.TI[:, :, k, :, s:s + 10], PN[:, :, :, 0:10], ["TI%d" % k], ["TI%d%d" % (k, s)], [7])
 
     def names_out(par, t):
         ti = "TI%d" % par
         for x in range(2):
             a = 2 * x + par
-            op("V", lambda x=x, a=a: g.vector.transpose(M[t][:, a * 512:(a + 1) * 512], T.TI[:, par, x]),
-               [ti, ti + "d"] + [ti + "_%d" % k for k in range(10)], ["M%d_%d" % (t, a)])
+            op("V", lambda x=x, a=a: g.vector.transpose(M[t][:, a * 512:(a + 1) * 512], T.TI[:, x, par]),
+               [ti, ti + "0", ti + "16"], ["M%d_%d" % (t, a)])
         if t:
-            send(["M%d_%d" % (t, par), "M%d_%d" % (t, 2 + par)])
+            send("M%d" % t, ["M%d_%d" % (t, par), "M%d_%d" % (t, 2 + par)])
 
     def carry(t, par):
-        for part in range(3):
+        for part in (0, M1, M2):
             for x in range(2):
-                a = part * PART + (2 * x + par) * 512
+                a = part + (2 * x + par) * 512
                 dma("S", M[t][:, a:a + 512], M[t - 1][:, a:a + 512], "cp%d" % t,
                     ["M%d_%d" % (t - 1, 2 * x + par)], (), ["aM%d" % (t - 1)])
 
-    cp(T.OF0[:], T.SLI[:, :, 0, :], ["SLI"], ["OF0"])
-    ts(T.SLB[:], T.SLI[:], 3840, Op.bitwise_and, ["SLI"], ["SLB"])
-    ts(T.RFB[:], T.RFI[:], 3840, Op.bitwise_and, ["RFI"], ["RFB"])
-    for par in range(2):
-        for x in range(2):
-            tt(T.SP[:, par, :, x, :], T.SLI[:, x, par, :], T.SLB[:, x, par, :], Op.add, ["SLI", "SLB"], ["SP%d" % par])
-        tt(T.R2[:, par, 0, :], T.RFI[:, :, par, :], T.RFB[:, :, par, :], Op.add, ["RFI", "RFB"], ["R2%d" % par])
-        cp(T.IA[:, 0:32], T.R2[:, par, 0, :], ["R2%d" % par], ["IA"])
-        place(T.R2[:, par, 1, :], T.IA[:, 0:32], T.IA[:, 0:32], ["IA", "C5"], ["R2%d" % par])
-        flags(par)
-        names_high(par)
-        offsets(par)
-        names_low(par)
-    ts(T.PV[:], T.PV[:], T.COL[:, 2:3], Op.add, ["PV0", "PV1", "C0"], ["PV"])
-    names_out(0, 0)
-    names_out(1, 0)
-    send(["M0_%d" % a for a in range(4)], after=["aT"])
-    for ps, sign, b in ((PA, T.IM, 6), (PN, T.IP, 7)):
-        for x in range(2):
-            v, u = slice((2 * x + 1) * C, (2 * x + 2) * C), slice(x * C, (x + 1) * C)
-            mm([(ps[:, u], T.IP[:], T.TH[:, v], True, False), (ps[:, u], sign[:], T.DL[:, v], False, False),
-                (ps[:, u], T.IP[:], T.DR[:, v], False, True)], THK + DLK + ["DR", "IP", "IM"], [b])
+    def tables():
+        for key, v in list(DIAG.items())[EARLY:]:
+            ts(T[key][:], T.IP[:], v, Op.mult, ["IP"], [key])
+        cp(T.IF[:], T.IP[:], ["IP"], ["IF"])
+        ts(T.TN[:], T.XI[:], T.COL[:, 4:5], Op.is_equal, ["XI", "C4"], ["TN"])
+        ts(T.E16[:], T.XI[:, 0:16], T.COL[:, 1:2], Op.is_equal, ["XI", "C0"], ["E16"])
+        ts(T.PV[:], T.PV[:], T.COL[:, 2:3], Op.add, ["PV", "C0"], ["PV"])
+        tt(T.KM[:, 0:4], T.E16[:, 0:4], T.E16[:, 4:8], Op.add, ["E16"], ["KM"])
+        tt(T.KM[:, 4:5], T.E16[:, 8:9], T.E16[:, 9:10], Op.add, ["E16"], ["KM4"])
+        ts(T.TNP[:], T.TN[:], 4 * KEY, Op.mult, ["TN"], ["TNP"])
+        ts(T.TNM[:], T.TN[:], -4 * KEY, Op.mult, ["TN"], ["TNM"])
+        for m in range(3):
+            ts(T.PVN[:, :, :, m, :], T.PV[:], -1.0, Op.mult, ["PV"], ["PVN%d" % m], float(SENT), Op.add)
+        for k in range(5):
+            ts(T.TJ[:, k, :], T.TN[:], T.KM[:, k:k + 1], Op.mult, ["TN", "KM", "KM4"], ["TJ%d" % k])
 
-    def first_drift():
-        for k, (ps, b) in enumerate(((PA, 6), (PN, 7))):
-            for x in range(2):
-                a = 2 * x + 1
-                act(T.W1[:, a * 512 + k * C:a * 512 + (k + 1) * C], ps[:, x * C:(x + 1) * C], (), ["W1_%d%s" % (a, "lh"[k])], [b])
-        send(["W1_1l", "W1_1h", "W1_3l", "W1_3h"], after=["aT"])
+    def drifts():
+        for a in (0, 2):
+            v = slice(a * C, (a + 1) * C)
+            act(wq(2, 0, a), T.DR[:, v], ["DR"], wk(2, a, "l"))
+            act(wq(2, 1, a), T.DR[:, v], ["DR"], wk(2, a, "h"), bias=0.125)
+            act(wq(3, 0, a + 1), T.DR[:, (a + 1) * C:(a + 2) * C], ["DR"], wk(3, a + 1, "l"), bias=0.125, scale=2.0)
 
-    def wkeys(t):
-        return ["W%d_%d%s" % (t, a, s) for a in range(4) for s in "lh"]
+    def first_names():
+        n = len(ops)
+        tables()
+        fill = ops[n:]
+        del ops[n:]
+        later(lambda: [first_refs(), names([0, 1]), names_out(0, 0), names_out(1, 0)])
+        while held:
+            drip(1)
+            ops.extend(fill[:5])
+            del fill[:5]
+        ops.extend(fill)
+        send("M0", ["M0_%d" % a for a in range(4)])
 
     BANKS = [(0, 2), (2, 4), (4, 5)]
 
-    def fetch(t, x):
+    def rows(b):
+        return slice(BANKS[b][0] * C, BANKS[b][1] * C)
+
+    def fetch(t, x, ends=(0, 1)):
         par = t & 1
-        lo, lk = LO[x], "LO%d" % x
+        lo, lk, ok = LO[x], "LO%d" % x, "OFW%d" % par
         if t == 0:
-            off = T.OF0[:, x, :]
             if x == 0:
                 for b in range(2):
-                    v, off = slice(b * 512, (b + 1) * 512), T.OF0[:, x, 32 * b:32 * b + 32]
-                    cp(T.TG[:, x, v], T.TH[:].indirect(off), THK + ["OF0"], ["TG0%d" % b], whole=["aT"])
-                    act(T.DG[:, x, v], T.DL[:].indirect(off), DLK + ["OF0"], ["DG0%d" % b], whole=["aT"])
+                    v, off = rows(b), T.OFW[:, x, par, 32 * b:32 * b + 32]
+                    cp(T.TG[:, x, v], T.TH[:].indirect(off), THK + [ok], ["TG0%d" % b], whole=["aT"])
+                    act(T.DG[:, x, v], T.DL[:].indirect(off), DLK + [ok], ["DG0%d" % b], whole=["aT"])
             else:
-                act(T.TG[:, x, :], T.TH[:].indirect(off), THK + ["OF0"], ["TG10", "TG11"], whole=["aT"])
-                act(T.DG[:, x, :], T.DL[:].indirect(off), DLK + ["OF0"], ["DG10", "DG11"], whole=["aT"])
+                off = T.OFW[:, x, par, :]
+                act(T.TG[:, x, :], T.TH[:].indirect(off), THK + [ok], ["TG10", "TG11"], whole=["aT"])
+                act(T.DG[:, x, :], T.DL[:].indirect(off), DLK + [ok], ["DG10", "DG11"], whole=["aT"])
             return
-        rd, wh, ok = wkeys(t), ["aW%d" % t], "OFW%d%d" % (par, x)
-        wl, whi = W[t][:, 0:3 * PART], W[t][:, C:3 * PART]
+        rd, wh = wkeys(t) + [ok], ["aW%d" % t]
         if x == 0:
-            cp(lo[:, 0:2 * C], wl.indirect(T.OFW[:, par, x, 0:32]), rd + [ok], [lk + "0"], whole=wh)
-            act(lo[:, 2 * C:4 * C], wl.indirect(T.OFW[:, par, x, 32:64]), rd + [ok], [lk + "1"], whole=wh)
-            lay_lo(t, x, [0, 1])
+            cp(lo[:, rows(0)], W[t][:, 0, :].indirect(T.OFW[:, x, par, 0:32]), rd, [lk + "0"], whole=wh)
+            act(lo[:, rows(1)], W[t][:, 0, :].indirect(T.OFW[:, x, par, 32:64]), rd, [lk + "1"], whole=wh)
+            lay(t, x, [0, 1])
             base(t, x, 0, [0, 1])
-        else:
-            act(lo[:, 0:4 * C], wl.indirect(T.OFW[:, par, x, :]), rd + [ok], [lk + "0", lk + "1"], whole=wh)
-        act(HI[x][:, 0:4 * C], whi.indirect(T.OFW[:, par, x, :]), rd + [ok], ["HI%d0" % x, "HI%d1" % x], bias=0.125, whole=wh)
+        elif 0 in ends:
+            act(lo[:, 0:4 * C], W[t][:, 0, :].indirect(T.OFW[:, x, par, :]), rd, [lk + "0", lk + "1"], whole=wh)
+        if 1 in ends:
+            act(HI[x][:, 0:4 * C], W[t][:, 1, :].indirect(T.OFW[:, x, par, :]), rd, ["HI%d0" % x, "HI%d1" % x], bias=0.125, whole=wh)
 
     def own(t, x):
         a = 2 * x + (t & 1)
-        act(LO[x][:, 4 * C:5 * C], W[t][:, a * 512:a * 512 + C], ["W%d_%dl" % (t, a)], ["LO%d2" % x])
-        act(HI[x][:, 4 * C:5 * C], W[t][:, a * 512 + C:a * 512 + 512], ["W%d_%dh" % (t, a)], ["HI%d2" % x], bias=0.125)
+        act(LO[x][:, rows(2)], wq(t, 0, a), wk(t, a, "l"), ["LO%d2" % x])
+        act(HI[x][:, rows(2)], wq(t, 1, a), wk(t, a, "h"), ["HI%d2" % x], bias=0.125)
 
     def region(x, k):
         return (PL, 0) if (x + k) & 1 == 0 else (PH, 3)
 
     def from_pair(x, out, bank, b, sign, stop):
-        a, v = 2 * x, slice(BANKS[b][0] * C, BANKS[b][1] * C)
+        a, v = 2 * x, rows(b)
         if b < 2:
             th, dl, rd = T.TG[:, x, v], T.DG[:, x, v], ["TG%d%d" % (x, b), "DG%d%d" % (x, b)]
         else:
             th, dl, rd = T.TH[:, a * C:(a + 1) * C], T.DL[:, a * C:(a + 1) * C], THK + DLK
         mm([(out, T.IP[:], th, True, False), (out, sign[:], dl, False, stop)], rd + ["IP", "IM"], [bank])
 
-    def lay_lo(t, x, banks):
+    def lay(t, x, banks):
         lo, lk = LO[x], "LO%d" % x
         ps, b0 = region(x, 0)
         for b in banks:
-            v = slice(BANKS[b][0] * C, BANKS[b][1] * C)
+            v = rows(b)
             if t == 0:
                 from_pair(x, ps[:, v], b0 + b, b, T.IM, True)
                 if x == 0 and b == 0:
                     cp(lo[:, v], ps[:, v], (), [lk + str(b)], [b0 + b])
-                else:
+                elif x == 0:
                     act(lo[:, v], ps[:, v], (), [lk + str(b)], [b0 + b])
             elif x == 0 and b == 0:
                 cp(ps[:, v], lo[:, v], [lk + str(b)], ["L0"], [b0 + b])
             else:
                 act(ps[:, v], lo[:, v], [lk + str(b)], (), [b0 + b])
 
-    def first_hi(x, banks):
+    def first_ends(x, high, banks):
         for b in banks:
-            v = slice(BANKS[b][0] * C, BANKS[b][1] * C)
-            out, bank = ((PA[:], 6), (PN[:], 7), (PA[:, 0:C], 6))[b]
-            from_pair(x, out, bank, b, T.IP, True)
-            act(HI[x][:, v], out, (), ["HI%d%d" % (x, b)], [bank])
+            out, bank = ((PN[:], 7) if x and high else (PA[:], 6), (PN[:], 7),
+                         ((PA[:, 0:C], 6), (PL[:, 2 * C:3 * C], 1), (PH[:, 2 * C:3 * C], 4))[x + high * x])[b]
+            from_pair(x, out, bank, b, T.IP if high else T.IM, True)
+            act((HI if high else LO)[x][:, rows(b)], out, (), ["%s%d%d" % ("HI" if high else "LO", x, b)], [bank])
 
     def base(t, x, high, banks):
         ps, b0 = region(x, 1 - high)
         for b in banks:
-            v = slice(BANKS[b][0] * C, BANKS[b][1] * C)
+            v = rows(b)
+            src, key = (HI[x], "HI%d%d" % (x, b)) if high else (LO[x], "LO%d%d" % (x, b))
             if t == 0:
                 from_pair(x, ps[:, v], b0 + b, b, T.IP if high else T.IM, False)
-            else:
-                src, key = (HI[x], "HI%d%d" % (x, b)) if high else (LO[x], "LO%d%d" % (x, b))
+            elif x == 0 and not high:
                 mm([(ps[:, v], T.IF[:], src[:, v], True, False)], [key, "IF"], [b0 + b])
+            else:
+                mm([(ps[:, v], T.IP[:], T.TH[:, 0:v.stop - v.start], True, False)], THK + ["IP"], [b0 + b])
+                act(ps[:, v], src[:, v], [key], (), [b0 + b])
 
     def spans(first, count):
         return [(max(first, p), min(first + count, q), b) for b, (p, q) in enumerate(BANKS) if max(first, p) < min(first + count, q)]
@@ -398,208 +429,182 @@ def rank_program(g, core, T, topo):
     def banks_of(first, count, b0):
         return [b0 + b for _, _, b in spans(first, count)]
 
-    def chunk(t, x, hook):
-        par = t & 1
-        a = 2 * x + par
-        lo, lks = LO[x], ["LO%d%d" % (x, b) for b in range(3)]
-        hi, hks = HI[x], ["HI%d%d" % (x, b) for b in range(3)]
-        (PO, ob), (PS, sb) = region(x, 0), region(x, 1)
-        steps = [("D", s) for s in range(1, 5)] + [("U", s) for s in range(1, 5)]
-        last = {0: ("U", 1), 1: ("U", 3), 2: ("U", 4)}
+    def keys_of(x):
+        return ["LO%d%d" % (x, b) for b in range(3)], ["HI%d%d" % (x, b) for b in range(3)]
 
-        def add(src, p, first, n, wt, key, step):
-            for lo_, hi_, b in spans(first, n):
-                mm([(PS[:, lo_ * C:hi_ * C], wt[:], src[:, (p + lo_ - first) * C:(p + hi_ - first) * C], False, last[b] == step)],
-                   [key, "IP16", "IM16"], [sb + b])
+    LAST = {0: ("U", 1), 1: ("U", 3), 2: ("U", 4)}
+
+    def add(x, src, p, first, n, wt, key, step):
+        PS, sb = region(x, 1)
+        for lo_, hi_, b in spans(first, n):
+            mm([(PS[:, lo_ * C:hi_ * C], wt[:], src[:, (p + lo_ - first) * C:(p + hi_ - first) * C], False, LAST[b] == step)],
+               [key, "IP16", "IM16"], [sb + b])
+
+    def lows(x, s):
+        (PO, ob), n, pos = region(x, 0), 5 - s, (0, 4, 7, 9)[s - 1]
+        tt(T.LL[:, pos * C:(pos + n) * C], PO[:, 0:n * C], LO[x][:, s * C:5 * C], Op.is_le, keys_of(x)[0] + ["L0"], ["LL%d" % s], banks_of(0, n, ob))
+
+    def lows_add(x, s):
+        n, pos = 5 - s, (0, 4, 7, 9)[s - 1]
+        add(x, T.LL, pos, 0, n, T.IM16, "LL%d" % s, None)
+        add(x, T.LL, pos, s, n, T.IP16, "LL%d" % s, None)
+
+    def highs(x, hook):
+        (PO, ob), (PS, sb), hi, hks = region(x, 0), region(x, 1), HI[x], keys_of(x)[1]
         pos = 0
-        for s in range(1, 5):
-            n = 5 - s
-            tt(T.LL[:, pos * C:(pos + n) * C], PO[:, 0:n * C], lo[:, s * C:5 * C], Op.is_le, lks + ["L0"], ["LL%d" % s], banks_of(0, n, ob))
-            add(T.LL, pos, 0, n, T.IM16, "LL%d" % s, None)
-            add(T.LL, pos, s, n, T.IP16, "LL%d" % s, None)
-            pos += n
-        hook("ll")
-        pos = 0
-        for kind, s in steps:
+        for kind, s in [("D", s) for s in range(1, 5)] + [("U", s) for s in range(1, 5)]:
             n, key = 5 - s, "LH%s%d" % (kind, s)
             out = T.LH[:, pos * C:(pos + n) * C]
             if kind == "D":
                 tt(out, PO[:, 0:n * C], hi[:, s * C:5 * C], Op.is_le, hks, [key], banks_of(0, n, ob))
-                add(T.LH, pos, 0, n, T.IP16, key, (kind, s))
+                add(x, T.LH, pos, 0, n, T.IP16, key, (kind, s))
             else:
                 tt(out, PO[:, s * C:5 * C], hi[:, 0:n * C], Op.is_gt, hks, [key], banks_of(s, n, ob))
-                add(T.LH, pos, s, n, T.IM16, key, (kind, s))
+                add(x, T.LH, pos, s, n, T.IM16, key, (kind, s))
             pos += n
             if (kind, s) == ("U", 1):
                 act(T.E1[:], PS[:, 0:2 * C], (), ["E1"], [sb])
             hook(kind + str(s))
+
+    def pa_of(x):
+        return PA[:, x * C:(x + 1) * C], "pa%d" % x
+
+    def greatest(t, x, hook):
+        (PS, sb), (pa, pk) = region(x, 1), pa_of(x)
         base(t, x, 1, [0, 1, 2])
         spare = PS[:, 5 * C:6 * C]
         tt(T.E2[:], PS[:, 2 * C:4 * C], T.E1[:], Op.max, ["E1"], ["E2"], [sb + 1])
-        hook("m")
+        hook("m1")
         tt(spare, PS[:, 4 * C:5 * C], T.E2[:, 0:C], Op.max, ["E2"], ["sp"], [sb + 2])
-        hook("m")
+        hook("m2")
         tt(T.MM[:], spare, T.E2[:, C:2 * C], Op.max, ["E2", "sp"], ["MM"], [sb + 2])
-        hook("m")
-        big = 1.5 * 2.0 ** 27
-        ts(spare, T.MM[:], big, Op.add, ["MM"], ["sp"], -big, Op.add, [sb + 2])
-        hook("m")
-        if t < 2:
-            A, B = W[t + 1][:, a * 512:a * 512 + C], W[t + 1][:, a * 512 + C:a * 512 + 512]
-            ak, bk_ = "W%d_%dl" % (t + 1, a), "W%d_%dh" % (t + 1, a)
-        else:
-            B, bk_ = T.AB[:, C:2 * C], "ABb"
-        pa = PA[:, x * C:(x + 1) * C]
-        tt(pa, T.MM[:], spare, Op.subtract, ["MM", "sp"], ["pa"], [sb + 2, 6])
-        if x == 1 and t < 2:
-            tt(A, T.MM[:], spare, Op.subtract, ["MM", "sp"], [ak], [sb + 2])
-            send([ak])
-        hook("A")
+        hook("m3")
+        ts(spare, T.MM[:], BIG16, Op.add, ["MM"], ["sp"], -BIG16, Op.add, [sb + 2])
+        hook("m4")
+        tt(pa, T.MM[:], spare, Op.subtract, ["MM", "sp"], [pk], [sb + 2, 6])
+
+    def under(x, hook):
+        (PO, ob), (pa, pk), hks = region(x, 0), pa_of(x), keys_of(x)[1]
         for b, (p, q) in enumerate(BANKS):
             for r in range(p, q):
-                tt(T.CH[:, r * C:(r + 1) * C], pa, hi[:, r * C:(r + 1) * C], Op.is_gt, hks + ["pa"], ["CH%d" % r], [6])
-            mm([(PO[:, p * C:q * C], T.IP16[:], T.CH[:, p * C:q * C], False, True)], ["CH%d" % r for r in range(p, q)] + ["IP16"], [ob + b])
+                tt(T.CH[:, x, r * C:(r + 1) * C], pa, HI[x][:, r * C:(r + 1) * C], Op.is_gt, hks + [pk], ["CH%d%d" % (x, r)], [6])
+            mm([(PO[:, rows(b)], T.IP16[:], T.CH[:, x, rows(b)], False, True)], ["CH%d%d" % (x, r) for r in range(p, q)] + ["IP16"], [ob + b])
             if b == 0:
                 act(T.E1[:], PO[:, 0:2 * C], (), ["E1"], [ob])
-        hook("pen")
-        n_ps = PN[:, x * 64:(x + 1) * 64]
-        mm([(n_ps, T.TNM[:, 15 - i:143 - i], T.CH[:, i:4 * C:16], i == 0, False) for i in range(16)],
-           ["CH%d" % r for r in range(4)] + ["TNM"], [7])
+            hook("c%d" % b)
 
-        def low(r):
-            tt(T.CL[:, r * C:(r + 1) * C], pa, lo[:, r * C:(r + 1) * C], Op.is_ge, lks + ["pa"], ["CL%d" % r], [6])
-        hook("C")
+    def least(x, B, bk_, between):
+        PO, ob = region(x, 0)
         spare = PO[:, 5 * C:6 * C]
-        low(0)
+        between(0)
         tt(T.E2[:], PO[:, 2 * C:4 * C], T.E1[:], Op.min, ["E1"], ["E2"], [ob + 1])
-        low(1)
+        between(1)
         tt(spare, PO[:, 4 * C:5 * C], T.E2[:, 0:C], Op.min, ["E2"], ["sq"], [ob + 2])
-        low(2)
-        tt(B, spare, T.E2[:, C:2 * C], Op.min, ["E2", "sq"], [bk_], [ob + 2])
-        if x == 1 and t < 2:
-            send([bk_])
-        low(3)
-        mm([(n_ps, T.TNP[:, 15 - i:143 - i], T.CL[:, i:4 * C:16], False, i == 15) for i in range(16)],
-           ["CL%d" % r for r in range(4)] + ["TNP"], [7])
-        if t == 2:
-            tt(T.W3[:, a * 512:a * 512 + C], pa, B, Op.add, [bk_], ["W3_%dl" % a], [6])
-            tt(T.W3[:, a * 512 + C:a * 512 + 512], B, pa, Op.subtract, [bk_], ["W3_%dh" % a], [6])
-            send(["W3_%dl" % a, "W3_%dh" % a])
-        elif x == 0:
-            act(A, pa, (), [ak], [6])
-            send([ak, bk_])
+        between(2)
+        tt(B, spare, T.E2[:, C:2 * C], Op.min, ["E2", "sq"], bk_, [ob + 2])
+
+    def low(x, r):
+        pa, pk = pa_of(x)
+        tt(T.CL[:, x, r * C:(r + 1) * C], pa, LO[x][:, r * C:(r + 1) * C], Op.is_ge, keys_of(x)[0] + [pk], ["CL%d%d" % (x, r)], [6])
+
+    def key_open(t):
+        lst, rd = placed(PKEY, t & 1)
+        mm([m + (i == 0, False) for i, m in enumerate(lst + [(PKEY, T.IP[:], T.KC[:])])], rd + ["KC"], [7])
+
+    def key_add(x, high, stop=False):
+        src, wt, key = (T.CH, T.TNM, "CH") if high else (T.CL, T.TNP, "CL")
+        mm([(PN[:, x], wt[:, 15 - i:143 - i], src[:, x, i:4 * C:16], False, stop and i == 15) for i in range(16)],
+           ["%s%d%d" % (key, x, r) for r in range(4)] + ["TNP", "TNM"], [7])
+
+    def drift(t):
+        both = (t, 2 + t)
+        for a in both:
+            v = slice(a * C, (a + 1) * C)
+            if t == 1:
+                act(wq(3, 1, a), wq(2, 0, a), wk(2, a, "l"), wk(3, a, "h"), bias=0.125, scale=-1.0)
+            add_dma(W[t + 2][:, :, v], W[t + 1][:, :, v], wk(t + 1, a), wk(t + 2, a), ["aW%d" % (t + 1)])
+        for a in both if t == 1 else ():
+            add_dma(wq(3, 0, a), wq(2, 1, a), wk(2, a), wk(3, a))
+        for a in both:
+            send("W%d_%d" % (t + 2, a), wk(t + 2, a))
 
     def ask(t, m):
-        act(T.GH[:, m, :], M[t][:].indirect(T.OFH[:, m, :]), ["M%d_%d" % (t, a) for a in range(4)] + ["Ms%d" % t, "OFH%d" % m],
-            ["GH%d" % m], whole=["aM%d" % t] + (["cp%d" % t] if t else []))
+        (cp if t == 2 else act)(T.GH[:, m, :], M[t][:].indirect(T.OFH[:, m, :]),
+                                ["M%d_%d" % (t, a) for a in range(4)] + ["Ms%d" % t, "OFH%d" % m],
+                                ["GH%d" % m], whole=["aM%d" % t] + (["cp%d" % t] if t else []))
 
-    def to_list(m, table, out, start, stop):
-        return [(out, T.TJ[:, table, 15 - i:143 - i], T.GH[:, m, i:512:16], start and i == 0, stop and i == 15) for i in range(16)]
+    def to_list(m, table, out):
+        return [(out, T.TJ[:, table, 15 - i:143 - i], T.GH[:, m, i:512:16]) for i in range(16)]
 
     def hop(t, m):
         ask(t, m)
-        mm(to_list(m, 4, PN[:, 384 + 32 * m:416 + 32 * m], True, True), ["GH%d" % m, "TJ4"], [7])
+        group(to_list(m, 4, PN[:, 6:8, m, :]), ["GH%d" % m, "TJ4"], [7])
 
     def hop_on(m):
-        cp(T.OFH[:, m + 1, :], PN[:, 384 + 32 * m:416 + 32 * m], (), ["OFH%d" % (m + 1)], [7])
-
-    def keys_under(t):
-        for j in range(4):
-            act(T.SC[:, j], T.SP[:, t & 1, j], ["SP%d" % (t & 1)], ["SC%d" % j], bias=KEY * (3 - j))
+        ts(T.OFH[:, m + 1, :], PN[:, 6:8, m, :], -1.0, Op.mult, (), ["OFH%d" % (m + 1)], float(SENT), Op.add, [7])
 
     def elect(t):
-        for x in range(2):
-            tt(T.KS[:, :, x, :], PN[:, x * 64:(x + 1) * 64], T.SC[:, :, x, :], Op.add, ["SC%d" % j for j in range(4)], ["KS%d" % x], [7])
-        tt(T.K2[:], T.KS[:, 0:2], T.KS[:, 2:4], Op.max, ["KS0", "KS1"], ["K2"])
-        tt(T.MXI[:], T.K2[:, 0, :], T.K2[:, 1, :], Op.max, ["K2"], ["MXI"])
+        ts(T.KS[:], PKEY, 24.0, Op.add, (), ["KS"], bk=[7])
+        tt(T.K2[:], T.KS[:, :, 0:2, :], T.KS[:, :, 2:4, :], Op.max, ["KS"], ["K2"])
+        tt(T.MXI[:], T.K2[:, :, 0, :], T.K2[:, :, 1, :], Op.max, ["K2"], ["MXI"])
         ts(T.CI[:], T.MXI[:], int(KEY) - 1, Op.bitwise_and, ["MXI"], ["CI"])
-        place(T.C2[:, 1, :], T.CI[:], T.CI[:], ["CI", "C5"], ["PC"])
-        cp(T.OFH[:, 0, :], T.C2[:, 1, :], ["PC"], ["OFH0"])
+        ts(T.OFH[:, 0, :], T.CI[:], float(SENT), Op.min, ["CI"], ["OFH0"])
         hop(t, 0)
 
     def beside(t):
-        par = t & 1
-        cp(T.C2[:, 0, :], T.CI[:], ["CI"], ["C20"])
-        ts(T.ST[:], T.KS[:], 36 * KEY, Op.is_ge, ["KS0", "KS1"], ["ST"], 2 * KEY, Op.mult)
-        ts(T.SM[:], T.MXI[:], 36 * KEY, Op.is_ge, ["MXI"], ["SM"])
-        ts(T.U1[:, 0:32], T.MXI[:], 36 * KEY, Op.is_lt, ["MXI"], ["U1"], 8.0, Op.mult)
-        ts(T.U1[:, 32:64], T.CI[:], float(PART), Op.is_ge, ["CI"], ["U1b"], 8.0, Op.mult)
-        tt(T.EQ[:, 3, :], T.C2[:, 1, :], T.PV[:, par, 0:32], Op.is_equal, ["PC", "PV"], ["EQ3"])
-        tt(T.FC[:], T.U1[:, 0:32], T.U1[:, 32:64], Op.add, ["U1", "U1b"], ["FC"])
-        tt(T.C2[:], T.C2[:], T.R2[:, par], Op.subtract, ["C20", "PC", "R2%d" % par], ["C2", "PC"])
+        act(T.ST[:], T.KS[:], ["KS"], ["ST"], bias=0.5 - 36 * KEY, fn=Fn.Sign)
+        ts(T.MXF[:], T.MXI[:], 36 * KEY, Op.max, ["MXI"], ["MXF"])
+        ts(T.NS[:], T.MXI[:], 36 * KEY, Op.is_lt, ["MXI"], ["NS"])
+        tt(T.EQ[:, :, 3, :], T.CI[:], T.PV[:, t & 1], Op.is_equal, ["CI", "PV"], ["EQ3"])
 
     def veto(t):
         par = t & 1
-        r2 = "R2%d" % par
-        tt(T.EQ[:, 0:3, :], PN[:, 384:480], T.PV[:, par, :], Op.is_equal, ["PV"], ["EQ"], [7])
-        tt(T.U1[:], T.EQ[:, 0:2, :], T.EQ[:, 2:4, :], Op.add, ["EQ", "EQ3"], ["U1", "U1b"])
-        tt(T.U2[:, 0:32], T.U1[:, 0:32], T.U1[:, 32:64], Op.add, ["U1"], ["U2"])
-        tt(T.NV[:], T.U2[:, 0:32], T.FC[:], Op.is_le, ["U2", "FC"], ["NV"])
-        tt(T.OK[:], T.NV[:], T.SM[:], Op.mult, ["NV", "SM"], ["OK"])
-        ts(T.U1[:, 0:32], T.NV[:], 2.0 ** 22, Op.mult, ["NV"], ["U1"])
-        for k in range(2):
-            tt(T.C2[:, k, :], T.C2[:, k, :], T.OK[:], Op.mult, ["C2", "OK"], ["C2%d" % k])
-        tt(T.UU[:], T.U1[:, 0:32], T.MXI[:], Op.add, ["U1", "MXI"], ["UU"])
-        tt(T.R2[:, par], T.R2[:, par], T.C2[:], Op.add, [r2, "C20", "C21"], [r2])
-        cp(T.OFH[:, 3, :], T.R2[:, par, 1, :], [r2], ["OFH3"])
+        r, rk = T.R[:, :, par], "R%d" % par
+        tt(T.EQ[:, :, 0:3, :], PN[:, 6:8, 0:3, :], T.PVN[:, par], Op.is_equal, ["PVN0", "PVN1", "PVN2"], ["EQ"], [7])
+        group([(PHOP, T.I8K[:], T.NS[:])] + [(PHOP, T.I8K[:], T.EQ[:, :, m, :]) for m in (3, 0, 1, 2)], ["EQ", "EQ3", "NS", "I8K"], [7])
+        tt(T.U1[:], T.CI[:], PHOP, Op.subtract, ["CI"], ["U1"], [7])
+        tt(T.U2[:], r, PHOP, Op.min, [rk], ["U2"], [7])
+        ts(T.UV[:], PHOP, -128.0, Op.mult, (), ["UV"], 128 * KEY, Op.add, [7])
+        tt(r, T.U1[:], T.U2[:], Op.max, ["U1", "U2"], [rk])
+        tt(T.UV[:], T.UV[:], T.MXF[:], Op.max, ["UV", "MXF"], ["UV"])
+        cp(T.OFH[:, 3, :], r, [rk], ["OFH3"])
         ask(t, 3)
-        flags(par)
+        ts(T.F1[:], r, float(M1), Op.is_ge, [rk], ["F1"], 2.0, Op.mult)
+        ts(T.F2[:], r, float(M2), Op.is_ge, [rk], ["F2"], 2.0, Op.mult)
+        lst = [(PAUX, T.IP[:], T.FL[:, :, par]), (PAUX, T.IP[:], T.SO[:, :, par])]
         for j in range(4):
-            tt(T.VE[:, 32 * j:32 * j + 32], T.KS[:, j], T.UU[:], Op.is_ge, ["KS0", "KS1", "UU"], ["VE%d" % j])
+            lst += [(PN[:, 4:6, j, :], T.I35[:], T.F1[:]), (PN[:, 4:6, j, :], T.IM5[:], T.F2[:])]
+        group(lst, ["FL%d" % par, "SO%d" % par, "IP", "I35", "IM5", "F1", "F2"], [7])
+        for j in range(4):
+            tt(T.VE[:, :, j, :], T.KS[:, :, j, :], T.UV[:], Op.is_ge, ["KS", "UV"], ["VE%d" % j])
+        if t == 2:
+            ts(T.SB[:], PAUX, -KEY, Op.add, (), ["SB"], bk=[7])
+        else:
+            act(T.SB[:], PAUX, (), ["SB"], [7], bias=-KEY)
 
     def rows_in(t):
-        par = t & 1
-        lst = [(PN[:, 256:384], T.IF[:], T.SP[:, par], True, False)]
+        lst = [(PROW, T.I8K[:], T.ST[:])]
         for j in range(4):
-            out = PN[:, 256 + 32 * j:288 + 32 * j]
-            lst += [(out, T.I34[:], T.F1[:], False, False), (out, T.IM[:], T.F2[:], False, j == 3)]
-        mm(lst, ["SP%d" % par, "IF", "I34", "IM", "F1", "F2"], [7])
-        act(T.S2[:], PN[:, 256:384], (), ["S2"], [7])
-        lst = [(PN[:, 128:256], T.IP[:], T.ST[:], True, False), (PN[:, 128:256], T.IVE[:], T.VE[:], False, False)]
-        for j in range(4):
-            out = PN[:, 128 + 32 * j:160 + 32 * j]
-            lst += [(out, T.IP[:], T.F1[:], False, False)] + to_list(3, j, out, False, j == 3)
-        mm(lst, ["ST", "IP", "IVE", "F1", "GH3"] + ["VE%d" % j for j in range(4)] + ["TJ%d" % j for j in range(4)], [7])
+            lst += to_list(3, j, PN[:, 2:4, j, :]) + [(PN[:, 2:4, j, :], T.I4K[:], T.F1[:])]
+        group(lst + [(PROW, T.IVE[:], T.VE[:])], ["ST", "I8K", "I4K", "IVE", "F1", "GH3"] + [k + str(j) for j in range(4) for k in ("VE", "TJ")], [7])
 
     def rows_out(t):
         par = t & 1
         sp = "SP%d" % par
-        ts(T.TK[:], PN[:, 128:256], KEY + PART, Op.is_lt, (), ["TK"], bk=[7])
-        tt(T.DD[:], PN[:, 128:256], T.S2[:], Op.subtract, ["S2"], ["DD"], [7])
+        ts(T.TK[:], PROW, 1024.0, Op.is_lt, (), ["TK"], bk=[7])
+        tt(T.DD[:], PROW, T.SB[:], Op.subtract, ["SB"], ["DD"], [7])
         tt(T.DD[:], T.DD[:], T.TK[:], Op.mult, ["DD", "TK"], ["DD"])
-        tt(T.SP[:, par], T.SP[:, par], T.DD[:], Op.add, [sp, "DD"], [sp])
-        offsets(par)
-
-    def drift(t):
-        par, keys = t & 1, []
-        for x in range(2):
-            a = 2 * x + par
-            pa, B, bk_ = PA[:, x * C:(x + 1) * C], W[t + 1][:, a * 512 + C:a * 512 + 512], "W%d_%dh" % (t + 1, a)
-            lo_, hi_ = W[t + 2][:, a * 512:a * 512 + C], W[t + 2][:, a * 512 + C:a * 512 + 512]
-            kl, kh = "W%d_%dl" % (t + 2, a), "W%d_%dh" % (t + 2, a)
-            u = slice(x * C, (x + 1) * C)
-            if t == 0:
-                tt(lo_, pa, T.DR[:, a * C:(a + 1) * C], Op.add, ["DR"], [kl], [6])
-                drip(2 * x)
-                tt(hi_, B, T.DRP[:, u], Op.add, [bk_, "DRP%d" % x], [kh])
-                drip(3)
-            else:
-                tt(T.AB[:, u], B, pa, Op.subtract, [bk_], ["AB" + "ab"[x]], [6])
-                drip(x)
-                tt(T.T0[:, u], pa, B, Op.add, [bk_], ["T0%d" % x], [6])
-                drip(3 - 2 * x)
-                act(hi_, T.AB[:, u], ["AB" + "ab"[x]], [kh], bias=0.125)
-                tt(lo_, T.T0[:, u], T.DR2[:, u], Op.add, ["T0%d" % x, "DR2%d" % x], [kl])
-                drip(1)
-            keys += [kl, kh]
-        send(keys, after=["aW%d" % (t + 1)])
+        tt(T.SP[:, :, par], T.SP[:, :, par], T.DD[:], Op.add, [sp, "DD"], [sp])
+        cp(T.OFW[:, :, par, :], T.SP[:, :, par], [sp], ["OFW%d" % par])
 
     def theta_out(par):
         for x in range(2):
             a = 2 * x + par
-            act(T.YT[:, a * C:(a + 1) * C], T.W3[:, a * 512:a * 512 + C], ["W3_%dl" % a], ["YT%d" % a], bias=-0.125, scale=0.5)
-            act(T.SV[:, a * C:(a + 1) * C], T.W3[:, a * 512:a * 512 + C], ["W3_%dl" % a], ["SV%d" % a])
-            dma("S", T.yt[:, a * C:(a + 1) * C], T.YT[:, a * C:(a + 1) * C], "out", ["YT%d" % a])
+            v = slice(a * C, (a + 1) * C)
+            dma("S", T.SV[:, v], wq(3, 0, a), "sv", wk(3, a, "l"), ["SV%d" % a])
+            act(T.YT[:, v], wq(3, 0, a), wk(3, a, "l"), ["YT%d" % a], bias=-0.125, scale=0.5)
+            dma("S", T.yt[:, v], T.YT[:, v], "out", ["YT%d" % a])
+            act(T.DH[:, v], wq(3, 1, a), wk(3, a, "h") + ["C7"], ["DH%d" % a], bias=0.03125, scale=T.COL[:, 7:8])
 
     held = []
 
@@ -616,84 +621,143 @@ def rank_program(g, core, T, topo):
 
     for t in range(3):
         par = t & 1
+        ax, ay = par, 2 + par
         if t == 0:
-            first_drift()
-            lay_lo(0, 0, [2])
-            first_hi(0, [2])
-            first_hi(1, [2])
+            lay(0, 0, [2])
+            first_ends(0, 1, [2])
+            first_ends(1, 1, [2])
+            first_ends(1, 0, [2])
             base(0, 0, 0, [2])
+            later(first_drift)
+            first_names()
             fetch(0, 0)
-            lay_lo(0, 0, [0, 1])
-            first_hi(0, [0, 1])
+            lay(0, 0, [0, 1])
+            first_ends(0, 1, [0, 1])
             base(0, 0, 0, [0, 1])
             fetch(0, 1)
         else:
             fetch(t, 0)
-
-        def hook_x(at, t=t, par=par):
-            if t and at == "ll":
+        for s in range(1, 5):
+            lows(0, s)
+            lows_add(0, s)
+            if t and s == 1:
                 carry(t, par)
+                hop_on(0)
+                hop(t - 1, 1)
+                fetch(t, 1, (0,))
+
+        def hook_x(at, t=t):
+            if t == 0 and at == "D2":
+                first_ends(1, 0, [0, 1])
+            if t == 0 and at in ("c0", "c2"):
+                first_ends(1, 1, [int(at[1]) // 2])
+            if t and at == "D2":
                 hop_on(1)
                 hop(t - 1, 2)
-                own(t, 1)
-                fetch(t, 1)
-            if t == 0 and at == "D3":
-                first_hi(1, [0, 1])
-            if t and at == "D2":
+            if t == 2 and at == "D3":
+                theta_out(1)
+            if t and at == "U2":
                 later(lambda: veto(t - 1))
-            if at[0] in "DU":
-                drip(2)
-            if at == "m":
-                drip(1)
-            if t and at == "pen":
-                rows_in(t - 1)
-            if at == "A":
+            if at[0] in "Um":
+                drip(1 + (at in ("U4", "m1", "m2", "m3")))
+            if at == "U2":
+                lay(t, 1, [0])
+            if at == "m1":
+                lay(t, 1, [1])
+            if at == "c0":
                 drip(99)
-                lay_lo(t, 1, [0, 1, 2])
+                base(t, 1, 0, [0])
+                lay(t, 1, [2])
+            if t and at == "c2":
+                rows_in(t - 1)
+                fetch(t, 1, (1,))
+
+        def lows_y(k, t=t):
+            if k == 1:
+                base(t, 1, 0, [1])
+            lows(1, k + 1)
+        highs(0, hook_x)
+        greatest(t, 0, hook_x)
+        under(0, hook_x)
+        (pa, pk) = pa_of(0)
+        if t < 2:
+            act(wq(t + 1, 0, ax), pa, [pk], wk(t + 1, ax, "l"), [6])
+            least(0, wq(t + 1, 1, ax), wk(t + 1, ax, "h"), lows_y)
+        else:
+            least(0, T.AB[:], ["AB"], lows_y)
+        base(t, 1, 0, [2])
+        lows(1, 4)
+        if t == 2:
+            tt(wq(3, 0, ax), pa, T.AB[:], Op.add, [pk, "AB"], wk(3, ax, "l"), [6])
+            tt(wq(3, 1, ax), T.AB[:], pa, Op.subtract, [pk, "AB"], wk(3, ax, "h"), [6])
+        send("W%d_%d" % (t + 1, ax), wk(t + 1, ax))
+        for s in range(1, 5):
+            lows_add(1, s)
+        if t:
+            later(lambda: [rows_out(t - 1), names([1 - par])])
+        else:
+            drifts()
 
         def hook_y(at, t=t, par=par):
-            if at == "ll":
-                keys_under(t)
-                if t:
-                    later(lambda: [rows_out(t - 1), names_high(1 - par), names_low(1 - par)])
-                else:
-                    drifts()
-            if at == "ll" or at[0] == "D":
+            if at[0] == "D":
                 drip(2)
-            if at == "U2" and t:
+            if at == "U1":
+                drip(99)
+            if t == 2 and at[0] == "U":
+                low(0, int(at[1]) - 1)
+            if at == "U4" and t:
                 names_out(1 - par, t)
-            if at == "pen" and t == 2:
-                theta_out(1)
-        chunk(t, 0, hook_x)
-        base(t, 1, 0, [0, 1, 2])
-        chunk(t, 1, hook_y)
+            if at == "m1":
+                key_open(t)
+                key_add(0, 1)
+                if t == 2:
+                    key_add(0, 0)
+            if at == "c2":
+                key_add(1, 1)
+        highs(1, hook_y)
+        greatest(t, 1, hook_y)
+        under(1, hook_y)
+        (pa, pk) = pa_of(1)
         if t < 2:
+            act(wq(t + 1, 0, ay), pa, [pk], wk(t + 1, ay, "l"), [6])
+            send("W%d_%dl" % (t + 1, ay), wk(t + 1, ay, "l"))
+            least(1, wq(t + 1, 1, ay), wk(t + 1, ay, "h"), lambda k: None)
+            send("W%d_%dh" % (t + 1, ay), wk(t + 1, ay, "h"))
             own(t + 1, 0)
-            lay_lo(t + 1, 0, [2])
+            lay(t + 1, 0, [2])
             base(t + 1, 0, 0, [2])
-            later(lambda: elect(t))
+            own(t + 1, 1)
             drift(t)
-            drip(99)
+            for x in range(2):
+                for r in range(4):
+                    low(x, r)
+                key_add(x, 0, x == 1)
         else:
-            elect(t)
+            least(1, T.AB[:], ["AB"], lambda k: low(1, k))
+            low(1, 3)
+            key_add(1, 0, True)
+            tt(wq(3, 0, ay), pa, T.AB[:], Op.add, [pk, "AB"], wk(3, ay, "l"), [6])
+            tt(wq(3, 1, ay), T.AB[:], pa, Op.subtract, [pk, "AB"], wk(3, ay, "h"), [6])
+            send("W3_%d" % ay, wk(3, ay))
+            theta_out(0)
+        elect(t)
         beside(t)
-        hop_on(0)
-        hop(t, 1)
-    hop_on(1)
-    hop(2, 2)
-    theta_out(0)
+    for m in range(2):
+        hop_on(m)
+        hop(2, m + 1)
 
     Z, D, P = LO, HI, [T.P0, T.P1]
     w3 = wkeys(3)
 
+    def sources(n, a):
+        act(D[n & 1][:, 0:4 * C], T.W3[:, 1, :].indirect(T.OFW[:, a >> 1, a & 1, :]), w3 + ["OFW%d" % (a & 1)],
+            ["D%d" % (n & 1), "HI%d0" % (n & 1), "HI%d1" % (n & 1)], bias=0.0625, scale=0.5, whole=["aW3"])
+
     def diffs(n, a, hs=(0, 1)):
         par, x = a & 1, a >> 1
-        ok = "OFW%d%d" % (par, x)
-        if 0 in hs:
-            act(D[n & 1][:, 0:4 * C], T.W3[:, C:3 * PART].indirect(T.OFW[:, par, x, :]), w3 + [ok],
-                ["D%d" % (n & 1), "HI%d0" % (n & 1), "HI%d1" % (n & 1)], bias=0.0625, scale=0.5, whole=["aW3"])
+        ok = "OFW%d" % par
         for j in range(2 * hs[0], 2 * hs[-1] + 2):
-            tt(Z[n & 1][:, j * C:(j + 1) * C], T.W3[:].indirect(T.OFW[:, par, x, 16 * j:16 * j + 16]), T.SV[:, a * C:(a + 1) * C],
+            tt(Z[n & 1][:, j * C:(j + 1) * C], T.W3[:, 0, :].indirect(T.OFW[:, x, par, 16 * j:16 * j + 16]), T.SV[:, a * C:(a + 1) * C],
                Op.subtract, w3 + [ok, "SV%d" % a], ["Z%d%d" % (n & 1, j)] + (["LO%d0" % n, "LO%d1" % n] if n < 2 and j == 0 else []), whole=["aW3"])
 
     def sig(n, hs=(0, 1)):
@@ -702,52 +766,59 @@ def rank_program(g, core, T, topo):
             act(ps[:, h * 512:(h + 1) * 512], Z[n & 1][:, h * 512:(h + 1) * 512], ["Z%d%d" % (n & 1, j) for j in (2 * h, 2 * h + 1)], (),
                 [b + h], scale=0.5, fn=Fn.Sigmoid)
 
-    def weigh(n, a, hs=(0, 1)):
+    def weigh(n, a, fine=False):
         ps, b = region(n & 1, 0)
         y = ps[:, 4 * C:5 * C]
-        if 0 in hs:
-            mm([(y, T.IQ[:], T.W3[:, a * 512 + C:a * 512 + 512], True, False)], ["IQ", "W3_%dh" % a], [b + 2])
-        for h in hs:
-            v = slice(h * 512, (h + 1) * 512)
-            tt(P[n & 1][:, v], ps[:, v], D[n & 1][:, v], Op.mult, ["D%d" % (n & 1)], ["P%d%d" % (n & 1, h)], [b + h])
-            mm([(y, T.IF[:], P[n & 1][:, j * C:(j + 1) * C], False, j == 3) for j in (2 * h, 2 * h + 1)],
-               ["IF", "P%d%d" % (n & 1, h)], [b + 2])
+        for js in ([(0,), (1,), (2,), (3,)] if fine else [(0, 1), (2, 3)]):
+            v = slice(js[0] * C, (js[-1] + 1) * C)
+            keys = ["P%d%d" % (n & 1, j) for j in js]
+            tt(P[n & 1][:, v], ps[:, v], D[n & 1][:, v], Op.mult, ["D%d" % (n & 1)], keys, [b + js[0] // 2])
+            mm([(y, T.IF[:], P[n & 1][:, j * C:(j + 1) * C], j == 0, j == 3) for j in js], ["IF"] + keys, [b + 2])
 
     def y_out(n, a):
         ps, b = region(n & 1, 0)
-        act(T.YQ[:, a * C:(a + 1) * C], ps[:, 4 * C:5 * C], (), ["YQ%d" % a], [b + 2], bias=0.03125)
-        dma("S", T.yq[:, a * C:(a + 1) * C], T.YQ[:, a * C:(a + 1) * C], "out", ["YQ%d" % a])
+        v = slice(a * C, (a + 1) * C)
+        tt(T.YQ[:, v], ps[:, 4 * C:5 * C], T.DH[:, v], Op.add, ["DH%d" % a], ["YQ%d" % a], [b + 2])
+        dma("S", T.yq[:, v], T.YQ[:, v], "out", ["YQ%d" % a])
 
+    def refs_out():
+        rk = ["R0", "R1"]
+        ts(T.RD[:, 0, 2], T.R[:], -15.5, Op.add, rk, ["RD2"], BIG32, Op.add)
+        act(T.FL[:, 0, 2], T.RD[:, 0, 2], ["RD2"], ["FL2"], bias=BIG32 / 2, scale=-0.5)
+        act(T.S1[:, 0, 2], T.R[:], rk, ["S12"], bias=M1 - 0.5, scale=-1.0, fn=Fn.Sign)
+        act(T.S2[:, 0, 2], T.R[:], rk, ["S22"], bias=M2 - 0.5, scale=-1.0, fn=Fn.Sign)
+        out = PA[0:64, 0:128]
+        group([(out, T.R[:], T.IF[:]), (out, T.FL[:, 0, 2], T.IP[:]), (out, T.S1[:, 0, 2], T.I8[:]), (out, T.S2[:, 0, 2], T.IC[:])],
+              rk + ["FL2", "S12", "S22", "IF", "IP", "IC", "I8"], [6])
+
+    def refs_store():
+        ts(T.YR[0:64, :], PA[0:64, 0:128], -16.0, Op.add, (), ["YR"], bk=[6])
+        for q in range(8):
+            dma("S", T.yr[q, :], T.YR[0:64, 16 * q:16 * q + 16], "out", ["YR"])
+
+    sources(0, 1)
+    sources(1, 3)
     veto(2)
     rows_in(2)
-    cp(T.IA[:], T.R2[:, :, 0, :], ["R20", "R21"], ["IA"])
-    ts(T.IB[:], T.IA[:], 7680, Op.bitwise_and, ["IA"], ["IB"])
-    ts(T.U1[:], T.IB[:], -0.5, Op.mult, ["IB"], ["U1", "U1b"])
-    for a in range(4):
-        v = slice((a & 1) * 32 + (a >> 1) * 16, (a & 1) * 32 + (a >> 1) * 16 + 16)
-        tt(T.RN[:, a * 16:(a + 1) * 16], T.U1[:, v], T.IA[:, v], Op.add, ["U1", "IA"], ["RN%d" % a])
-    mm([(PA[0:64, 0:128], T.RN[:], T.IF[:], True, True)], ["IF"] + ["RN%d" % a for a in range(4)], [6])
     diffs(0, 1)
     sig(0)
-    rows_out(2)
-    cp(T.YR[0:64, :], PA[0:64, 0:128], (), ["YR"], [6])
-    for q in range(8):
-        dma("S", T.yr[q, :], T.YR[0:64, 16 * q:16 * q + 16], "out", ["YR"])
     diffs(1, 3)
     sig(1)
     weigh(0, 1)
-    diffs(2, 0)
+    refs_out()
+    rows_out(2)
+    sources(2, 0)
     weigh(1, 3)
+    sources(3, 2)
+    diffs(2, 0)
     sig(2)
+    refs_store()
     y_out(0, 1)
-    diffs(3, 2, (0,))
-    weigh(2, 0, (0,))
+    diffs(3, 2)
+    sig(3)
     y_out(1, 3)
-    sig(3, (0,))
-    diffs(3, 2, (1,))
-    sig(3, (1,))
-    weigh(2, 0, (1,))
-    weigh(3, 2)
+    weigh(2, 0)
+    weigh(3, 2, fine=True)
     y_out(2, 0)
     y_out(3, 2)
 

@@ -55,7 +55,7 @@ def pieces():
         return ("%s_%d" % (w, a), "a" + w, [(w, 0, a * C, C), (w, 1, a * C, C)])
 
     def end(w, a, k):
-        return ("%s_%d%s" % (w, a, "lh"[k]), "a" + w, [(w, k, a * C, C // 2), (w, k, a * C + C // 2, C // 2)])
+        return ("%s_%d%s" % (w, a, "lh"[k]), "ab"[k] + w, [(w, k, a * C, C // 2), (w, k, a * C + C // 2, C // 2)])
 
     def names(t, a, b, n):
         return ("M%d" % t, "aM%d" % t, [("M%d" % t, None, a, n), ("M%d" % t, None, b, n)])
@@ -63,11 +63,11 @@ def pieces():
     out += [ends("W1", 1), ends("W1", 3), names(0, 0, 1024, 1024)]
     out += [ends("W1", 0), end("W1", 2, 0), end("W1", 2, 1), ends("W2", 0), ends("W2", 2)]
     out += [ends("W2", 1), names(1, 0, 1024, 512), end("W2", 3, 0), end("W2", 3, 1), ends("W3", 1), ends("W3", 3)]
-    out += [ends("W3", 0), names(2, 512, 1536, 512), ends("W3", 2)]
+    out += [ends("W3", 0), names(2, 512, 1536, 512), end("W3", 2, 0), end("W3", 2, 1)]
     return out
 
 
-SEMAPHORES = (["V", "A", "P", "G", "sent", "out", "cp1", "cp2", "aT", "aW1", "aW2", "aW3", "aM0", "aM1", "aM2",
+SEMAPHORES = (["V", "A", "P", "G", "sent", "out", "cp1", "cp2", "aT", "aW1", "aW2", "aW3", "bW1", "bW2", "bW3", "aM0", "aM1", "aM2",
                "lt0", "lt1", "ld0", "ld1", "ldr", "lsl", "lrf", "sv"] + ["r%d" % k for k in range(len(pieces()))]
               + ["gd%d" % k for k in range(6)])
 
@@ -94,22 +94,25 @@ def bits(engines):
     return sum(1 << e for e in engines)
 
 
-def share(engines, k):
-    n = len(engines) // 2
-    return engines[k * n:(k + 1) * n] if k < 2 else engines
+def onward(topo, core, dst, k):
+    eng = topo.engines(core, dst)
+    n = len(eng) // 2
+    return eng[k * n:(k + 1) * n] if k < 2 else eng
 
 
-def relay_program(g, core, T, topo, r, h):
-    dst, halves = route(T, topo, r)
-    rid, pid = topo.addr(dst, core)
+def relay_program(g, core, T, topo, r):
     sent = 0
-    for k, (_, sem, two) in enumerate(pieces()):
-        ap = view(T, two[h], 1)
-        eng = share(topo.engines(core, dst), k)
-        g.wait_ge(T.sem["r%d" % k], len(halves[h][1]))
-        g.remote_dma(ap, ap, T.sem[sem], T.sem.sent, pid, rid, bits(eng))
-        sent += len(eng)
-    g.wait_ge(T.sem.sent, sent)
+    dst, ways = route(T, topo, r)
+    for k, (_, sem, parts) in enumerate(pieces()):
+        for part, (c, e) in zip(parts, ways):
+            if c == core:
+                rid, pid = topo.addr(dst, core)
+                ap, eng = view(T, part, 1), onward(topo, core, dst, k)
+                g.wait_ge(T.sem["r%d" % k], len(e))
+                g.remote_dma(ap, ap, T.sem[sem], T.sem.sent, pid, rid, bits(eng))
+                sent += len(eng)
+    if sent:
+        g.wait_ge(T.sem.sent, sent)
 
 
 def rank_program(g, core, T, topo):
@@ -117,9 +120,8 @@ def rank_program(g, core, T, topo):
     n_ranks = len(T.cores)
     if rank is None:
         for r in range(n_ranks):
-            for h, (c, _) in enumerate(route(T, topo, r)[1]):
-                if c == core:
-                    relay_program(g, core, T, topo, r, h)
+            if core in topo.cores_of(T.cores[r]):
+                relay_program(g, core, T, topo, r)
         return
     ops = []
     total = {}
@@ -165,11 +167,11 @@ def rank_program(g, core, T, topo):
         added[0] += 1
         op("G", lambda: g.dma_start(out, a, accum_op=Op.add).then_inc(T.sem[sem], 16), rd, wr, (), (sem, 16), whole)
 
-    dst, halves = route(T, topo, rank)
     plan = pieces()
-    for k, (_, sem, two) in enumerate(plan):
+    dst, halves = route(T, topo, rank)
+    for k, (_, sem, parts) in enumerate(plan):
         for c, e in route(T, topo, (rank + 1) % n_ranks)[1]:
-            total[sem] = total.get(sem, 0) + len(e if c == core else share(topo.engines(c, core), k))
+            total[sem] = total.get(sem, 0) + len(e if c == core else onward(topo, c, core, k))
     called = [0]
 
     def send(name, rd, shift=True, after=()):
@@ -361,7 +363,7 @@ def rank_program(g, core, T, topo):
                 act(T.DG[:, x, :], T.DL[:].indirect(off), DLK + [ok], ["DG10", "DG11"], whole=["aT"])
             return
         rd, wh = wkeys(t) + [ok], ["aW%d" % t]
-        if x == 0:
+        if x == 0 and 0 in ends:
             cp(lo[:, rows(0)], W[t][:, 0, :].indirect(T.OFW[:, x, par, 0:32]), rd, [lk + "0"], whole=wh)
             act(lo[:, rows(1)], W[t][:, 0, :].indirect(T.OFW[:, x, par, 32:64]), rd, [lk + "1"], whole=wh)
             lay(t, x, [0, 1])
@@ -369,7 +371,8 @@ def rank_program(g, core, T, topo):
         elif 0 in ends:
             act(lo[:, 0:4 * C], W[t][:, 0, :].indirect(T.OFW[:, x, par, :]), rd, [lk + "0", lk + "1"], whole=wh)
         if 1 in ends:
-            act(HI[x][:, 0:4 * C], W[t][:, 1, :].indirect(T.OFW[:, x, par, :]), rd, ["HI%d0" % x, "HI%d1" % x], bias=0.125, whole=wh)
+            act(HI[x][:, 0:4 * C], W[t][:, 1, :].indirect(T.OFW[:, x, par, :]), rd, ["HI%d0" % x, "HI%d1" % x], bias=0.125,
+                whole=wh + ["bW%d" % t])
 
     def own(t, x):
         a = 2 * x + (t & 1)
@@ -398,8 +401,6 @@ def rank_program(g, core, T, topo):
                     cp(lo[:, v], ps[:, v], (), [lk + str(b)], [b0 + b])
                 elif x == 0:
                     act(lo[:, v], ps[:, v], (), [lk + str(b)], [b0 + b])
-            elif x == 0 and b == 0:
-                cp(ps[:, v], lo[:, v], [lk + str(b)], ["L0"], [b0 + b])
             else:
                 act(ps[:, v], lo[:, v], [lk + str(b)], (), [b0 + b])
 
@@ -481,6 +482,10 @@ def rank_program(g, core, T, topo):
         hook("m3")
         ts(spare, T.MM[:], BIG16, Op.add, ["MM"], ["sp"], -BIG16, Op.add, [sb + 2])
         hook("m4")
+        if x == 1 and t < 2:
+            a = 2 + t
+            tt(wq(t + 1, 0, a), T.MM[:], spare, Op.subtract, ["MM", "sp"], wk(t + 1, a, "l"), [sb + 2])
+            send("W%d_%dl" % (t + 1, a), wk(t + 1, a, "l"))
         tt(pa, T.MM[:], spare, Op.subtract, ["MM", "sp"], [pk], [sb + 2, 6])
 
     def under(x, hook):
@@ -522,22 +527,21 @@ def rank_program(g, core, T, topo):
             v = slice(a * C, (a + 1) * C)
             if t == 1:
                 act(wq(3, 1, a), wq(2, 0, a), wk(2, a, "l"), wk(3, a, "h"), bias=0.125, scale=-1.0)
-            add_dma(W[t + 2][:, :, v], W[t + 1][:, :, v], wk(t + 1, a), wk(t + 2, a), ["aW%d" % (t + 1)])
+            add_dma(W[t + 2][:, :, v], W[t + 1][:, :, v], wk(t + 1, a), wk(t + 2, a), ["aW%d" % (t + 1), "bW%d" % (t + 1)])
         for a in both if t == 1 else ():
             add_dma(wq(3, 0, a), wq(2, 1, a), wk(2, a), wk(3, a))
         for a in both:
             send("W%d_%d" % (t + 2, a), wk(t + 2, a))
 
     def ask(t, m):
-        (cp if t == 2 else act)(T.GH[:, m, :], M[t][:].indirect(T.OFH[:, m, :]),
+        (cp if t == 2 and m < 2 else act)(T.GH[:, m, :], M[t][:].indirect(T.OFH[:, m, :]),
                                 ["M%d_%d" % (t, a) for a in range(4)] + ["Ms%d" % t, "OFH%d" % m],
                                 ["GH%d" % m], whole=["aM%d" % t] + (["cp%d" % t] if t else []))
 
     def to_list(m, table, out):
         return [(out, T.TJ[:, table, 15 - i:143 - i], T.GH[:, m, i:512:16]) for i in range(16)]
 
-    def hop(t, m):
-        ask(t, m)
+    def answer(m):
         group(to_list(m, 4, PN[:, 6:8, m, :]), ["GH%d" % m, "TJ4"], [7])
 
     def hop_on(m):
@@ -549,7 +553,7 @@ def rank_program(g, core, T, topo):
         tt(T.MXI[:], T.K2[:, :, 0, :], T.K2[:, :, 1, :], Op.max, ["K2"], ["MXI"])
         ts(T.CI[:], T.MXI[:], int(KEY) - 1, Op.bitwise_and, ["MXI"], ["CI"])
         ts(T.OFH[:, 0, :], T.CI[:], float(SENT), Op.min, ["CI"], ["OFH0"])
-        hop(t, 0)
+        ask(t, 0)
 
     def beside(t):
         act(T.ST[:], T.KS[:], ["KS"], ["ST"], bias=0.5 - 36 * KEY, fn=Fn.Sign)
@@ -591,10 +595,10 @@ def rank_program(g, core, T, topo):
     def rows_out(t):
         par = t & 1
         sp = "SP%d" % par
-        ts(T.TK[:], PROW, 1024.0, Op.is_lt, (), ["TK"], bk=[7])
+        ts(PAUX, PROW, 1024.0, Op.is_lt, (), ["TK"], bk=[7])
         tt(T.DD[:], PROW, T.SB[:], Op.subtract, ["SB"], ["DD"], [7])
-        tt(T.DD[:], T.DD[:], T.TK[:], Op.mult, ["DD", "TK"], ["DD"])
-        tt(T.SP[:, :, par], T.SP[:, :, par], T.DD[:], Op.add, [sp, "DD"], [sp])
+        tt(PROW, PAUX, T.DD[:], Op.mult, ["DD", "TK"], ["DT"], [7])
+        tt(T.SP[:, :, par], PROW, T.SP[:, :, par], Op.add, [sp, "DT"], [sp], [7])
         cp(T.OFW[:, :, par, :], T.SP[:, :, par], [sp], ["OFW%d" % par])
 
     def theta_out(par):
@@ -636,14 +640,20 @@ def rank_program(g, core, T, topo):
             base(0, 0, 0, [0, 1])
             fetch(0, 1)
         else:
-            fetch(t, 0)
-        for s in range(1, 5):
+            fetch(t, 0, (0,))
+            elect(t - 1)
+        for s in (3, 4, 1, 2):
             lows(0, s)
             lows_add(0, s)
-            if t and s == 1:
+            if t and s == 3:
+                fetch(t, 0, (1,))
+                beside(t - 1)
                 carry(t, par)
+            if t and s == 4:
+                answer(0)
+            if t and s == 2:
                 hop_on(0)
-                hop(t - 1, 1)
+                ask(t - 1, 1)
                 fetch(t, 1, (0,))
 
         def hook_x(at, t=t):
@@ -651,23 +661,24 @@ def rank_program(g, core, T, topo):
                 first_ends(1, 0, [0, 1])
             if t == 0 and at in ("c0", "c2"):
                 first_ends(1, 1, [int(at[1]) // 2])
-            if t and at == "D2":
+            if t and at in ("D1", "D4"):
+                answer(1 + (at == "D4"))
+            if t and at == "D3":
                 hop_on(1)
-                hop(t - 1, 2)
-            if t == 2 and at == "D3":
-                theta_out(1)
+                ask(t - 1, 2)
             if t and at == "U2":
                 later(lambda: veto(t - 1))
             if at[0] in "Um":
-                drip(1 + (at in ("U4", "m1", "m2", "m3")))
+                drip({"U2": 1, "U3": 3, "U4": 3}.get(at, 2))
             if at == "U2":
                 lay(t, 1, [0])
             if at == "m1":
                 lay(t, 1, [1])
             if at == "c0":
                 drip(99)
-                base(t, 1, 0, [0])
                 lay(t, 1, [2])
+            if at == "c2":
+                base(t, 1, 0, [0])
             if t and at == "c2":
                 rows_in(t - 1)
                 fetch(t, 1, (1,))
@@ -703,6 +714,8 @@ def rank_program(g, core, T, topo):
                 drip(2)
             if at == "U1":
                 drip(99)
+            if t == 2 and at == "U2":
+                theta_out(1)
             if t == 2 and at[0] == "U":
                 low(0, int(at[1]) - 1)
             if at == "U4" and t:
@@ -719,9 +732,7 @@ def rank_program(g, core, T, topo):
         under(1, hook_y)
         (pa, pk) = pa_of(1)
         if t < 2:
-            act(wq(t + 1, 0, ay), pa, [pk], wk(t + 1, ay, "l"), [6])
-            send("W%d_%dl" % (t + 1, ay), wk(t + 1, ay, "l"))
-            least(1, wq(t + 1, 1, ay), wk(t + 1, ay, "h"), lambda k: None)
+            least(1, wq(t + 1, 1, ay), wk(t + 1, ay, "h"), lambda k: k or low(0, 0))
             send("W%d_%dh" % (t + 1, ay), wk(t + 1, ay, "h"))
             own(t + 1, 0)
             lay(t + 1, 0, [2])
@@ -729,29 +740,26 @@ def rank_program(g, core, T, topo):
             own(t + 1, 1)
             drift(t)
             for x in range(2):
-                for r in range(4):
+                for r in range(1 - x, 4):
                     low(x, r)
                 key_add(x, 0, x == 1)
         else:
-            least(1, T.AB[:], ["AB"], lambda k: low(1, k))
-            low(1, 3)
-            key_add(1, 0, True)
+            least(1, T.AB[:], ["AB"], lambda k: k or low(1, 0))
             tt(wq(3, 0, ay), pa, T.AB[:], Op.add, [pk, "AB"], wk(3, ay, "l"), [6])
+            send("W3_%dl" % ay, wk(3, ay, "l"))
             tt(wq(3, 1, ay), T.AB[:], pa, Op.subtract, [pk, "AB"], wk(3, ay, "h"), [6])
-            send("W3_%d" % ay, wk(3, ay))
+            send("W3_%dh" % ay, wk(3, ay, "h"))
+            for r in range(1, 4):
+                low(1, r)
+            key_add(1, 0, True)
             theta_out(0)
-        elect(t)
-        beside(t)
-    for m in range(2):
-        hop_on(m)
-        hop(2, m + 1)
 
     Z, D, P = LO, HI, [T.P0, T.P1]
     w3 = wkeys(3)
 
     def sources(n, a):
         act(D[n & 1][:, 0:4 * C], T.W3[:, 1, :].indirect(T.OFW[:, a >> 1, a & 1, :]), w3 + ["OFW%d" % (a & 1)],
-            ["D%d" % (n & 1), "HI%d0" % (n & 1), "HI%d1" % (n & 1)], bias=0.0625, scale=0.5, whole=["aW3"])
+            ["D%d" % (n & 1), "HI%d0" % (n & 1), "HI%d1" % (n & 1)], bias=0.0625, scale=0.5, whole=["aW3", "bW3"])
 
     def diffs(n, a, hs=(0, 1)):
         par, x = a & 1, a >> 1
@@ -766,14 +774,29 @@ def rank_program(g, core, T, topo):
             act(ps[:, h * 512:(h + 1) * 512], Z[n & 1][:, h * 512:(h + 1) * 512], ["Z%d%d" % (n & 1, j) for j in (2 * h, 2 * h + 1)], (),
                 [b + h], scale=0.5, fn=Fn.Sigmoid)
 
-    def weigh(n, a, fine=False):
+    def weigh(n, a):
         ps, b = region(n & 1, 0)
         y = ps[:, 4 * C:5 * C]
-        for js in ([(0,), (1,), (2,), (3,)] if fine else [(0, 1), (2, 3)]):
+        for js in ((0, 1), (2, 3)):
             v = slice(js[0] * C, (js[-1] + 1) * C)
             keys = ["P%d%d" % (n & 1, j) for j in js]
             tt(P[n & 1][:, v], ps[:, v], D[n & 1][:, v], Op.mult, ["D%d" % (n & 1)], keys, [b + js[0] // 2])
             mm([(y, T.IF[:], P[n & 1][:, j * C:(j + 1) * C], j == 0, j == 3) for j in js], ["IF"] + keys, [b + 2])
+
+    def weigh_last(n, a):
+        (ps, b), p, d, dk = region(n & 1, 0), P[n & 1], D[n & 1], "D%d" % (n & 1)
+        y, v = ps[:, 4 * C:5 * C], slice(a * C, (a + 1) * C)
+        row = [slice(j * C, (j + 1) * C) for j in range(4)]
+        keys = ["P%d%d" % (n & 1, j) for j in range(4)]
+        mm([(y, T.IF[:], T.DH[:, v], True, False)], ["IF", "DH%d" % a], [b + 2])
+        for j in range(3):
+            tt(p[:, row[j]], ps[:, row[j]], d[:, row[j]], Op.mult, [dk], [keys[j]], [b + j // 2])
+            if j < 2:
+                mm([(y, T.IF[:], p[:, row[j]], False, j == 1)], ["IF", keys[j]], [b + 2])
+        tt(ps[:, row[3]], ps[:, row[3]], d[:, row[3]], Op.mult, [dk], ["PL3"], [b + 1])
+        tt(p[:, row[3]], ps[:, row[3]], p[:, row[2]], Op.add, ["PL3", keys[2]], [keys[3]], [b + 1])
+        tt(T.YQ[:, v], y, p[:, row[3]], Op.add, [keys[3]], ["YQ%d" % a], [b + 2])
+        dma("S", T.yq[:, v], T.YQ[:, v], "out", ["YQ%d" % a])
 
     def y_out(n, a):
         ps, b = region(n & 1, 0)
@@ -796,31 +819,44 @@ def rank_program(g, core, T, topo):
         for q in range(8):
             dma("S", T.yr[q, :], T.YR[0:64, 16 * q:16 * q + 16], "out", ["YR"])
 
+    elect(2)
+    answer(0)
+    beside(2)
+    hop_on(0)
+    ask(2, 1)
+    answer(1)
+    hop_on(1)
+    ask(2, 2)
+    answer(2)
+    diffs(0, 1, (0,))
+    later(lambda: veto(2))
+    drip(1)
     sources(0, 1)
-    sources(1, 3)
-    veto(2)
+    diffs(0, 1, (1,))
+    drip(99)
     rows_in(2)
-    diffs(0, 1)
     sig(0)
     diffs(1, 3)
-    sig(1)
+    sources(1, 3)
     weigh(0, 1)
+    sig(1)
     refs_out()
     rows_out(2)
     sources(2, 0)
     weigh(1, 3)
-    sources(3, 2)
     diffs(2, 0)
     sig(2)
-    refs_store()
+    sources(3, 2)
     y_out(0, 1)
-    diffs(3, 2)
-    sig(3)
-    y_out(1, 3)
+    diffs(3, 2, (0,))
     weigh(2, 0)
-    weigh(3, 2, fine=True)
+    sig(3, (0,))
+    diffs(3, 2, (1,))
+    sig(3, (1,))
+    refs_store()
+    y_out(1, 3)
     y_out(2, 0)
-    y_out(3, 2)
+    weigh_last(3, 2)
 
     writer, readers, bank = {}, {}, {}
     deps = []

@@ -5,7 +5,10 @@ C = 256
 SENT = 2048
 M1, M2 = SENT + 32, SENT + 32 + 2048
 KEY = 8192.0
-BIG16, BIG32 = 1.5 * 2.0 ** 27, 1.5 * 2.0 ** 28
+BIG1, BIG16, BIG32 = 1.5 * 2.0 ** 23, 1.5 * 2.0 ** 27, 1.5 * 2.0 ** 28
+F = 1.0 / 16
+WIDE = 0.125 * F
+MID = 192.0
 f32, b16, i32, u16 = "float32", "bfloat16", "int32", "uint16"
 
 
@@ -13,9 +16,9 @@ def _s(shape, d):
     return ("sbuf", [128] + shape, d)
 
 
-DIAG = {"IP": 1.0, "IM": -1.0, "IP16": 16.0, "I2": 2.0, "IM16": -16.0, "I8": 8.0, "I8K": 8192.0, "I4K": 4096.0, "I35": 3584.0,
-        "IM5": -512.0, "IVE": -16384.0}
-EARLY = 4
+DIAG = {"IP": 1.0, "IQ": F, "IQM": -F, "IP16": 16.0, "I2": 2.0, "IM": -1.0, "I8": 8.0, "I8K": 8192.0, "I4K": 4096.0,
+        "I35": 3584.0, "IM5": -512.0, "IVE": -16384.0}
+EARLY = 5
 SCRATCH = {
     "TH": _s([3072], b16), "DL": _s([3072], b16), "DR": _s([1024], b16),
     "W1": _s([2, 3072], f32), "W2": _s([2, 3072], f32), "W3": _s([2, 3072], f32),
@@ -33,7 +36,7 @@ SCRATCH = {
     "LO0": _s([5 * C], f32), "LO1": _s([5 * C], f32), "HI0": _s([5 * C], f32), "HI1": _s([5 * C], f32),
     "TG": _s([2, 4 * C], b16), "DG": _s([2, 4 * C], b16),
     "LL": _s([10 * C], b16), "LH": _s([20 * C], b16), "CH": _s([2, 5 * C], b16), "CL": _s([2, 4 * C], b16),
-    "E1": _s([2 * C], f32), "E2": _s([2 * C], f32), "MM": _s([C], f32), "AB": _s([C], f32),
+    "E1": _s([2 * C], f32), "E2": _s([2 * C], f32), "MM": _s([C], f32), "AB": _s([C], f32), "AX": _s([C], f32), "RB": _s([C], b16), "CK": _s([C], b16),
     "GH": _s([4, 512], b16),
     "KS": _s([2, 4, 16], f32), "K2": _s([2, 2, 16], f32), "MXI": _s([32], i32), "MXF": _s([32], f32), "CI": _s([32], i32),
     "EQ": _s([2, 4, 16], b16), "U1": _s([32], f32), "U2": _s([32], f32),
@@ -57,19 +60,22 @@ def pieces():
     def end(w, a, k):
         return ("%s_%d%s" % (w, a, "lh"[k]), "ab"[k] + w, [(w, k, a * C, C // 2), (w, k, a * C + C // 2, C // 2)])
 
+    def folded(w, a):
+        return ("%s_%df" % (w, a), None if w == "W3" else "b" + w, [(w, 1, a * C, C)])
+
     def names(t, a, b, n):
         return ("M%d" % t, "aM%d" % t, [("M%d" % t, None, a, n), ("M%d" % t, None, b, n)])
     out = [("T%d" % h, "aT", [("TH", None, h * 512, 512), ("DL", None, h * 512, 512)]) for h in range(2)]
     out += [ends("W1", 1), ends("W1", 3), names(0, 0, 1024, 1024)]
-    out += [ends("W1", 0), end("W1", 2, 0), end("W1", 2, 1), ends("W2", 0), ends("W2", 2)]
-    out += [ends("W2", 1), names(1, 0, 1024, 512), end("W2", 3, 0), end("W2", 3, 1), ends("W3", 1), ends("W3", 3)]
-    out += [ends("W3", 0), names(2, 512, 1536, 512), end("W3", 2, 0), end("W3", 2, 1)]
+    out += [end("W1", 0, 0), folded("W1", 0), end("W1", 2, 0), end("W1", 2, 1), ends("W2", 0), ends("W2", 2)]
+    out += [end("W2", 1, 0), folded("W2", 1), names(1, 0, 1024, 512), end("W2", 3, 0), end("W2", 3, 1), ends("W3", 1), ends("W3", 3)]
+    out += [folded("W3", 0), names(2, 512, 1536, 512), ends("W3", 0), end("W3", 2, 0), end("W3", 2, 1)]
     return out
 
 
 SEMAPHORES = (["V", "A", "P", "G", "sent", "out", "cp1", "cp2", "aT", "aW1", "aW2", "aW3", "bW1", "bW2", "bW3", "aM0", "aM1", "aM2",
                "lt0", "lt1", "ld0", "ld1", "ldr", "lsl", "lrf", "sv"] + ["r%d" % k for k in range(len(pieces()))]
-              + ["gd%d" % k for k in range(6)])
+              + ["gd%d" % k for k in range(9)] + ["bk1", "bk2", "bk3"])
 
 
 def view(T, piece, part, rows=slice(0, 128)):
@@ -78,15 +84,17 @@ def view(T, piece, part, rows=slice(0, 128)):
     return T[buf][rows, a:a + n] if k is None else T[buf][rows, k, a:a + n]
 
 
-def route(T, topo, r):
+def route(T, topo, r, parts):
     src, dst = T.cores[r], T.cores[(r - 1) % len(T.cores)]
     able = [c for c in topo.cores_of(src) if c != src and T.rank_of(c) is None and topo.may_write(c, dst)]
     far = [c for c in able if topo.die(c) != topo.die(src)][0]
-    if topo.may_write(src, dst):
-        out = topo.engines(src, dst)
-        return dst, [(dst, out), (far, [e for e in topo.engines(src, far) if e not in out])]
     near = [c for c in able if topo.die(c) == topo.die(src)][0]
     eng = topo.engines(src, near)
+    if parts == 1:
+        return dst, [(far if topo.may_write(src, dst) else near, eng)]
+    if topo.may_write(src, dst):
+        out = topo.engines(src, dst)
+        return dst, [(dst, out), (far, [e for e in eng if e not in out])]
     return dst, [(near, eng[:len(eng) // 2]), (far, eng[len(eng) // 2:])]
 
 
@@ -100,17 +108,34 @@ def onward(topo, core, dst, k):
     return eng[k * n:(k + 1) * n] if k < 2 else eng
 
 
+def back(topo, core, src, dst):
+    return [e for e in topo.engines(core, src) if e not in topo.engines(core, dst)]
+
+
 def relay_program(g, core, T, topo, r):
     sent = 0
-    dst, ways = route(T, topo, r)
+    src = T.cores[r]
     for k, (_, sem, parts) in enumerate(pieces()):
+        dst, ways = route(T, topo, r, len(parts))
         for part, (c, e) in zip(parts, ways):
-            if c == core:
-                rid, pid = topo.addr(dst, core)
-                ap, eng = view(T, part, 1), onward(topo, core, dst, k)
+            if c != core:
+                continue
+            rid, pid = topo.addr(dst, core)
+            ap, eng = view(T, part, 1), onward(topo, core, dst, k)
+            if len(parts) == 2:
                 g.wait_ge(T.sem["r%d" % k], len(e))
                 g.remote_dma(ap, ap, T.sem[sem], T.sem.sent, pid, rid, bits(eng))
-                sent += len(eng)
+            else:
+                home, (rid2, pid2) = back(topo, core, src, dst), topo.addr(src, core)
+                g.wait_ge(T.sem["r%d" % k], len(e))
+                trs = [RemoteDMATransfer(dst_ids=[DstId(rid=rid2, pnc=pid2)], dma_engine_mask=bits(home), remote_sem=T.sem["bk" + part[0][1]],
+                                         src=ap, dst=view(T, part, 0) if sem else T.AX[:])]
+                if sem:
+                    trs.append(RemoteDMATransfer(dst_ids=[DstId(rid=rid, pnc=pid)], dma_engine_mask=bits(eng),
+                                                 remote_sem=T.sem[sem], src=ap, dst=ap))
+                g.remote_dma_fused(trs, local_sem=T.sem.sent)
+                sent += len(home) - (0 if sem else len(eng))
+            sent += len(eng)
     if sent:
         g.wait_ge(T.sem.sent, sent)
 
@@ -168,13 +193,13 @@ def rank_program(g, core, T, topo):
         op("G", lambda: g.dma_start(out, a, accum_op=Op.add).then_inc(T.sem[sem], 16), rd, wr, (), (sem, 16), whole)
 
     plan = pieces()
-    dst, halves = route(T, topo, rank)
+    dst, halves = route(T, topo, rank, 2)
     for k, (_, sem, parts) in enumerate(plan):
-        for c, e in route(T, topo, (rank + 1) % n_ranks)[1]:
+        for c, e in route(T, topo, (rank + 1) % n_ranks, len(parts))[1]:
             total[sem] = total.get(sem, 0) + len(e if c == core else onward(topo, c, core, k))
     called = [0]
 
-    def send(name, rd, shift=True, after=()):
+    def send(name, rd, local=True, after=()):
         k = called[0]
         called[0] += 1
         what, sem, two = plan[k]
@@ -186,15 +211,18 @@ def rank_program(g, core, T, topo):
                                          remote_sem=T.sem[sem if to == dst else "r%d" % k],
                                          src=view(T, piece, 0), dst=view(T, piece, 1)))
         op("G", lambda: g.remote_dma_fused(trs, local_sem=T.sem.sent), rd, (), (), ("sent", sum(len(e) for _, e in halves)), after)
-        if shift:
+        if local:
             (buf, k0, a, n), (_, k1, a2, _) = two
             if k0 != k1:
                 two = [(buf, slice(0, 2), a, n)]
             elif a + n == a2:
                 two = [(buf, k0, a, 2 * n)]
             for piece in two:
-                dma("S", view(T, piece, 2, slice(0, 112)), view(T, piece, 0, slice(16, 128)), sem, rd, (), after)
-                dma("S", view(T, piece, 2, slice(112, 128)), view(T, piece, 0, slice(0, 16)), sem, rd)
+                shift(piece, sem, rd, after)
+
+    def shift(piece, sem, rd, after=()):
+        dma("S", view(T, piece, 2, slice(0, 112)), view(T, piece, 0, slice(16, 128)), sem, rd, (), after)
+        dma("S", view(T, piece, 2, slice(112, 128)), view(T, piece, 0, slice(0, 16)), sem, rd)
 
     W = [None, T.W1, T.W2, T.W3]
     M = [T.M0, T.M1, T.M2]
@@ -219,7 +247,7 @@ def rank_program(g, core, T, topo):
     op("G", lambda: g.iota(T.PI[:], [[0, 8]], 0, 1), (), ["PI"])
     op("G", lambda: g.iota(T.XI[:], [[1, 144]], 0, 0, allow_small_or_imprecise_dtypes=True), (), ["XI"])
     for h in range(2):
-        send("T%d" % h, [THK[h], DLK[h]], shift=False)
+        send("T%d" % h, [THK[h], DLK[h]], local=False)
     op("G", lambda: g.iota(T.PV[:], [[512, 2], [1024, 2], [32, 16]], 0, 0, allow_small_or_imprecise_dtypes=True), (), ["PV"])
     op("G", lambda: g.iota(T.KC[:], [[0, 2], [-int(KEY), 4], [0, 16]], 3 * int(KEY), 0, allow_small_or_imprecise_dtypes=True), (), ["KC"])
     dma("S", T.DR[:], T.dr[:], "ldr", (), ["DR"])
@@ -229,6 +257,7 @@ def rank_program(g, core, T, topo):
         dma("S", buf[0:112, 2048:3072], src[16:128, :], "aT", ())
         dma("S", buf[112:128, 2048:3072], src[0:16, :], "aT", ())
     op("V", lambda: g.vector.memset(T.TI[:], 0.0), (), ["TI0", "TI1"])
+    op("V", lambda: g.vector.memset(T.CK[:], MID), (), ["CK"])
     for t in range(3):
         op("V", lambda t=t: g.vector.memset(M[t][:, SENT:M1], 0.0), (), ["Ms%d" % t])
     for k, m in ((0, 127), (1, 15), (2, 31), (3, 16), (4, 112)):
@@ -241,7 +270,7 @@ def rank_program(g, core, T, topo):
         ts(T[key][:], T.IP[:], v, Op.mult, ["IP"], [key])
     ts(T.IC[:], T.IP[:], T.COL[:, 5:6], Op.mult, ["IP", "C5"], ["IC"])
     act(T.COL[:, 6:7], T.COL[:, 0:1], ["C0"], ["C6"], scale=0.0, fn=Fn.Sigmoid)
-    act(T.COL[:, 7:8], T.COL[:, 6:7], ["C6"], ["C7"], scale=0.5)
+    act(T.COL[:, 7:8], T.COL[:, 6:7], ["C6"], ["C7"], scale=0.5 / F)
     cp(T.RF[:], T.RFI[:], ["RFI"], ["RF"])
     cp(T.SP[:], T.SLI[:], ["SLI"], ["SP0", "SP1"])
     cp(T.OFW[:], T.SLI[:], ["SLI"], ["OFW0", "OFW1"])
@@ -250,10 +279,10 @@ def rank_program(g, core, T, topo):
         for x, ps in enumerate((PL, PH)):
             a = 2 * x + 1
             v = slice(a * C, (a + 1) * C)
-            for k, sign in enumerate((T.IM, T.IP)):
+            for k, sign in enumerate((T.IQM, T.IQ)):
                 out = ps[:, k * C:(k + 1) * C]
-                group([(out, T.IP[:], T.TH[:, v]), (out, sign[:], T.DL[:, v]), (out, T.IP[:], T.DR[:, v])],
-                      THK + DLK + ["DR", "IP", "IM"], [3 * x])
+                group([(out, T.IQ[:], T.TH[:, v]), (out, sign[:], T.DL[:, v]), (out, T.IQ[:], T.DR[:, v])],
+                      THK + DLK + ["DR", "IQ", "IQM"], [3 * x])
             act(W[1][:, :, v], ps[:, 0:2 * C], (), wk(1, a), [3 * x])
         for a in (1, 3):
             send("W1_%d" % a, wk(1, a), after=["aT"])
@@ -326,9 +355,9 @@ def rank_program(g, core, T, topo):
     def drifts():
         for a in (0, 2):
             v = slice(a * C, (a + 1) * C)
-            act(wq(2, 0, a), T.DR[:, v], ["DR"], wk(2, a, "l"))
-            act(wq(2, 1, a), T.DR[:, v], ["DR"], wk(2, a, "h"), bias=0.125)
-            act(wq(3, 0, a + 1), T.DR[:, (a + 1) * C:(a + 2) * C], ["DR"], wk(3, a + 1, "l"), bias=0.125, scale=2.0)
+            act(wq(2, 0, a), T.DR[:, v], ["DR"], wk(2, a, "l"), scale=F)
+            act(wq(2, 1, a), T.DR[:, v], ["DR"], wk(2, a, "h"), bias=WIDE, scale=F)
+            act(wq(3, 0, a + 1), T.DR[:, (a + 1) * C:(a + 2) * C], ["DR"], wk(3, a + 1, "l"), bias=WIDE, scale=2 * F)
 
     def first_names():
         n = len(ops)
@@ -371,13 +400,15 @@ def rank_program(g, core, T, topo):
         elif 0 in ends:
             act(lo[:, 0:4 * C], W[t][:, 0, :].indirect(T.OFW[:, x, par, :]), rd, [lk + "0", lk + "1"], whole=wh)
         if 1 in ends:
-            act(HI[x][:, 0:4 * C], W[t][:, 1, :].indirect(T.OFW[:, x, par, :]), rd, ["HI%d0" % x, "HI%d1" % x], bias=0.125,
+            act(HI[x][:, 0:4 * C], W[t][:, 1, :].indirect(T.OFW[:, x, par, :]), rd, ["HI%d0" % x, "HI%d1" % x], bias=WIDE,
                 whole=wh + ["bW%d" % t])
 
-    def own(t, x):
+    def own(t, x, high):
         a = 2 * x + (t & 1)
-        act(LO[x][:, rows(2)], wq(t, 0, a), wk(t, a, "l"), ["LO%d2" % x])
-        act(HI[x][:, rows(2)], wq(t, 1, a), wk(t, a, "h"), ["HI%d2" % x], bias=0.125)
+        if high:
+            act(HI[x][:, rows(2)], wq(t, 1, a), wk(t, a, "h"), ["HI%d2" % x], bias=WIDE)
+        else:
+            act(LO[x][:, rows(2)], wq(t, 0, a), wk(t, a, "l"), ["LO%d2" % x])
 
     def region(x, k):
         return (PL, 0) if (x + k) & 1 == 0 else (PH, 3)
@@ -388,19 +419,16 @@ def rank_program(g, core, T, topo):
             th, dl, rd = T.TG[:, x, v], T.DG[:, x, v], ["TG%d%d" % (x, b), "DG%d%d" % (x, b)]
         else:
             th, dl, rd = T.TH[:, a * C:(a + 1) * C], T.DL[:, a * C:(a + 1) * C], THK + DLK
-        mm([(out, T.IP[:], th, True, False), (out, sign[:], dl, False, stop)], rd + ["IP", "IM"], [bank])
+        mm([(out, T.IQ[:], th, True, False), (out, sign[:], dl, False, stop)], rd + ["IQ", "IQM"], [bank])
 
     def lay(t, x, banks):
         lo, lk = LO[x], "LO%d" % x
         ps, b0 = region(x, 0)
         for b in banks:
             v = rows(b)
-            if t == 0:
-                from_pair(x, ps[:, v], b0 + b, b, T.IM, True)
-                if x == 0 and b == 0:
-                    cp(lo[:, v], ps[:, v], (), [lk + str(b)], [b0 + b])
-                elif x == 0:
-                    act(lo[:, v], ps[:, v], (), [lk + str(b)], [b0 + b])
+            if t == 0 and x == 0:
+                from_pair(x, ps[:, v], b0 + b, b, T.IQM, True)
+                (cp if b < 2 else act)(lo[:, v], ps[:, v], (), [lk + str(b)], [b0 + b])
             else:
                 act(ps[:, v], lo[:, v], [lk + str(b)], (), [b0 + b])
 
@@ -408,21 +436,23 @@ def rank_program(g, core, T, topo):
         for b in banks:
             out, bank = ((PN[:], 7) if x and high else (PA[:], 6), (PN[:], 7),
                          ((PA[:, 0:C], 6), (PL[:, 2 * C:3 * C], 1), (PH[:, 2 * C:3 * C], 4))[x + high * x])[b]
-            from_pair(x, out, bank, b, T.IP if high else T.IM, True)
+            from_pair(x, out, bank, b, T.IQ if high else T.IQM, True)
             act((HI if high else LO)[x][:, rows(b)], out, (), ["%s%d%d" % ("HI" if high else "LO", x, b)], [bank])
 
-    def base(t, x, high, banks):
+    def base(t, x, high, banks, step=None):
         ps, b0 = region(x, 1 - high)
         for b in banks:
             v = rows(b)
             src, key = (HI[x], "HI%d%d" % (x, b)) if high else (LO[x], "LO%d%d" % (x, b))
             if t == 0:
-                from_pair(x, ps[:, v], b0 + b, b, T.IP if high else T.IM, False)
+                from_pair(x, ps[:, v], b0 + b, b, T.IQ if high else T.IQM, False)
             elif x == 0 and not high:
                 mm([(ps[:, v], T.IF[:], src[:, v], True, False)], [key, "IF"], [b0 + b])
             else:
-                mm([(ps[:, v], T.IP[:], T.TH[:, 0:v.stop - v.start], True, False)], THK + ["IP"], [b0 + b])
-                act(ps[:, v], src[:, v], [key], (), [b0 + b])
+                if step != 1:
+                    mm([(ps[:, v], T.IP[:], T.TH[:, 0:v.stop - v.start], True, False)], THK + ["IP"], [b0 + b])
+                if step != 0:
+                    act(ps[:, v], src[:, v], [key], (), [b0 + b])
 
     def spans(first, count):
         return [(max(first, p), min(first + count, q), b) for b, (p, q) in enumerate(BANKS) if max(first, p) < min(first + count, q)]
@@ -439,7 +469,7 @@ def rank_program(g, core, T, topo):
         PS, sb = region(x, 1)
         for lo_, hi_, b in spans(first, n):
             mm([(PS[:, lo_ * C:hi_ * C], wt[:], src[:, (p + lo_ - first) * C:(p + hi_ - first) * C], False, LAST[b] == step)],
-               [key, "IP16", "IM16"], [sb + b])
+               [key, "IP", "IM"], [sb + b])
 
     def lows(x, s):
         (PO, ob), n, pos = region(x, 0), 5 - s, (0, 4, 7, 9)[s - 1]
@@ -447,8 +477,8 @@ def rank_program(g, core, T, topo):
 
     def lows_add(x, s):
         n, pos = 5 - s, (0, 4, 7, 9)[s - 1]
-        add(x, T.LL, pos, 0, n, T.IM16, "LL%d" % s, None)
-        add(x, T.LL, pos, s, n, T.IP16, "LL%d" % s, None)
+        add(x, T.LL, pos, 0, n, T.IM, "LL%d" % s, None)
+        add(x, T.LL, pos, s, n, T.IP, "LL%d" % s, None)
 
     def highs(x, hook):
         (PO, ob), (PS, sb), hi, hks = region(x, 0), region(x, 1), HI[x], keys_of(x)[1]
@@ -458,10 +488,10 @@ def rank_program(g, core, T, topo):
             out = T.LH[:, pos * C:(pos + n) * C]
             if kind == "D":
                 tt(out, PO[:, 0:n * C], hi[:, s * C:5 * C], Op.is_le, hks, [key], banks_of(0, n, ob))
-                add(x, T.LH, pos, 0, n, T.IP16, key, (kind, s))
+                add(x, T.LH, pos, 0, n, T.IP, key, (kind, s))
             else:
                 tt(out, PO[:, s * C:5 * C], hi[:, 0:n * C], Op.is_gt, hks, [key], banks_of(s, n, ob))
-                add(x, T.LH, pos, s, n, T.IM16, key, (kind, s))
+                add(x, T.LH, pos, s, n, T.IM, key, (kind, s))
             pos += n
             if (kind, s) == ("U", 1):
                 act(T.E1[:], PS[:, 0:2 * C], (), ["E1"], [sb])
@@ -472,31 +502,52 @@ def rank_program(g, core, T, topo):
 
     def greatest(t, x, hook):
         (PS, sb), (pa, pk) = region(x, 1), pa_of(x)
-        base(t, x, 1, [0, 1, 2])
         spare = PS[:, 5 * C:6 * C]
         tt(T.E2[:], PS[:, 2 * C:4 * C], T.E1[:], Op.max, ["E1"], ["E2"], [sb + 1])
         hook("m1")
         tt(spare, PS[:, 4 * C:5 * C], T.E2[:, 0:C], Op.max, ["E2"], ["sp"], [sb + 2])
         hook("m2")
         tt(T.MM[:], spare, T.E2[:, C:2 * C], Op.max, ["E2", "sp"], ["MM"], [sb + 2])
-        hook("m3")
-        ts(spare, T.MM[:], BIG16, Op.add, ["MM"], ["sp"], -BIG16, Op.add, [sb + 2])
-        hook("m4")
-        if x == 1 and t < 2:
+        if x == 0:
+            act(T.RB[:], T.MM[:], ["MM"], ["RB"], bias=MID)
+            op("P", lambda: [g.tensor.matmul(pa, T.IM[:], T.RB[:], True, False), g.tensor.matmul(pa, T.IP[:], T.CK[:], False, False),
+                             g.tensor.matmul(pa, T.IF[:], T.MM[:], False, True)][-1], ["MM", "RB", "CK", "IM", "IP", "IF"], [pk], [6])
+            hook("m3")
+            return
+        ts(spare, T.MM[:], BIG1, Op.add, ["MM"], ["sp"], -BIG1, Op.add, [sb + 2])
+        if t < 2:
             a = 2 + t
             tt(wq(t + 1, 0, a), T.MM[:], spare, Op.subtract, ["MM", "sp"], wk(t + 1, a, "l"), [sb + 2])
             send("W%d_%dl" % (t + 1, a), wk(t + 1, a, "l"))
         tt(pa, T.MM[:], spare, Op.subtract, ["MM", "sp"], [pk], [sb + 2, 6])
 
-    def under(x, hook):
+    def under(x, hook, fold=0):
         (PO, ob), (pa, pk), hks = region(x, 0), pa_of(x), keys_of(x)[1]
         for b, (p, q) in enumerate(BANKS):
+            keys = ["CH%d%d" % (x, r) for r in range(p, q)]
             for r in range(p, q):
-                tt(T.CH[:, x, r * C:(r + 1) * C], pa, HI[x][:, r * C:(r + 1) * C], Op.is_gt, hks + [pk], ["CH%d%d" % (x, r)], [6])
-            mm([(PO[:, rows(b)], T.IP16[:], T.CH[:, x, rows(b)], False, True)], ["CH%d%d" % (x, r) for r in range(p, q)] + ["IP16"], [ob + b])
-            if b == 0:
-                act(T.E1[:], PO[:, 0:2 * C], (), ["E1"], [ob])
+                tt(T.CH[:, x, r * C:(r + 1) * C], pa, HI[x][:, r * C:(r + 1) * C], Op.is_gt, [hks[b], pk], [keys[r - p]], [6])
+            if not fold:
+                mm([(PO[:, rows(b)], T.IP[:], T.CH[:, x, rows(b)], False, True)], keys + ["IP"], [ob + b])
+                if b == 0:
+                    act(T.E1[:], PO[:, 0:2 * C], (), ["E1"], [ob])
             hook("c%d" % b)
+        if fold:
+            add_dma(HI[x][:], T.CH[:, x, :], ["CH%d%d" % (x, r) for r in range(5)], hks + ["HIP%d" % fold])
+
+    def fold(t, a):
+        k = called[0]
+        called[0] += 1
+        what, sem, (piece,) = plan[k]
+        assert what == "W%d_%df" % (t, a)
+        to, eng = route(T, topo, rank, 1)[1][0]
+        rid, pid = topo.addr(to, core)
+        tr = RemoteDMATransfer(dst_ids=[DstId(rid=rid, pnc=pid)], dma_engine_mask=bits(eng), remote_sem=T.sem["r%d" % k],
+                               srcs=[T.HI0[:, r * C:(r + 1) * C] for r in range(5)], dsts=[view(T, piece, 1)], alu_op=3)
+        op("G", lambda: g.remote_dma_fused([tr], local_sem=T.sem.sent), ["HIP%d" % t], (), (), ("sent", len(eng)))
+        mine = wk(t, a, "h") if sem else ["AX"]
+        op("X", None, (), keys_of(0)[1] + mine, (), ("bk%d" % t, len(back(topo, to, core, dst))))
+        return lambda: shift(piece, sem, mine)
 
     def least(x, B, bk_, between):
         PO, ob = region(x, 0)
@@ -510,7 +561,7 @@ def rank_program(g, core, T, topo):
 
     def low(x, r):
         pa, pk = pa_of(x)
-        tt(T.CL[:, x, r * C:(r + 1) * C], pa, LO[x][:, r * C:(r + 1) * C], Op.is_ge, keys_of(x)[0] + [pk], ["CL%d%d" % (x, r)], [6])
+        tt(T.CL[:, x, r * C:(r + 1) * C], pa, LO[x][:, r * C:(r + 1) * C], Op.is_ge, [keys_of(x)[0][r // 2], pk], ["CL%d%d" % (x, r)], [6])
 
     def key_open(t):
         lst, rd = placed(PKEY, t & 1)
@@ -526,7 +577,7 @@ def rank_program(g, core, T, topo):
         for a in both:
             v = slice(a * C, (a + 1) * C)
             if t == 1:
-                act(wq(3, 1, a), wq(2, 0, a), wk(2, a, "l"), wk(3, a, "h"), bias=0.125, scale=-1.0)
+                act(wq(3, 1, a), wq(2, 0, a), wk(2, a, "l"), wk(3, a, "h"), bias=WIDE, scale=-1.0)
             add_dma(W[t + 2][:, :, v], W[t + 1][:, :, v], wk(t + 1, a), wk(t + 2, a), ["aW%d" % (t + 1), "bW%d" % (t + 1)])
         for a in both if t == 1 else ():
             add_dma(wq(3, 0, a), wq(2, 1, a), wk(2, a), wk(3, a))
@@ -534,7 +585,7 @@ def rank_program(g, core, T, topo):
             send("W%d_%d" % (t + 2, a), wk(t + 2, a))
 
     def ask(t, m):
-        (cp if t == 2 and m < 2 else act)(T.GH[:, m, :], M[t][:].indirect(T.OFH[:, m, :]),
+        (cp if t == 2 and m != 2 else act)(T.GH[:, m, :], M[t][:].indirect(T.OFH[:, m, :]),
                                 ["M%d_%d" % (t, a) for a in range(4)] + ["Ms%d" % t, "OFH%d" % m],
                                 ["GH%d" % m], whole=["aM%d" % t] + (["cp%d" % t] if t else []))
 
@@ -579,12 +630,12 @@ def rank_program(g, core, T, topo):
         for j in range(4):
             lst += [(PN[:, 4:6, j, :], T.I35[:], T.F1[:]), (PN[:, 4:6, j, :], T.IM5[:], T.F2[:])]
         group(lst, ["FL%d" % par, "SO%d" % par, "IP", "I35", "IM5", "F1", "F2"], [7])
+        if t < 2:
+            act(T.SB[:], PAUX, (), ["SB"], [7], bias=-KEY)
         for j in range(4):
             tt(T.VE[:, :, j, :], T.KS[:, :, j, :], T.UV[:], Op.is_ge, ["KS", "UV"], ["VE%d" % j])
         if t == 2:
             ts(T.SB[:], PAUX, -KEY, Op.add, (), ["SB"], bk=[7])
-        else:
-            act(T.SB[:], PAUX, (), ["SB"], [7], bias=-KEY)
 
     def rows_in(t):
         lst = [(PROW, T.I8K[:], T.ST[:])]
@@ -606,7 +657,7 @@ def rank_program(g, core, T, topo):
             a = 2 * x + par
             v = slice(a * C, (a + 1) * C)
             dma("S", T.SV[:, v], wq(3, 0, a), "sv", wk(3, a, "l"), ["SV%d" % a])
-            act(T.YT[:, v], wq(3, 0, a), wk(3, a, "l"), ["YT%d" % a], bias=-0.125, scale=0.5)
+            act(T.YT[:, v], wq(3, 0, a), wk(3, a, "l"), ["YT%d" % a], bias=-0.125, scale=0.5 / F)
             dma("S", T.yt[:, v], T.YT[:, v], "out", ["YT%d" % a])
             act(T.DH[:, v], wq(3, 1, a), wk(3, a, "h") + ["C7"], ["DH%d" % a], bias=0.03125, scale=T.COL[:, 7:8])
 
@@ -659,49 +710,44 @@ def rank_program(g, core, T, topo):
         def hook_x(at, t=t):
             if t == 0 and at == "D2":
                 first_ends(1, 0, [0, 1])
-            if t == 0 and at in ("c0", "c2"):
-                first_ends(1, 1, [int(at[1]) // 2])
-            if t and at in ("D1", "D4"):
-                answer(1 + (at == "D4"))
-            if t and at == "D3":
+            if t and at in ("D1", "U1"):
+                answer(1 + (at == "U1"))
+            if t and at == "D4":
                 hop_on(1)
                 ask(t - 1, 2)
-            if t and at == "U2":
+            if t and at == "U3":
                 later(lambda: veto(t - 1))
             if at[0] in "Um":
-                drip({"U2": 1, "U3": 3, "U4": 3}.get(at, 2))
+                drip({"U3": 1, "m1": 3, "m2": 5}.get(at, 0))
+            if at == "U4":
+                base(t, 1, 0, [0, 1, 2], 0)
             if at == "U2":
                 lay(t, 1, [0])
             if at == "m1":
                 lay(t, 1, [1])
-            if at == "c0":
+            if at == "m3":
+                if t:
+                    fetch(t, 1, (1,))
+                else:
+                    first_ends(1, 1, [0, 1])
+                lows(1, 1)
                 drip(99)
+                if t:
+                    base(t, 1, 0, [0, 1, 2], 1)
                 lay(t, 1, [2])
-            if at == "c2":
-                base(t, 1, 0, [0])
-            if t and at == "c2":
-                rows_in(t - 1)
-                fetch(t, 1, (1,))
-
-        def lows_y(k, t=t):
-            if k == 1:
-                base(t, 1, 0, [1])
-            lows(1, k + 1)
+                lows(1, 2)
+                if t:
+                    rows_in(t - 1)
         highs(0, hook_x)
         greatest(t, 0, hook_x)
-        under(0, hook_x)
+        under(0, hook_x, t + 1)
         (pa, pk) = pa_of(0)
         if t < 2:
             act(wq(t + 1, 0, ax), pa, [pk], wk(t + 1, ax, "l"), [6])
-            least(0, wq(t + 1, 1, ax), wk(t + 1, ax, "h"), lows_y)
-        else:
-            least(0, T.AB[:], ["AB"], lows_y)
-        base(t, 1, 0, [2])
+            send("W%d_%dl" % (t + 1, ax), wk(t + 1, ax, "l"))
+        folded_shift = fold(t + 1, ax)
+        lows(1, 3)
         lows(1, 4)
-        if t == 2:
-            tt(wq(3, 0, ax), pa, T.AB[:], Op.add, [pk, "AB"], wk(3, ax, "l"), [6])
-            tt(wq(3, 1, ax), T.AB[:], pa, Op.subtract, [pk, "AB"], wk(3, ax, "h"), [6])
-        send("W%d_%d" % (t + 1, ax), wk(t + 1, ax))
         for s in range(1, 5):
             lows_add(1, s)
         if t:
@@ -711,15 +757,22 @@ def rank_program(g, core, T, topo):
 
         def hook_y(at, t=t, par=par):
             if at[0] == "D":
-                drip(2)
+                drip({"D1": 3, "D2": 3, "D4": 2}.get(at, 0))
             if at == "U1":
                 drip(99)
             if t == 2 and at == "U2":
                 theta_out(1)
             if t == 2 and at[0] == "U":
                 low(0, int(at[1]) - 1)
-            if at == "U4" and t:
+            if at == "U4":
+                base(t, 1, 1, [0, 1, 2])
+            if t and at == "U3":
                 names_out(1 - par, t)
+            if at == "c0" and t == 2:
+                pa, pk = pa_of(0)
+                tt(wq(3, 0, 0), pa, T.AX[:], Op.add, [pk, "AX"], wk(3, 0, "l"), [6])
+                tt(wq(3, 1, 0), T.AX[:], pa, Op.subtract, [pk, "AX"], wk(3, 0, "h"), [6])
+                send("W3_0", wk(3, 0))
             if at == "m1":
                 key_open(t)
                 key_add(0, 1)
@@ -732,12 +785,15 @@ def rank_program(g, core, T, topo):
         under(1, hook_y)
         (pa, pk) = pa_of(1)
         if t < 2:
+            folded_shift()
             least(1, wq(t + 1, 1, ay), wk(t + 1, ay, "h"), lambda k: k or low(0, 0))
             send("W%d_%dh" % (t + 1, ay), wk(t + 1, ay, "h"))
-            own(t + 1, 0)
+            own(t + 1, 0, 0)
             lay(t + 1, 0, [2])
             base(t + 1, 0, 0, [2])
-            own(t + 1, 1)
+            own(t + 1, 1, 0)
+            own(t + 1, 1, 1)
+            own(t + 1, 0, 1)
             drift(t)
             for x in range(2):
                 for r in range(1 - x, 4):
@@ -759,7 +815,7 @@ def rank_program(g, core, T, topo):
 
     def sources(n, a):
         act(D[n & 1][:, 0:4 * C], T.W3[:, 1, :].indirect(T.OFW[:, a >> 1, a & 1, :]), w3 + ["OFW%d" % (a & 1)],
-            ["D%d" % (n & 1), "HI%d0" % (n & 1), "HI%d1" % (n & 1)], bias=0.0625, scale=0.5, whole=["aW3", "bW3"])
+            ["D%d" % (n & 1), "HI%d0" % (n & 1), "HI%d1" % (n & 1)], bias=0.0625, scale=0.5 / F, whole=["aW3", "bW3"])
 
     def diffs(n, a, hs=(0, 1)):
         par, x = a & 1, a >> 1
@@ -772,7 +828,7 @@ def rank_program(g, core, T, topo):
         ps, b = region(n & 1, 0)
         for h in hs:
             act(ps[:, h * 512:(h + 1) * 512], Z[n & 1][:, h * 512:(h + 1) * 512], ["Z%d%d" % (n & 1, j) for j in (2 * h, 2 * h + 1)], (),
-                [b + h], scale=0.5, fn=Fn.Sigmoid)
+                [b + h], scale=0.5 / F, fn=Fn.Sigmoid)
 
     def weigh(n, a):
         ps, b = region(n & 1, 0)
@@ -828,22 +884,22 @@ def rank_program(g, core, T, topo):
     hop_on(1)
     ask(2, 2)
     answer(2)
-    diffs(0, 1, (0,))
+    diffs(0, 1)
     later(lambda: veto(2))
     drip(1)
     sources(0, 1)
-    diffs(0, 1, (1,))
+    sig(0)
+    diffs(1, 3, (0,))
     drip(99)
     rows_in(2)
-    sig(0)
-    diffs(1, 3)
+    diffs(1, 3, (1,))
     sources(1, 3)
     weigh(0, 1)
     sig(1)
+    weigh(1, 3)
     refs_out()
     rows_out(2)
     sources(2, 0)
-    weigh(1, 3)
     diffs(2, 0)
     sig(2)
     sources(3, 2)
@@ -882,6 +938,9 @@ def rank_program(g, core, T, topo):
     seen = {q: {} for q in "VAPGS"}
     need = []
     for i, d in enumerate(deps):
+        if ops[i][0] == "X":
+            need.append([])
+            continue
         mine, lst = seen[ops[i][0]], []
         newest = {}
         for j in d:
@@ -906,6 +965,8 @@ def rank_program(g, core, T, topo):
         value[j] = count[ops[j][0]]
     queue = {"V": g.vector, "A": g.scalar, "P": g.tensor, "G": g, "S": g.sync}
     for i, o in enumerate(ops):
+        if o[0] == "X":
+            continue
         for k in need[i]:
             if isinstance(k, int):
                 queue[o[0]].wait_ge(T.sem[ops[k][0]], value[k])

@@ -16,9 +16,9 @@ def _s(shape, d):
     return ("sbuf", [128] + shape, d)
 
 
-DIAG = {"IP": 1.0, "IQ": F, "IQM": -F, "IP16": 16.0, "I2": 2.0, "IM": -1.0, "I8": 8.0, "I8K": 8192.0, "I4K": 4096.0,
+DIAG = {"IP": 1.0, "IQ": F, "IQM": -F, "IM": -1.0, "IP16": 16.0, "I2": 2.0, "I8": 8.0, "I8K": 8192.0, "I4K": 4096.0,
         "I35": 3584.0, "IM5": -512.0, "IVE": -16384.0}
-EARLY = 5
+EARLY = 6
 SCRATCH = {
     "TH": _s([3072], b16), "DL": _s([3072], b16), "DR": _s([1024], b16),
     "W1": _s([2, 3072], f32), "W2": _s([2, 3072], f32), "W3": _s([2, 3072], f32),
@@ -45,7 +45,6 @@ SCRATCH = {
     "SB": _s([128], f32), "TK": _s([128], f32), "DD": _s([128], f32),
     "RH": _s([2, 2, 16], b16), "RS": _s([2, 2, 16], f32),
     "TI": _s([2, 2, 16, 32], b16),
-    "P0": _s([4 * C], f32), "P1": _s([4 * C], f32),
     "SV": _s([1024], f32), "YT": _s([1024], f32), "YQ": _s([1024], f32), "YR": _s([128], f32),
     "PL": ("psum", [128, 1536], f32), "PH": ("psum", [128, 1536], f32),
     "PA": ("psum", [128, 512], f32), "PN": ("psum", [128, 8, 4, 16], f32),
@@ -61,7 +60,10 @@ def pieces():
         return ("%s_%d%s" % (w, a, "lh"[k]), "ab"[k] + w, [(w, k, a * C, C // 2), (w, k, a * C + C // 2, C // 2)])
 
     def folded(w, a):
-        return ("%s_%df" % (w, a), None if w == "W3" else "b" + w, [(w, 1, a * C, C)])
+        return ("%s_%df" % (w, a), "b" + w, [(w, 1, a * C, C)]) if w != "W3" else home("AX", 0)
+
+    def home(buf, a):
+        return ("%s_%d" % (buf, a), None, [(buf, None, a * C, C)])
 
     def names(t, a, b, n):
         return ("M%d" % t, "aM%d" % t, [("M%d" % t, None, a, n), ("M%d" % t, None, b, n)])
@@ -69,13 +71,15 @@ def pieces():
     out += [ends("W1", 1), ends("W1", 3), names(0, 0, 1024, 1024)]
     out += [end("W1", 0, 0), folded("W1", 0), end("W1", 2, 0), end("W1", 2, 1), ends("W2", 0), ends("W2", 2)]
     out += [end("W2", 1, 0), folded("W2", 1), names(1, 0, 1024, 512), end("W2", 3, 0), end("W2", 3, 1), ends("W3", 1), ends("W3", 3)]
-    out += [folded("W3", 0), names(2, 512, 1536, 512), ends("W3", 0), end("W3", 2, 0), end("W3", 2, 1)]
+    out += [folded("W3", 0), names(2, 512, 1536, 512), end("W3", 0, 0), end("W3", 2, 0),
+            ("W3_h", "bW3", [("W3", 1, 0, C), ("W3", 1, 2 * C, C)])]
+    out += [home("YQ", 1)]
     return out
 
 
 SEMAPHORES = (["V", "A", "P", "G", "sent", "out", "cp1", "cp2", "aT", "aW1", "aW2", "aW3", "bW1", "bW2", "bW3", "aM0", "aM1", "aM2",
                "lt0", "lt1", "ld0", "ld1", "ldr", "lsl", "lrf", "sv"] + ["r%d" % k for k in range(len(pieces()))]
-              + ["gd%d" % k for k in range(9)] + ["bk1", "bk2", "bk3"])
+              + ["gd%d" % k for k in range(16)] + ["bk%d" % k for k, p in enumerate(pieces()) if len(p[2]) == 1])
 
 
 def view(T, piece, part, rows=slice(0, 128)):
@@ -102,40 +106,38 @@ def bits(engines):
     return sum(1 << e for e in engines)
 
 
-def onward(topo, core, dst, k):
-    eng = topo.engines(core, dst)
-    n = len(eng) // 2
-    return eng[k * n:(k + 1) * n] if k < 2 else eng
-
-
 def back(topo, core, src, dst):
     return [e for e in topo.engines(core, src) if e not in topo.engines(core, dst)]
+
+
+BEHIND = ("W1_2l", "W2_3l")
 
 
 def relay_program(g, core, T, topo, r):
     sent = 0
     src = T.cores[r]
-    for k, (_, sem, parts) in enumerate(pieces()):
+    waiting = []
+    for k, (name, sem, parts) in enumerate(pieces()):
         dst, ways = route(T, topo, r, len(parts))
         for part, (c, e) in zip(parts, ways):
             if c != core:
                 continue
             rid, pid = topo.addr(dst, core)
-            ap, eng = view(T, part, 1), onward(topo, core, dst, k)
+            ap, eng = view(T, part, 1 if sem else 0), topo.engines(core, dst)
             if len(parts) == 2:
                 g.wait_ge(T.sem["r%d" % k], len(e))
                 g.remote_dma(ap, ap, T.sem[sem], T.sem.sent, pid, rid, bits(eng))
             else:
                 home, (rid2, pid2) = back(topo, core, src, dst), topo.addr(src, core)
                 g.wait_ge(T.sem["r%d" % k], len(e))
-                trs = [RemoteDMATransfer(dst_ids=[DstId(rid=rid2, pnc=pid2)], dma_engine_mask=bits(home), remote_sem=T.sem["bk" + part[0][1]],
-                                         src=ap, dst=view(T, part, 0) if sem else T.AX[:])]
-                if sem:
-                    trs.append(RemoteDMATransfer(dst_ids=[DstId(rid=rid, pnc=pid)], dma_engine_mask=bits(eng),
-                                                 remote_sem=T.sem[sem], src=ap, dst=ap))
-                g.remote_dma_fused(trs, local_sem=T.sem.sent)
+                g.remote_dma(view(T, part, 0), ap, T.sem["bk%d" % k], T.sem.sent, pid2, rid2, bits(home))
                 sent += len(home) - (0 if sem else len(eng))
+                if sem:
+                    waiting.append((ap, sem))
             sent += len(eng)
+            if waiting and name in BEHIND:
+                ap, sem = waiting.pop()
+                g.remote_dma(ap, ap, T.sem[sem], T.sem.sent, pid, rid, bits(eng))
     if sent:
         g.wait_ge(T.sem.sent, sent)
 
@@ -187,16 +189,17 @@ def rank_program(g, core, T, topo):
 
     added = [0]
 
-    def add_dma(out, a, rd, wr, whole=()):
+    def add_dma(out, a, rd, wr, whole=(), add=True):
         sem = "gd%d" % added[0]
         added[0] += 1
-        op("G", lambda: g.dma_start(out, a, accum_op=Op.add).then_inc(T.sem[sem], 16), rd, wr, (), (sem, 16), whole)
+        how = {"accum_op": Op.add} if add else {}
+        op("G", lambda: g.dma_start(out, a, **how).then_inc(T.sem[sem], 16), rd, wr, (), (sem, 16), whole)
 
     plan = pieces()
     dst, halves = route(T, topo, rank, 2)
     for k, (_, sem, parts) in enumerate(plan):
         for c, e in route(T, topo, (rank + 1) % n_ranks, len(parts))[1]:
-            total[sem] = total.get(sem, 0) + len(e if c == core else onward(topo, c, core, k))
+            total[sem] = total.get(sem, 0) + len(e if c == core else topo.engines(c, core))
     called = [0]
 
     def send(name, rd, local=True, after=()):
@@ -250,7 +253,8 @@ def rank_program(g, core, T, topo):
         send("T%d" % h, [THK[h], DLK[h]], local=False)
     op("G", lambda: g.iota(T.PV[:], [[512, 2], [1024, 2], [32, 16]], 0, 0, allow_small_or_imprecise_dtypes=True), (), ["PV"])
     op("G", lambda: g.iota(T.KC[:], [[0, 2], [-int(KEY), 4], [0, 16]], 3 * int(KEY), 0, allow_small_or_imprecise_dtypes=True), (), ["KC"])
-    dma("S", T.DR[:], T.dr[:], "ldr", (), ["DR"])
+    dma("S", T.DR[:, C:4 * C], T.dr[:, C:4 * C], "ldr", (), ["DR"])
+    add_dma(T.DR[:, 0:C], T.dr[:, 0:C], (), ["DR0"], add=False)
     dma("S", T.SLI[:], T.sl[:], "lsl", (), ["SLI"])
     dma("S", T.RFI[:], T.rf[:], "lrf", (), ["RFI"])
     for buf, src in ((T.TH, T.th), (T.DL, T.dl)):
@@ -355,20 +359,23 @@ def rank_program(g, core, T, topo):
     def drifts():
         for a in (0, 2):
             v = slice(a * C, (a + 1) * C)
-            act(wq(2, 0, a), T.DR[:, v], ["DR"], wk(2, a, "l"), scale=F)
-            act(wq(2, 1, a), T.DR[:, v], ["DR"], wk(2, a, "h"), bias=WIDE, scale=F)
+            act(wq(2, 0, a), T.DR[:, v], ["DR", "DR0"], wk(2, a, "l"), scale=F)
+            act(wq(2, 1, a), T.DR[:, v], ["DR", "DR0"], wk(2, a, "h"), bias=WIDE, scale=F)
             act(wq(3, 0, a + 1), T.DR[:, (a + 1) * C:(a + 2) * C], ["DR"], wk(3, a + 1, "l"), bias=WIDE, scale=2 * F)
 
-    def first_names():
+    def first_names(pauses):
         n = len(ops)
         tables()
         fill = ops[n:]
         del ops[n:]
         later(lambda: [first_refs(), names([0, 1]), names_out(0, 0), names_out(1, 0)])
+        pauses = list(pauses)
         while held:
             drip(1)
             ops.extend(fill[:5])
             del fill[:5]
+            if pauses:
+                pauses.pop(0)()
         ops.extend(fill)
         send("M0", ["M0_%d" % a for a in range(4)])
 
@@ -388,8 +395,8 @@ def rank_program(g, core, T, topo):
                     act(T.DG[:, x, v], T.DL[:].indirect(off), DLK + [ok], ["DG0%d" % b], whole=["aT"])
             else:
                 off = T.OFW[:, x, par, :]
-                act(T.TG[:, x, :], T.TH[:].indirect(off), THK + [ok], ["TG10", "TG11"], whole=["aT"])
-                act(T.DG[:, x, :], T.DL[:].indirect(off), DLK + [ok], ["DG10", "DG11"], whole=["aT"])
+                act(T.TG[:, x, :], T.TH[:].indirect(off), THK + [ok], ["TG10", "TG11"], scale=F, whole=["aT"])
+                act(T.DG[:, x, :], T.DL[:].indirect(off), DLK + [ok], ["DG10", "DG11"], scale=F, whole=["aT"])
             return
         rd, wh = wkeys(t) + [ok], ["aW%d" % t]
         if x == 0 and 0 in ends:
@@ -413,22 +420,23 @@ def rank_program(g, core, T, topo):
     def region(x, k):
         return (PL, 0) if (x + k) & 1 == 0 else (PH, 3)
 
-    def from_pair(x, out, bank, b, sign, stop):
+    def from_pair(x, out, bank, b, high, stop):
         a, v = 2 * x, rows(b)
         if b < 2:
             th, dl, rd = T.TG[:, x, v], T.DG[:, x, v], ["TG%d%d" % (x, b), "DG%d%d" % (x, b)]
         else:
             th, dl, rd = T.TH[:, a * C:(a + 1) * C], T.DL[:, a * C:(a + 1) * C], THK + DLK
-        mm([(out, T.IQ[:], th, True, False), (out, sign[:], dl, False, stop)], rd + ["IQ", "IQM"], [bank])
+        plus, minus = (T.IP, T.IM) if x and b < 2 else (T.IQ, T.IQM)
+        mm([(out, plus[:], th, True, False), (out, (plus if high else minus)[:], dl, False, stop)], rd + ["IQ", "IQM", "IP", "IM"], [bank])
 
     def lay(t, x, banks):
         lo, lk = LO[x], "LO%d" % x
         ps, b0 = region(x, 0)
         for b in banks:
             v = rows(b)
-            if t == 0 and x == 0:
-                from_pair(x, ps[:, v], b0 + b, b, T.IQM, True)
-                (cp if b < 2 else act)(lo[:, v], ps[:, v], (), [lk + str(b)], [b0 + b])
+            if t == 0 and (x == 0 or b < 2):
+                from_pair(x, ps[:, v], b0 + b, b, 0, True)
+                (cp if (x, b) == (0, 1) else act)(lo[:, v], ps[:, v], (), [lk + str(b)], [b0 + b])
             else:
                 act(ps[:, v], lo[:, v], [lk + str(b)], (), [b0 + b])
 
@@ -436,7 +444,7 @@ def rank_program(g, core, T, topo):
         for b in banks:
             out, bank = ((PN[:], 7) if x and high else (PA[:], 6), (PN[:], 7),
                          ((PA[:, 0:C], 6), (PL[:, 2 * C:3 * C], 1), (PH[:, 2 * C:3 * C], 4))[x + high * x])[b]
-            from_pair(x, out, bank, b, T.IQ if high else T.IQM, True)
+            from_pair(x, out, bank, b, high, True)
             act((HI if high else LO)[x][:, rows(b)], out, (), ["%s%d%d" % ("HI" if high else "LO", x, b)], [bank])
 
     def base(t, x, high, banks, step=None):
@@ -445,7 +453,7 @@ def rank_program(g, core, T, topo):
             v = rows(b)
             src, key = (HI[x], "HI%d%d" % (x, b)) if high else (LO[x], "LO%d%d" % (x, b))
             if t == 0:
-                from_pair(x, ps[:, v], b0 + b, b, T.IQ if high else T.IQM, False)
+                from_pair(x, ps[:, v], b0 + b, b, high, False)
             elif x == 0 and not high:
                 mm([(ps[:, v], T.IF[:], src[:, v], True, False)], [key, "IF"], [b0 + b])
             else:
@@ -473,26 +481,27 @@ def rank_program(g, core, T, topo):
 
     def lows(x, s):
         (PO, ob), n, pos = region(x, 0), 5 - s, (0, 4, 7, 9)[s - 1]
-        tt(T.LL[:, pos * C:(pos + n) * C], PO[:, 0:n * C], LO[x][:, s * C:5 * C], Op.is_le, keys_of(x)[0] + ["L0"], ["LL%d" % s], banks_of(0, n, ob))
+        tt(T.LL[:, pos * C:(pos + n) * C], PO[:, 0:n * C], LO[x][:, s * C:5 * C], Op.is_le, keys_of(x)[0][s // 2:], ["LL%d" % s], banks_of(0, n, ob))
 
     def lows_add(x, s):
         n, pos = 5 - s, (0, 4, 7, 9)[s - 1]
         add(x, T.LL, pos, 0, n, T.IM, "LL%d" % s, None)
         add(x, T.LL, pos, s, n, T.IP, "LL%d" % s, None)
 
-    def highs(x, hook):
+    STEPS = [("D", s) for s in (4, 1, 2, 3)] + [("U", s) for s in range(1, 5)]
+
+    def highs(x, hook, steps=STEPS):
         (PO, ob), (PS, sb), hi, hks = region(x, 0), region(x, 1), HI[x], keys_of(x)[1]
-        pos = 0
-        for kind, s in [("D", s) for s in range(1, 5)] + [("U", s) for s in range(1, 5)]:
+        for kind, s in steps:
             n, key = 5 - s, "LH%s%d" % (kind, s)
+            pos = (0, 4, 7, 9)[s - 1] + 10 * (kind == "U")
             out = T.LH[:, pos * C:(pos + n) * C]
             if kind == "D":
-                tt(out, PO[:, 0:n * C], hi[:, s * C:5 * C], Op.is_le, hks, [key], banks_of(0, n, ob))
+                tt(out, PO[:, 0:n * C], hi[:, s * C:5 * C], Op.is_le, hks[s // 2:], [key], banks_of(0, n, ob))
                 add(x, T.LH, pos, 0, n, T.IP, key, (kind, s))
             else:
                 tt(out, PO[:, s * C:5 * C], hi[:, 0:n * C], Op.is_gt, hks, [key], banks_of(s, n, ob))
                 add(x, T.LH, pos, s, n, T.IM, key, (kind, s))
-            pos += n
             if (kind, s) == ("U", 1):
                 act(T.E1[:], PS[:, 0:2 * C], (), ["E1"], [sb])
             hook(kind + str(s))
@@ -535,19 +544,21 @@ def rank_program(g, core, T, topo):
         if fold:
             add_dma(HI[x][:], T.CH[:, x, :], ["CH%d%d" % (x, r) for r in range(5)], hks + ["HIP%d" % fold])
 
-    def fold(t, a):
+    def fold(name, srcs, alu, rd, mine, freed=()):
         k = called[0]
         called[0] += 1
         what, sem, (piece,) = plan[k]
-        assert what == "W%d_%df" % (t, a)
+        assert what == name
         to, eng = route(T, topo, rank, 1)[1][0]
         rid, pid = topo.addr(to, core)
         tr = RemoteDMATransfer(dst_ids=[DstId(rid=rid, pnc=pid)], dma_engine_mask=bits(eng), remote_sem=T.sem["r%d" % k],
-                               srcs=[T.HI0[:, r * C:(r + 1) * C] for r in range(5)], dsts=[view(T, piece, 1)], alu_op=3)
-        op("G", lambda: g.remote_dma_fused([tr], local_sem=T.sem.sent), ["HIP%d" % t], (), (), ("sent", len(eng)))
-        mine = wk(t, a, "h") if sem else ["AX"]
-        op("X", None, (), keys_of(0)[1] + mine, (), ("bk%d" % t, len(back(topo, to, core, dst))))
+                               srcs=srcs, dsts=[view(T, piece, 1 if sem else 0)], alu_op=alu)
+        op("G", lambda: g.remote_dma_fused([tr], local_sem=T.sem.sent), rd, (), (), ("sent", len(eng)))
+        op("X", None, (), list(freed) + mine, (), ("bk%d" % k, len(back(topo, to, core, dst))))
         return lambda: shift(piece, sem, mine)
+
+    def by_scalar(out, d, sign, rd, wr):
+        act(out, d, rd, wr, bias=256.0, scale=sign * 2.0 ** 29, fn=Fn.Sigmoid)
 
     def least(x, B, bk_, between):
         PO, ob = region(x, 0)
@@ -585,15 +596,17 @@ def rank_program(g, core, T, topo):
             send("W%d_%d" % (t + 2, a), wk(t + 2, a))
 
     def ask(t, m):
-        (cp if t == 2 and m != 2 else act)(T.GH[:, m, :], M[t][:].indirect(T.OFH[:, m, :]),
-                                ["M%d_%d" % (t, a) for a in range(4)] + ["Ms%d" % t, "OFH%d" % m],
-                                ["GH%d" % m], whole=["aM%d" % t] + (["cp%d" % t] if t else []))
+        rd = ["M%d_%d" % (t, a) for a in range(4)] + ["Ms%d" % t, "OFH%d" % m]
+        ways = [(act, 0, 32)] if t < 2 else [(cp, 0, 32)] if m == 3 else [(cp, 0, 16), (act, 16, 32)]
+        for fn, a, b in ways:
+            fn(T.GH[:, m, 16 * a:16 * b], M[t][:].indirect(T.OFH[:, m, a:b]), rd, ["GH%d%d" % (m, k) for k in range(a // 16, b // 16)],
+               whole=["aM%d" % t] + (["cp%d" % t] if t else []))
 
     def to_list(m, table, out):
         return [(out, T.TJ[:, table, 15 - i:143 - i], T.GH[:, m, i:512:16]) for i in range(16)]
 
     def answer(m):
-        group(to_list(m, 4, PN[:, 6:8, m, :]), ["GH%d" % m, "TJ4"], [7])
+        group(to_list(m, 4, PN[:, 6:8, m, :]), ["GH%d0" % m, "GH%d1" % m, "TJ4"], [7])
 
     def hop_on(m):
         ts(T.OFH[:, m + 1, :], PN[:, 6:8, m, :], -1.0, Op.mult, (), ["OFH%d" % (m + 1)], float(SENT), Op.add, [7])
@@ -623,7 +636,8 @@ def rank_program(g, core, T, topo):
         tt(r, T.U1[:], T.U2[:], Op.max, ["U1", "U2"], [rk])
         tt(T.UV[:], T.UV[:], T.MXF[:], Op.max, ["UV", "MXF"], ["UV"])
         cp(T.OFH[:, 3, :], r, [rk], ["OFH3"])
-        ask(t, 3)
+        if t < 2:
+            ask(t, 3)
         ts(T.F1[:], r, float(M1), Op.is_ge, [rk], ["F1"], 2.0, Op.mult)
         ts(T.F2[:], r, float(M2), Op.is_ge, [rk], ["F2"], 2.0, Op.mult)
         lst = [(PAUX, T.IP[:], T.FL[:, :, par]), (PAUX, T.IP[:], T.SO[:, :, par])]
@@ -632,16 +646,18 @@ def rank_program(g, core, T, topo):
         group(lst, ["FL%d" % par, "SO%d" % par, "IP", "I35", "IM5", "F1", "F2"], [7])
         if t < 2:
             act(T.SB[:], PAUX, (), ["SB"], [7], bias=-KEY)
+        else:
+            ask(t, 3)
+            ts(T.SB[:], PAUX, -KEY, Op.add, (), ["SB"], bk=[7])
         for j in range(4):
             tt(T.VE[:, :, j, :], T.KS[:, :, j, :], T.UV[:], Op.is_ge, ["KS", "UV"], ["VE%d" % j])
-        if t == 2:
-            ts(T.SB[:], PAUX, -KEY, Op.add, (), ["SB"], bk=[7])
 
     def rows_in(t):
         lst = [(PROW, T.I8K[:], T.ST[:])]
         for j in range(4):
             lst += to_list(3, j, PN[:, 2:4, j, :]) + [(PN[:, 2:4, j, :], T.I4K[:], T.F1[:])]
-        group(lst + [(PROW, T.IVE[:], T.VE[:])], ["ST", "I8K", "I4K", "IVE", "F1", "GH3"] + [k + str(j) for j in range(4) for k in ("VE", "TJ")], [7])
+        mm([m + (i == 0, False) for i, m in enumerate(lst)], ["ST", "I8K", "I4K", "F1", "GH30", "GH31"] + ["TJ%d" % j for j in range(4)], [7])
+        mm([(PROW, T.IVE[:], T.VE[:], False, True)], ["IVE"] + ["VE%d" % j for j in range(4)], [7])
 
     def rows_out(t):
         par = t & 1
@@ -678,23 +694,24 @@ def rank_program(g, core, T, topo):
         par = t & 1
         ax, ay = par, 2 + par
         if t == 0:
-            lay(0, 0, [2])
-            first_ends(0, 1, [2])
-            first_ends(1, 1, [2])
-            first_ends(1, 0, [2])
-            base(0, 0, 0, [2])
-            later(first_drift)
-            first_names()
+            first_names([lambda: [lay(0, 0, [2]), first_ends(0, 1, [2]), base(0, 0, 0, [2])], lambda: None,
+                         lambda: [first_ends(1, 1, [2]), first_ends(1, 0, [2])], lambda: None, first_drift])
             fetch(0, 0)
-            lay(0, 0, [0, 1])
+            later(lambda: [lay(0, 0, [0]), lows(0, 4), highs(0, lambda at: None, STEPS[:1])])
+            to_sbuf, add_d4 = held.pop(1), held.pop()
+            drip(99)
+            ops.append(to_sbuf)
+            lay(0, 0, [1])
             first_ends(0, 1, [0, 1])
             base(0, 0, 0, [0, 1])
+            ops.append(add_d4)
             fetch(0, 1)
         else:
             fetch(t, 0, (0,))
             elect(t - 1)
         for s in (3, 4, 1, 2):
-            lows(0, s)
+            if t or s != 4:
+                lows(0, s)
             lows_add(0, s)
             if t and s == 3:
                 fetch(t, 0, (1,))
@@ -708,78 +725,76 @@ def rank_program(g, core, T, topo):
                 fetch(t, 1, (0,))
 
         def hook_x(at, t=t):
-            if t == 0 and at == "D2":
-                first_ends(1, 0, [0, 1])
-            if t and at in ("D1", "U1"):
+            if t and at in ("D4", "U1"):
                 answer(1 + (at == "U1"))
-            if t and at == "D4":
+            if t and at == "D3":
                 hop_on(1)
                 ask(t - 1, 2)
             if t and at == "U3":
                 later(lambda: veto(t - 1))
             if at[0] in "Um":
                 drip({"U3": 1, "m1": 3, "m2": 5}.get(at, 0))
-            if at == "U4":
-                base(t, 1, 0, [0, 1, 2], 0)
-            if at == "U2":
+            if at == ("U2" if t else "U4"):
                 lay(t, 1, [0])
             if at == "m1":
                 lay(t, 1, [1])
+            if at == ("U4" if t else "m1"):
+                base(t, 1, 0, [0, 1, 2], 0)
             if at == "m3":
                 if t:
                     fetch(t, 1, (1,))
+                    lows(1, 1)
+                    drip(99)
+                    base(t, 1, 0, [0, 1, 2], 1)
+                    lay(t, 1, [2])
+                    lows(1, 2)
+                    rows_in(t - 1)
                 else:
                     first_ends(1, 1, [0, 1])
-                lows(1, 1)
-                drip(99)
-                if t:
-                    base(t, 1, 0, [0, 1, 2], 1)
-                lay(t, 1, [2])
-                lows(1, 2)
-                if t:
-                    rows_in(t - 1)
-        highs(0, hook_x)
+                    lay(t, 1, [2])
+                    for s in (4, 3, 2):
+                        lows(1, s)
+        highs(0, hook_x, STEPS[t == 0:])
         greatest(t, 0, hook_x)
         under(0, hook_x, t + 1)
         (pa, pk) = pa_of(0)
         if t < 2:
             act(wq(t + 1, 0, ax), pa, [pk], wk(t + 1, ax, "l"), [6])
             send("W%d_%dl" % (t + 1, ax), wk(t + 1, ax, "l"))
-        folded_shift = fold(t + 1, ax)
-        lows(1, 3)
-        lows(1, 4)
+        if t == 2:
+            act(wq(1, 1, 4), pa, [pk], ["NA0"], [6], scale=-1.0)
+            act(wq(1, 1, 5), wq(1, 1, 4), ["NA0"], ["NA1"])
+        folded_shift = fold("W%d_%df" % (t + 1, ax) if t < 2 else "AX_0", [T.HI0[:, r * C:(r + 1) * C] for r in range(5)], 3,
+                            ["HIP%d" % (t + 1)], wk(t + 1, ax, "h") if t < 2 else ["AX"], keys_of(0)[1])
+        for b in range(2) if t == 2 else ():
+            add_dma(T.LO0[:, rows(b)], T.W1[:, 1, 4 * C:6 * C], ["NA0", "NA1"], ["LO0%d" % b])
+        for s in (3, 4) if t else (1,):
+            lows(1, s)
         for s in range(1, 5):
             lows_add(1, s)
         if t:
             later(lambda: [rows_out(t - 1), names([1 - par])])
-        else:
-            drifts()
 
         def hook_y(at, t=t, par=par):
             if at[0] == "D":
-                drip({"D1": 3, "D2": 3, "D4": 2}.get(at, 0))
+                drip({"D1": 3, "D2": 3, "D3": 2}.get(at, 0))
             if at == "U1":
                 drip(99)
-            if t == 2 and at == "U2":
-                theta_out(1)
-            if t == 2 and at[0] == "U":
-                low(0, int(at[1]) - 1)
+            if t == 0 and at == "U2":
+                drifts()
+            if t == 2 and at == "c0":
+                by_scalar(T.CL[:, 0, :], T.LO0[:, 0:4 * C], -1.0, ["LO00", "LO01"], ["CL0%d" % r for r in range(4)])
             if at == "U4":
                 base(t, 1, 1, [0, 1, 2])
             if t and at == "U3":
                 names_out(1 - par, t)
-            if at == "c0" and t == 2:
-                pa, pk = pa_of(0)
-                tt(wq(3, 0, 0), pa, T.AX[:], Op.add, [pk, "AX"], wk(3, 0, "l"), [6])
-                tt(wq(3, 1, 0), T.AX[:], pa, Op.subtract, [pk, "AX"], wk(3, 0, "h"), [6])
-                send("W3_0", wk(3, 0))
             if at == "m1":
                 key_open(t)
                 key_add(0, 1)
-                if t == 2:
-                    key_add(0, 0)
             if at == "c2":
                 key_add(1, 1)
+                if t == 2:
+                    key_add(0, 0)
         highs(1, hook_y)
         greatest(t, 1, hook_y)
         under(1, hook_y)
@@ -800,17 +815,29 @@ def rank_program(g, core, T, topo):
                     low(x, r)
                 key_add(x, 0, x == 1)
         else:
-            least(1, T.AB[:], ["AB"], lambda k: k or low(1, 0))
+            def first_chunk(k, pa=pa_of(0)[0]):
+                if k == 0:
+                    low(1, 0)
+                elif k == 1:
+                    tt(wq(3, 0, 0), pa, T.AX[:], Op.add, ["pa0", "AX"], wk(3, 0, "l"), [6])
+                    send("W3_0l", wk(3, 0, "l"))
+                else:
+                    tt(wq(3, 1, 0), T.AX[:], pa, Op.subtract, ["pa0", "AX"], wk(3, 0, "h"), [6])
+            least(1, T.AB[:], ["AB"], first_chunk)
             tt(wq(3, 0, ay), pa, T.AB[:], Op.add, [pk, "AB"], wk(3, ay, "l"), [6])
             send("W3_%dl" % ay, wk(3, ay, "l"))
-            tt(wq(3, 1, ay), T.AB[:], pa, Op.subtract, [pk, "AB"], wk(3, ay, "h"), [6])
-            send("W3_%dh" % ay, wk(3, ay, "h"))
             for r in range(1, 4):
                 low(1, r)
             key_add(1, 0, True)
+            tt(wq(3, 1, ay), T.AB[:], pa, Op.subtract, [pk, "AB"], wk(3, ay, "h"), [6])
+            send("W3_h", wk(3, ax, "h") + wk(3, ay, "h"))
+            theta_out(1)
             theta_out(0)
 
-    Z, D, P = LO, HI, [T.P0, T.P1]
+    Z, D = LO, HI
+
+    def prod(n, j, m=1):
+        return T.W1[:, n & 1, 1024 * (1 + n // 2) + j * C:1024 * (1 + n // 2) + (j + m) * C]
     w3 = wkeys(3)
 
     def sources(n, a):
@@ -835,23 +862,30 @@ def rank_program(g, core, T, topo):
         y = ps[:, 4 * C:5 * C]
         for js in ((0, 1), (2, 3)):
             v = slice(js[0] * C, (js[-1] + 1) * C)
-            keys = ["P%d%d" % (n & 1, j) for j in js]
-            tt(P[n & 1][:, v], ps[:, v], D[n & 1][:, v], Op.mult, ["D%d" % (n & 1)], keys, [b + js[0] // 2])
-            mm([(y, T.IF[:], P[n & 1][:, j * C:(j + 1) * C], j == 0, j == 3) for j in js], ["IF"] + keys, [b + 2])
+            keys = ["P%d%d" % (n, j) for j in js]
+            tt(prod(n, js[0], 2), ps[:, v], D[n & 1][:, v], Op.mult, ["D%d" % (n & 1)], keys + ["NA0", "NA1"], [b + js[0] // 2])
+            if n:
+                mm([(y, T.IF[:], prod(n, j), j == 0, j == 3) for j in js], ["IF"] + keys, [b + 2])
+        if n == 0:
+            v = slice(a * C, (a + 1) * C)
+            fold("YQ_%d" % a, [prod(n, j) for j in range(4)] + [T.DH[:, v]], 1, ["P%d%d" % (n, j) for j in range(4)] + ["DH%d" % a], ["YQ%d" % a])
+
+    def store(a):
+        dma("S", T.yq[:, a * C:(a + 1) * C], T.YQ[:, a * C:(a + 1) * C], "out", ["YQ%d" % a])
 
     def weigh_last(n, a):
-        (ps, b), p, d, dk = region(n & 1, 0), P[n & 1], D[n & 1], "D%d" % (n & 1)
+        (ps, b), d, dk = region(n & 1, 0), D[n & 1], "D%d" % (n & 1)
         y, v = ps[:, 4 * C:5 * C], slice(a * C, (a + 1) * C)
         row = [slice(j * C, (j + 1) * C) for j in range(4)]
-        keys = ["P%d%d" % (n & 1, j) for j in range(4)]
+        keys = ["P%d%d" % (n, j) for j in range(4)]
         mm([(y, T.IF[:], T.DH[:, v], True, False)], ["IF", "DH%d" % a], [b + 2])
         for j in range(3):
-            tt(p[:, row[j]], ps[:, row[j]], d[:, row[j]], Op.mult, [dk], [keys[j]], [b + j // 2])
+            tt(prod(n, j), ps[:, row[j]], d[:, row[j]], Op.mult, [dk], [keys[j]], [b + j // 2])
             if j < 2:
-                mm([(y, T.IF[:], p[:, row[j]], False, j == 1)], ["IF", keys[j]], [b + 2])
+                mm([(y, T.IF[:], prod(n, j), False, j == 1)], ["IF", keys[j]], [b + 2])
         tt(ps[:, row[3]], ps[:, row[3]], d[:, row[3]], Op.mult, [dk], ["PL3"], [b + 1])
-        tt(p[:, row[3]], ps[:, row[3]], p[:, row[2]], Op.add, ["PL3", keys[2]], [keys[3]], [b + 1])
-        tt(T.YQ[:, v], y, p[:, row[3]], Op.add, [keys[3]], ["YQ%d" % a], [b + 2])
+        tt(prod(n, 3), ps[:, row[3]], prod(n, 2), Op.add, ["PL3", keys[2]], [keys[3]], [b + 1])
+        tt(T.YQ[:, v], y, prod(n, 3), Op.add, [keys[3]], ["YQ%d" % a], [b + 2])
         dma("S", T.yq[:, v], T.YQ[:, v], "out", ["YQ%d" % a])
 
     def y_out(n, a):
@@ -884,35 +918,38 @@ def rank_program(g, core, T, topo):
     hop_on(1)
     ask(2, 2)
     answer(2)
-    diffs(0, 1)
+    sources(0, 1)
+    diffs(0, 1, (0,))
     later(lambda: veto(2))
     drip(1)
-    sources(0, 1)
+    diffs(0, 1, (1,))
     sig(0)
-    diffs(1, 3, (0,))
     drip(99)
     rows_in(2)
-    diffs(1, 3, (1,))
     sources(1, 3)
-    weigh(0, 1)
+    diffs(1, 3)
     sig(1)
-    weigh(1, 3)
+    weigh(0, 1)
     refs_out()
     rows_out(2)
     sources(2, 0)
+    weigh(1, 3)
     diffs(2, 0)
     sig(2)
     sources(3, 2)
-    y_out(0, 1)
     diffs(3, 2, (0,))
+    y_out(1, 3)
+    later(lambda: weigh_last(3, 2))
+    drip(0)
     weigh(2, 0)
     sig(3, (0,))
     diffs(3, 2, (1,))
     sig(3, (1,))
     refs_store()
-    y_out(1, 3)
+    store(1)
+    drip(2)
     y_out(2, 0)
-    weigh_last(3, 2)
+    drip(99)
 
     writer, readers, bank = {}, {}, {}
     deps = []

from concourse.bass import DstId, RemoteDMATransfer
from concourse.mybir import AluOpType as Op, ActivationFunctionType as Fn

C = 256
SENT = 2048
M1, M2 = SENT + 32, SENT + 32 + 2048
KEY = 8192.0
BIG1, BIG16, BIG32 = 1.5 * 2.0 ** 23, 1.5 * 2.0 ** 27, 1.5 * 2.0 ** 28
F = 1.0 / 16
WIDE = 0.125 * F
MID = 192.0
f32, b16, i32, u16 = "float32", "bfloat16", "int32", "uint16"


def _s(shape, d):
    return ("sbuf", [128] + shape, d)


DIAG = {"IP": 1.0, "IQ": F, "IQM": -F, "IM": -1.0, "IP16": 16.0, "I2": 2.0, "I8": 8.0, "I8K": 8192.0, "I4K": 4096.0,
        "I35": 3584.0, "IM5": -512.0, "IVE": -16384.0}
EARLY = 6
SCRATCH = {
    "TH": _s([3072], b16), "DL": _s([3072], b16), "DR": _s([1024], b16),
    "W1": _s([2, 3072], f32), "W2": _s([2, 3072], f32), "W3": _s([2, 3072], f32),
    "M0": _s([M2 + 2048], b16), "M1": _s([M2 + 2048], b16), "M2": _s([M2 + 2048], b16),
    "SLI": _s([2, 2, 4, 16], i32), "RFI": _s([64], i32),
    "XI": _s([144], f32), "PI": _s([8], i32), "PJ": _s([8], i32), "COL": _s([8], f32),
    "E16": _s([16], f32), "KM": _s([8], f32), "IC": _s([128], b16),
    "IF": _s([128], f32), "RO": _s([2, 2, 16], b16), "UV": _s([2, 16], f32), "DH": _s([1024], f32),
    "TN": _s([144], b16), "TNP": _s([144], b16), "TNM": _s([144], b16), "TJ": _s([5, 144], b16),
    "PV": _s([2, 2, 16], f32), "PVN": _s([2, 2, 3, 16], f32), "KC": _s([2, 4, 16], b16),
    "SP": _s([2, 2, 4, 16], f32), "RF": _s([64], f32), "R": _s([2, 2, 16], f32),
    "OFW": _s([2, 2, 64], u16), "OFH": _s([4, 32], u16),
    "RD": _s([2, 3, 4, 16], f32), "FL": _s([2, 3, 4, 16], b16), "SO": _s([2, 3, 4, 16], b16),
    "S1": _s([2, 3, 4, 16], b16), "S2": _s([2, 3, 4, 16], b16),
    "LO0": _s([5 * C], f32), "LO1": _s([5 * C], f32), "HI0": _s([5 * C], f32), "HI1": _s([5 * C], f32),
    "TG": _s([2, 4 * C], b16), "DG": _s([2, 4 * C], b16),
    "LL": _s([10 * C], b16), "LH": _s([20 * C], b16), "CH": _s([2, 5 * C], b16), "CL": _s([2, 4 * C], b16),
    "E1": _s([2 * C], f32), "E2": _s([2 * C], f32), "MM": _s([C], f32), "AB": _s([C], f32), "AX": _s([C], f32), "RB": _s([C], b16), "CK": _s([C], b16),
    "GH": _s([4, 512], b16),
    "KS": _s([2, 4, 16], f32), "K2": _s([2, 2, 16], f32), "MXI": _s([32], i32), "MXF": _s([32], f32), "CI": _s([32], i32),
    "EQ": _s([2, 4, 16], b16), "U1": _s([32], f32), "U2": _s([32], f32),
    "ST": _s([2, 4, 16], b16), "VE": _s([2, 4, 16], b16),
    "NS": _s([32], b16), "F1": _s([32], b16), "F2": _s([32], b16),
    "SB": _s([128], f32), "TK": _s([128], f32), "DD": _s([128], f32),
    "RH": _s([2, 2, 16], b16), "RS": _s([2, 2, 16], f32),
    "TI": _s([2, 2, 16, 32], b16),
    "SV": _s([1024], f32), "YT": _s([1024], f32), "YQ": _s([1024], f32), "YR": _s([128], f32),
    "PL": ("psum", [128, 1536], f32), "PH": ("psum", [128, 1536], f32),
    "PA": ("psum", [128, 512], f32), "PN": ("psum", [128, 8, 4, 16], f32),
}
SCRATCH.update({k: _s([128], b16) for k in DIAG})


def pieces():
    def ends(w, a):
        return ("%s_%d" % (w, a), "a" + w, [(w, 0, a * C, C), (w, 1, a * C, C)])

    def end(w, a, k):
        return ("%s_%d%s" % (w, a, "lh"[k]), "ab"[k] + w, [(w, k, a * C, C // 2), (w, k, a * C + C // 2, C // 2)])

    def folded(w, a):
        return ("%s_%df" % (w, a), "b" + w, [(w, 1, a * C, C)]) if w != "W3" else home("AX", 0)

    def home(buf, a):
        return ("%s_%d" % (buf, a), None, [(buf, None, a * C, C)])

    def names(t, a, b, n):
        return ("M%d" % t, "aM%d" % t, [("M%d" % t, None, a, n), ("M%d" % t, None, b, n)])
    out = [("T%d" % h, "aT", [("TH", None, h * 512, 512), ("DL", None, h * 512, 512)]) for h in range(2)]
    out += [ends("W1", 1), ends("W1", 3), names(0, 0, 1024, 1024)]
    out += [end("W1", 0, 0), folded("W1", 0), end("W1", 2, 0), end("W1", 2, 1), ends("W2", 0), ends("W2", 2)]
    out += [end("W2", 1, 0), folded("W2", 1), names(1, 0, 1024, 512), end("W2", 3, 0), end("W2", 3, 1), ends("W3", 1), ends("W3", 3)]
    out += [folded("W3", 0), names(2, 512, 1536, 512), end("W3", 0, 0), end("W3", 2, 0),
            ("W3_h", "bW3", [("W3", 1, 0, C), ("W3", 1, 2 * C, C)])]
    out += [home("YQ", 1)]
    return out


SEMAPHORES = (["V", "A", "P", "G", "sent", "out", "cp1", "cp2", "aT", "aW1", "aW2", "aW3", "bW1", "bW2", "bW3", "aM0", "aM1", "aM2",
               "lt0", "lt1", "ld0", "ld1", "ldr", "lsl", "lrf", "sv"] + ["r%d" % k for k in range(len(pieces()))]
              + ["gd%d" % k for k in range(16)] + ["bk%d" % k for k, p in enumerate(pieces()) if len(p[2]) == 1])


def view(T, piece, part, rows=slice(0, 128)):
    buf, k, a, n = piece
    a += (0, M1, M2)[part] if buf[0] == "M" else 1024 * part
    return T[buf][rows, a:a + n] if k is None else T[buf][rows, k, a:a + n]


def route(T, topo, r, parts):
    src, dst = T.cores[r], T.cores[(r - 1) % len(T.cores)]
    able = [c for c in topo.cores_of(src) if c != src and T.rank_of(c) is None and topo.may_write(c, dst)]
    far = [c for c in able if topo.die(c) != topo.die(src)][0]
    near = [c for c in able if topo.die(c) == topo.die(src)][0]
    eng = topo.engines(src, near)
    if parts == 1:
        return dst, [(far if topo.may_write(src, dst) else near, eng)]
    if topo.may_write(src, dst):
        out = topo.engines(src, dst)
        return dst, [(dst, out), (far, [e for e in eng if e not in out])]
    return dst, [(near, eng[:len(eng) // 2]), (far, eng[len(eng) // 2:])]


def bits(engines):
    return sum(1 << e for e in engines)


def back(topo, core, src, dst):
    return [e for e in topo.engines(core, src) if e not in topo.engines(core, dst)]


BEHIND = ("W1_2l", "W2_3l")


def relay_program(g, core, T, topo, r):
    sent = 0
    src = T.cores[r]
    waiting = []
    for k, (name, sem, parts) in enumerate(pieces()):
        dst, ways = route(T, topo, r, len(parts))
        for part, (c, e) in zip(parts, ways):
            if c != core:
                continue
            rid, pid = topo.addr(dst, core)
            ap, eng = view(T, part, 1 if sem else 0), topo.engines(core, dst)
            if len(parts) == 2:
                g.wait_ge(T.sem["r%d" % k], len(e))
                g.remote_dma(ap, ap, T.sem[sem], T.sem.sent, pid, rid, bits(eng))
            else:
                home, (rid2, pid2) = back(topo, core, src, dst), topo.addr(src, core)
                g.wait_ge(T.sem["r%d" % k], len(e))
                g.remote_dma(view(T, part, 0), ap, T.sem["bk%d" % k], T.sem.sent, pid2, rid2, bits(home))
                sent += len(home) - (0 if sem else len(eng))
                if sem:
                    waiting.append((ap, sem))
            sent += len(eng)
            if waiting and name in BEHIND:
                ap, sem = waiting.pop()
                g.remote_dma(ap, ap, T.sem[sem], T.sem.sent, pid, rid, bits(eng))
    if sent:
        g.wait_ge(T.sem.sent, sent)


def rank_program(g, core, T, topo):
    rank = T.rank_of(core)
    n_ranks = len(T.cores)
    if rank is None:
        for r in range(n_ranks):
            if core in topo.cores_of(T.cores[r]):
                relay_program(g, core, T, topo, r)
        return
    ops = []
    total = {}

    def op(q, fn, rd=(), wr=(), bk=(), dma=None, whole=()):
        ops.append([q, fn, list(rd), list(wr), list(bk), dma, list(whole)])
        if dma:
            total[dma[0]] = total.get(dma[0], 0) + dma[1]

    def tt(out, a, b, o, rd, wr, bk=(), whole=()):
        op("V", lambda: g.vector.tensor_tensor(out, a, b, o), rd, wr, bk, None, whole)

    def ts(out, a, s1, o0, rd, wr, s2=None, o1=None, bk=(), whole=()):
        if s2 is None:
            op("V", lambda: g.vector.tensor_scalar(out, a, s1, None, o0), rd, wr, bk, None, whole)
        else:
            op("V", lambda: g.vector.tensor_scalar(out, a, s1, s2, o0, o1), rd, wr, bk, None, whole)

    def cp(out, a, rd, wr, bk=(), whole=()):
        op("V", lambda: g.vector.tensor_copy(out, a), rd, wr, bk, None, whole)

    def act(out, a, rd, wr, bk=(), bias=0.0, scale=1.0, fn=Fn.Identity, whole=()):
        op("A", lambda: g.scalar.activation(out, a, fn, bias=bias, scale=scale), rd, wr, bk, None, whole)

    def mm(lst, rd, bk):
        def emit():
            for m in lst:
                last = g.tensor.matmul(*m)
            return last
        op("P", emit, rd, (), bk)

    def group(terms, rd, bk):
        mm([(o, w, x, i == 0, i == len(terms) - 1) for i, (o, w, x) in enumerate(terms)], rd, bk)

    def dma(q, out, a, sem, rd, wr=(), whole=()):
        e = g.sync if q == "S" else g.scalar
        op(q, lambda: e.dma_start(out, a).then_inc(T.sem[sem], 16), rd, wr, (), (sem, 16), whole)

    added = [0]

    def add_dma(out, a, rd, wr, whole=(), add=True):
        sem = "gd%d" % added[0]
        added[0] += 1
        how = {"accum_op": Op.add} if add else {}
        op("G", lambda: g.dma_start(out, a, **how).then_inc(T.sem[sem], 16), rd, wr, (), (sem, 16), whole)

    plan = pieces()
    dst, halves = route(T, topo, rank, 2)
    for k, (_, sem, parts) in enumerate(plan):
        for c, e in route(T, topo, (rank + 1) % n_ranks, len(parts))[1]:
            total[sem] = total.get(sem, 0) + len(e if c == core else topo.engines(c, core))
    called = [0]

    def send(name, rd, local=True, after=()):
        k = called[0]
        called[0] += 1
        what, sem, two = plan[k]
        assert what == name
        trs = []
        for piece, (to, eng) in zip(two, halves):
            rid, pid = topo.addr(to, core)
            trs.append(RemoteDMATransfer(dst_ids=[DstId(rid=rid, pnc=pid)], dma_engine_mask=bits(eng),
                                         remote_sem=T.sem[sem if to == dst else "r%d" % k],
                                         src=view(T, piece, 0), dst=view(T, piece, 1)))
        op("G", lambda: g.remote_dma_fused(trs, local_sem=T.sem.sent), rd, (), (), ("sent", sum(len(e) for _, e in halves)), after)
        if local:
            (buf, k0, a, n), (_, k1, a2, _) = two
            if k0 != k1:
                two = [(buf, slice(0, 2), a, n)]
            elif a + n == a2:
                two = [(buf, k0, a, 2 * n)]
            for piece in two:
                shift(piece, sem, rd, after)

    def shift(piece, sem, rd, after=()):
        dma("S", view(T, piece, 2, slice(0, 112)), view(T, piece, 0, slice(16, 128)), sem, rd, (), after)
        dma("S", view(T, piece, 2, slice(112, 128)), view(T, piece, 0, slice(0, 16)), sem, rd)

    W = [None, T.W1, T.W2, T.W3]
    M = [T.M0, T.M1, T.M2]
    LO, HI = [T.LO0, T.LO1], [T.HI0, T.HI1]
    PL, PH, PA, PN = T.PL, T.PH, T.PA, T.PN
    THK, DLK = ["TH0", "TH1"], ["DL0", "DL1"]
    PKEY, PROW, PAUX, PHOP = PN[:, 0:2], PN[:, 2:4], PN[:, 4:6], PN[:, 6:8, 3, :]

    def wq(t, k, a):
        return W[t][:, k, a * C:(a + 1) * C]

    def wk(t, a, s="lh"):
        return ["W%d_%d%s" % (t, a, c) for c in s]

    def wkeys(t):
        return [k for a in range(4) for k in wk(t, a)]

    for h in range(2):
        v = slice(h * 512, (h + 1) * 512)
        dma("S", T.TH[:, v], T.th[:, v], "lt%d" % h, (), [THK[h]])
        dma("A", T.DL[:, v], T.dl[:, v], "ld%d" % h, (), [DLK[h]])
    op("G", lambda: g.iota(T.PI[:], [[0, 8]], 0, 1), (), ["PI"])
    op("G", lambda: g.iota(T.XI[:], [[1, 144]], 0, 0, allow_small_or_imprecise_dtypes=True), (), ["XI"])
    for h in range(2):
        send("T%d" % h, [THK[h], DLK[h]], local=False)
    op("G", lambda: g.iota(T.PV[:], [[512, 2], [1024, 2], [32, 16]], 0, 0, allow_small_or_imprecise_dtypes=True), (), ["PV"])
    op("G", lambda: g.iota(T.KC[:], [[0, 2], [-int(KEY), 4], [0, 16]], 3 * int(KEY), 0, allow_small_or_imprecise_dtypes=True), (), ["KC"])
    dma("S", T.DR[:, C:4 * C], T.dr[:, C:4 * C], "ldr", (), ["DR"])
    add_dma(T.DR[:, 0:C], T.dr[:, 0:C], (), ["DR0"], add=False)
    dma("S", T.SLI[:], T.sl[:], "lsl", (), ["SLI"])
    dma("S", T.RFI[:], T.rf[:], "lrf", (), ["RFI"])
    for buf, src in ((T.TH, T.th), (T.DL, T.dl)):
        dma("S", buf[0:112, 2048:3072], src[16:128, :], "aT", ())
        dma("S", buf[112:128, 2048:3072], src[0:16, :], "aT", ())
    op("V", lambda: g.vector.memset(T.TI[:], 0.0), (), ["TI0", "TI1"])
    op("V", lambda: g.vector.memset(T.CK[:], MID), (), ["CK"])
    for t in range(3):
        op("V", lambda t=t: g.vector.memset(M[t][:, SENT:M1], 0.0), (), ["Ms%d" % t])
    for k, m in ((0, 127), (1, 15), (2, 31), (3, 16), (4, 112)):
        ts(T.PJ[:, k:k + 1], T.PI[:, k:k + 1], m, Op.bitwise_and, ["PI"], ["PJ%d" % k])
    cp(T.COL[:, 0:5], T.PJ[:, 0:5], ["PJ%d" % k for k in range(5)], ["C0"])
    ts(T.IP[:], T.XI[:, 0:128], T.COL[:, 0:1], Op.is_equal, ["XI", "C0"], ["IP"])
    ts(T.COL[:, 5:6], T.COL[:, 3:4], -1.0, Op.mult, ["C0"], ["C5"], 8.0, Op.add)
    ts(T.COL[:, 4:5], T.COL[:, 4:5], 15.0, Op.add, ["C0"], ["C4"])
    for key, v in list(DIAG.items())[1:EARLY]:
        ts(T[key][:], T.IP[:], v, Op.mult, ["IP"], [key])
    ts(T.IC[:], T.IP[:], T.COL[:, 5:6], Op.mult, ["IP", "C5"], ["IC"])
    act(T.COL[:, 6:7], T.COL[:, 0:1], ["C0"], ["C6"], scale=0.0, fn=Fn.Sigmoid)
    act(T.COL[:, 7:8], T.COL[:, 6:7], ["C6"], ["C7"], scale=0.5 / F)
    cp(T.RF[:], T.RFI[:], ["RFI"], ["RF"])
    cp(T.SP[:], T.SLI[:], ["SLI"], ["SP0", "SP1"])
    cp(T.OFW[:], T.SLI[:], ["SLI"], ["OFW0", "OFW1"])

    def first_drift():
        for x, ps in enumerate((PL, PH)):
            a = 2 * x + 1
            v = slice(a * C, (a + 1) * C)
            for k, sign in enumerate((T.IQM, T.IQ)):
                out = ps[:, k * C:(k + 1) * C]
                group([(out, T.IQ[:], T.TH[:, v]), (out, sign[:], T.DL[:, v]), (out, T.IQ[:], T.DR[:, v])],
                      THK + DLK + ["DR", "IQ", "IQM"], [3 * x])
            act(W[1][:, :, v], ps[:, 0:2 * C], (), wk(1, a), [3 * x])
        for a in (1, 3):
            send("W1_%d" % a, wk(1, a), after=["aT"])

    def cut(b, ks):
        return b[:, 0, 2] if ks == [2] else b[:, :, ks[0] if len(ks) == 1 else slice(0, 2)]

    def placing(src, keys, ks):
        def named(b):
            return [b + str(k) for k in ks]
        ts(cut(T.RD, ks), src, -7.5, Op.add, keys, named("RD"), BIG16, Op.add)
        act(cut(T.FL, ks), cut(T.RD, ks), named("RD"), named("FL"), bias=-BIG16)
        act(cut(T.S1, ks), src, keys, named("S1"), bias=-1023.5, fn=Fn.Sign)
        act(cut(T.S2, ks), src, keys, named("S2"), bias=-2047.5, fn=Fn.Sign)
        tt(cut(T.SO, ks), src, cut(T.FL, ks), Op.subtract, keys + named("FL"), named("SO"))

    def placed(out, k):
        return ([(out, w[:], cut(b, [k])) for w, b in ((T.IP, T.SO), (T.I2, T.FL), (T.IP16, T.S1), (T.IC, T.S2))],
                [b + str(k) for b in ("FL", "SO", "S1", "S2")] + ["IP", "I2", "IP16", "IC"])

    def first_refs():
        placing(T.RF[:], ["RF"], [2])
        group(*placed(PN[:, 0], 2), [7])
        act(T.R[:], PN[:, 0], (), ["R0", "R1"], [7], bias=24.0)

    def names(ks):
        v = ks[0] if len(ks) == 1 else slice(0, 2)
        act(T.RS[:, :, v], T.R[:, :, v], ["R%d" % k for k in ks], ["RS"], bias=float(SENT), scale=-1.0, fn=Fn.Relu)
        act(T.RH[:, :, v], T.RS[:, :, v], ["RS"], ["RH"])
        placing(T.SP[:, :, v], ["SP%d" % k for k in ks], ks)
        tt(T.RO[:, :, v], T.RS[:, :, v], T.RH[:, :, v], Op.subtract, ["RS", "RH"], ["RO"])
        for k in ks:
            parts = [b[:, :, k, j, :] for b in (T.FL, T.SO) for j in range(4)] + [T.RH[:, :, k], T.RO[:, :, k]]
            mm([(PN[:, :, :, s], T.IP[:], p, True, True) for s, p in enumerate(parts)], ["FL%d" % k, "SO%d" % k, "RH", "RO", "IP"], [7])
            for s in (0, 16):
                act(T.TI[:, :, k, :, s:s + 10], PN[:, :, :, 0:10], ["TI%d" % k], ["TI%d%d" % (k, s)], [7])

    def names_out(par, t):
        ti = "TI%d" % par
        for x in range(2):
            a = 2 * x + par
            op("V", lambda x=x, a=a: g.vector.transpose(M[t][:, a * 512:(a + 1) * 512], T.TI[:, x, par]),
               [ti, ti + "0", ti + "16"], ["M%d_%d" % (t, a)])
        if t:
            send("M%d" % t, ["M%d_%d" % (t, par), "M%d_%d" % (t, 2 + par)])

    def carry(t, par):
        for part in (0, M1, M2):
            for x in range(2):
                a = part + (2 * x + par) * 512
                dma("S", M[t][:, a:a + 512], M[t - 1][:, a:a + 512], "cp%d" % t,
                    ["M%d_%d" % (t - 1, 2 * x + par)], (), ["aM%d" % (t - 1)])

    def tables():
        for key, v in list(DIAG.items())[EARLY:]:
            ts(T[key][:], T.IP[:], v, Op.mult, ["IP"], [key])
        cp(T.IF[:], T.IP[:], ["IP"], ["IF"])
        ts(T.TN[:], T.XI[:], T.COL[:, 4:5], Op.is_equal, ["XI", "C4"], ["TN"])
        ts(T.E16[:], T.XI[:, 0:16], T.COL[:, 1:2], Op.is_equal, ["XI", "C0"], ["E16"])
        ts(T.PV[:], T.PV[:], T.COL[:, 2:3], Op.add, ["PV", "C0"], ["PV"])
        tt(T.KM[:, 0:4], T.E16[:, 0:4], T.E16[:, 4:8], Op.add, ["E16"], ["KM"])
        tt(T.KM[:, 4:5], T.E16[:, 8:9], T.E16[:, 9:10], Op.add, ["E16"], ["KM4"])
        ts(T.TNP[:], T.TN[:], 4 * KEY, Op.mult, ["TN"], ["TNP"])
        ts(T.TNM[:], T.TN[:], -4 * KEY, Op.mult, ["TN"], ["TNM"])
        for m in range(3):
            ts(T.PVN[:, :, :, m, :], T.PV[:], -1.0, Op.mult, ["PV"], ["PVN%d" % m], float(SENT), Op.add)
        for k in range(5):
            ts(T.TJ[:, k, :], T.TN[:], T.KM[:, k:k + 1], Op.mult, ["TN", "KM", "KM4"], ["TJ%d" % k])

    def drifts():
        for a in (0, 2):
            v = slice(a * C, (a + 1) * C)
            act(wq(2, 0, a), T.DR[:, v], ["DR", "DR0"], wk(2, a, "l"), scale=F)
            act(wq(2, 1, a), T.DR[:, v], ["DR", "DR0"], wk(2, a, "h"), bias=WIDE, scale=F)
            act(wq(3, 0, a + 1), T.DR[:, (a + 1) * C:(a + 2) * C], ["DR"], wk(3, a + 1, "l"), bias=WIDE, scale=2 * F)

    def first_names(pauses):
        n = len(ops)
        tables()
        fill = ops[n:]
        del ops[n:]
        later(lambda: [first_refs(), names([0, 1]), names_out(0, 0), names_out(1, 0)])
        pauses = list(pauses)
        while held:
            drip(1)
            ops.extend(fill[:5])
            del fill[:5]
            if pauses:
                pauses.pop(0)()
        ops.extend(fill)
        send("M0", ["M0_%d" % a for a in range(4)])

    BANKS = [(0, 2), (2, 4), (4, 5)]

    def rows(b):
        return slice(BANKS[b][0] * C, BANKS[b][1] * C)

    def fetch(t, x, ends=(0, 1)):
        par = t & 1
        lo, lk, ok = LO[x], "LO%d" % x, "OFW%d" % par
        if t == 0:
            if x == 0:
                for b in range(2):
                    v, off = rows(b), T.OFW[:, x, par, 32 * b:32 * b + 32]
                    cp(T.TG[:, x, v], T.TH[:].indirect(off), THK + [ok], ["TG0%d" % b], whole=["aT"])
                    act(T.DG[:, x, v], T.DL[:].indirect(off), DLK + [ok], ["DG0%d" % b], whole=["aT"])
            else:
                off = T.OFW[:, x, par, :]
                act(T.TG[:, x, :], T.TH[:].indirect(off), THK + [ok], ["TG10", "TG11"], scale=F, whole=["aT"])
                act(T.DG[:, x, :], T.DL[:].indirect(off), DLK + [ok], ["DG10", "DG11"], scale=F, whole=["aT"])
            return
        rd, wh = wkeys(t) + [ok], ["aW%d" % t]
        if x == 0 and 0 in ends:
            cp(lo[:, rows(0)], W[t][:, 0, :].indirect(T.OFW[:, x, par, 0:32]), rd, [lk + "0"], whole=wh)
            act(lo[:, rows(1)], W[t][:, 0, :].indirect(T.OFW[:, x, par, 32:64]), rd, [lk + "1"], whole=wh)
            lay(t, x, [0, 1])
            base(t, x, 0, [0, 1])
        elif 0 in ends:
            act(lo[:, 0:4 * C], W[t][:, 0, :].indirect(T.OFW[:, x, par, :]), rd, [lk + "0", lk + "1"], whole=wh)
        if 1 in ends:
            act(HI[x][:, 0:4 * C], W[t][:, 1, :].indirect(T.OFW[:, x, par, :]), rd, ["HI%d0" % x, "HI%d1" % x], bias=WIDE,
                whole=wh + ["bW%d" % t])

    def own(t, x, high):
        a = 2 * x + (t & 1)
        if high:
            act(HI[x][:, rows(2)], wq(t, 1, a), wk(t, a, "h"), ["HI%d2" % x], bias=WIDE)
        else:
            act(LO[x][:, rows(2)], wq(t, 0, a), wk(t, a, "l"), ["LO%d2" % x])

    def region(x, k):
        return (PL, 0) if (x + k) & 1 == 0 else (PH, 3)

    def from_pair(x, out, bank, b, high, stop):
        a, v = 2 * x, rows(b)
        if b < 2:
            th, dl, rd = T.TG[:, x, v], T.DG[:, x, v], ["TG%d%d" % (x, b), "DG%d%d" % (x, b)]
        else:
            th, dl, rd = T.TH[:, a * C:(a + 1) * C], T.DL[:, a * C:(a + 1) * C], THK + DLK
        plus, minus = (T.IP, T.IM) if x and b < 2 else (T.IQ, T.IQM)
        mm([(out, plus[:], th, True, False), (out, (plus if high else minus)[:], dl, False, stop)], rd + ["IQ", "IQM", "IP", "IM"], [bank])

    def lay(t, x, banks):
        lo, lk = LO[x], "LO%d" % x
        ps, b0 = region(x, 0)
        for b in banks:
            v = rows(b)
            if t == 0 and (x == 0 or b < 2):
                from_pair(x, ps[:, v], b0 + b, b, 0, True)
                (cp if (x, b) == (0, 1) else act)(lo[:, v], ps[:, v], (), [lk + str(b)], [b0 + b])
            else:
                act(ps[:, v], lo[:, v], [lk + str(b)], (), [b0 + b])

    def first_ends(x, high, banks):
        for b in banks:
            out, bank = ((PN[:], 7) if x and high else (PA[:], 6), (PN[:], 7),
                         ((PA[:, 0:C], 6), (PL[:, 2 * C:3 * C], 1), (PH[:, 2 * C:3 * C], 4))[x + high * x])[b]
            from_pair(x, out, bank, b, high, True)
            act((HI if high else LO)[x][:, rows(b)], out, (), ["%s%d%d" % ("HI" if high else "LO", x, b)], [bank])

    def base(t, x, high, banks, step=None):
        ps, b0 = region(x, 1 - high)
        for b in banks:
            v = rows(b)
            src, key = (HI[x], "HI%d%d" % (x, b)) if high else (LO[x], "LO%d%d" % (x, b))
            if t == 0:
                from_pair(x, ps[:, v], b0 + b, b, high, False)
            elif x == 0 and not high:
                mm([(ps[:, v], T.IF[:], src[:, v], True, False)], [key, "IF"], [b0 + b])
            else:
                if step != 1:
                    mm([(ps[:, v], T.IP[:], T.TH[:, 0:v.stop - v.start], True, False)], THK + ["IP"], [b0 + b])
                if step != 0:
                    act(ps[:, v], src[:, v], [key], (), [b0 + b])

    def spans(first, count):
        return [(max(first, p), min(first + count, q), b) for b, (p, q) in enumerate(BANKS) if max(first, p) < min(first + count, q)]

    def banks_of(first, count, b0):
        return [b0 + b for _, _, b in spans(first, count)]

    def keys_of(x):
        return ["LO%d%d" % (x, b) for b in range(3)], ["HI%d%d" % (x, b) for b in range(3)]

    LAST = {0: ("U", 1), 1: ("U", 3), 2: ("U", 4)}

    def add(x, src, p, first, n, wt, key, step):
        PS, sb = region(x, 1)
        for lo_, hi_, b in spans(first, n):
            mm([(PS[:, lo_ * C:hi_ * C], wt[:], src[:, (p + lo_ - first) * C:(p + hi_ - first) * C], False, LAST[b] == step)],
               [key, "IP", "IM"], [sb + b])

    def lows(x, s):
        (PO, ob), n, pos = region(x, 0), 5 - s, (0, 4, 7, 9)[s - 1]
        tt(T.LL[:, pos * C:(pos + n) * C], PO[:, 0:n * C], LO[x][:, s * C:5 * C], Op.is_le, keys_of(x)[0][s // 2:], ["LL%d" % s], banks_of(0, n, ob))

    def lows_add(x, s):
        n, pos = 5 - s, (0, 4, 7, 9)[s - 1]
        add(x, T.LL, pos, 0, n, T.IM, "LL%d" % s, None)
        add(x, T.LL, pos, s, n, T.IP, "LL%d" % s, None)

    STEPS = [("D", s) for s in (4, 1, 2, 3)] + [("U", s) for s in range(1, 5)]

    def highs(x, hook, steps=STEPS):
        (PO, ob), (PS, sb), hi, hks = region(x, 0), region(x, 1), HI[x], keys_of(x)[1]
        for kind, s in steps:
            n, key = 5 - s, "LH%s%d" % (kind, s)
            pos = (0, 4, 7, 9)[s - 1] + 10 * (kind == "U")
            out = T.LH[:, pos * C:(pos + n) * C]
            if kind == "D":
                tt(out, PO[:, 0:n * C], hi[:, s * C:5 * C], Op.is_le, hks[s // 2:], [key], banks_of(0, n, ob))
                add(x, T.LH, pos, 0, n, T.IP, key, (kind, s))
            else:
                tt(out, PO[:, s * C:5 * C], hi[:, 0:n * C], Op.is_gt, hks, [key], banks_of(s, n, ob))
                add(x, T.LH, pos, s, n, T.IM, key, (kind, s))
            if (kind, s) == ("U", 1):
                act(T.E1[:], PS[:, 0:2 * C], (), ["E1"], [sb])
            hook(kind + str(s))

    def pa_of(x):
        return PA[:, x * C:(x + 1) * C], "pa%d" % x

    def greatest(t, x, hook):
        (PS, sb), (pa, pk) = region(x, 1), pa_of(x)
        spare = PS[:, 5 * C:6 * C]
        tt(T.E2[:], PS[:, 2 * C:4 * C], T.E1[:], Op.max, ["E1"], ["E2"], [sb + 1])
        hook("m1")
        tt(spare, PS[:, 4 * C:5 * C], T.E2[:, 0:C], Op.max, ["E2"], ["sp"], [sb + 2])
        hook("m2")
        tt(T.MM[:], spare, T.E2[:, C:2 * C], Op.max, ["E2", "sp"], ["MM"], [sb + 2])
        if x == 0:
            act(T.RB[:], T.MM[:], ["MM"], ["RB"], bias=MID)
            op("P", lambda: [g.tensor.matmul(pa, T.IM[:], T.RB[:], True, False), g.tensor.matmul(pa, T.IP[:], T.CK[:], False, False),
                             g.tensor.matmul(pa, T.IF[:], T.MM[:], False, True)][-1], ["MM", "RB", "CK", "IM", "IP", "IF"], [pk], [6])
            hook("m3")
            return
        ts(spare, T.MM[:], BIG1, Op.add, ["MM"], ["sp"], -BIG1, Op.add, [sb + 2])
        if t < 2:
            a = 2 + t
            tt(wq(t + 1, 0, a), T.MM[:], spare, Op.subtract, ["MM", "sp"], wk(t + 1, a, "l"), [sb + 2])
            send("W%d_%dl" % (t + 1, a), wk(t + 1, a, "l"))
        tt(pa, T.MM[:], spare, Op.subtract, ["MM", "sp"], [pk], [sb + 2, 6])

    def under(x, hook, fold=0):
        (PO, ob), (pa, pk), hks = region(x, 0), pa_of(x), keys_of(x)[1]
        for b, (p, q) in enumerate(BANKS):
            keys = ["CH%d%d" % (x, r) for r in range(p, q)]
            for r in range(p, q):
                tt(T.CH[:, x, r * C:(r + 1) * C], pa, HI[x][:, r * C:(r + 1) * C], Op.is_gt, [hks[b], pk], [keys[r - p]], [6])
            if not fold:
                mm([(PO[:, rows(b)], T.IP[:], T.CH[:, x, rows(b)], False, True)], keys + ["IP"], [ob + b])
                if b == 0:
                    act(T.E1[:], PO[:, 0:2 * C], (), ["E1"], [ob])
            hook("c%d" % b)
        if fold:
            add_dma(HI[x][:], T.CH[:, x, :], ["CH%d%d" % (x, r) for r in range(5)], hks + ["HIP%d" % fold])

    def fold(name, srcs, alu, rd, mine, freed=()):
        k = called[0]
        called[0] += 1
        what, sem, (piece,) = plan[k]
        assert what == name
        to, eng = route(T, topo, rank, 1)[1][0]
        rid, pid = topo.addr(to, core)
        tr = RemoteDMATransfer(dst_ids=[DstId(rid=rid, pnc=pid)], dma_engine_mask=bits(eng), remote_sem=T.sem["r%d" % k],
                               srcs=srcs, dsts=[view(T, piece, 1 if sem else 0)], alu_op=alu)
        op("G", lambda: g.remote_dma_fused([tr], local_sem=T.sem.sent), rd, (), (), ("sent", len(eng)))
        op("X", None, (), list(freed) + mine, (), ("bk%d" % k, len(back(topo, to, core, dst))))
        return lambda: shift(piece, sem, mine)

    def by_scalar(out, d, sign, rd, wr):
        act(out, d, rd, wr, bias=256.0, scale=sign * 2.0 ** 29, fn=Fn.Sigmoid)

    def least(x, B, bk_, between):
        PO, ob = region(x, 0)
        spare = PO[:, 5 * C:6 * C]
        between(0)
        tt(T.E2[:], PO[:, 2 * C:4 * C], T.E1[:], Op.min, ["E1"], ["E2"], [ob + 1])
        between(1)
        tt(spare, PO[:, 4 * C:5 * C], T.E2[:, 0:C], Op.min, ["E2"], ["sq"], [ob + 2])
        between(2)
        tt(B, spare, T.E2[:, C:2 * C], Op.min, ["E2", "sq"], bk_, [ob + 2])

    def low(x, r):
        pa, pk = pa_of(x)
        tt(T.CL[:, x, r * C:(r + 1) * C], pa, LO[x][:, r * C:(r + 1) * C], Op.is_ge, [keys_of(x)[0][r // 2], pk], ["CL%d%d" % (x, r)], [6])

    def key_open(t):
        lst, rd = placed(PKEY, t & 1)
        mm([m + (i == 0, False) for i, m in enumerate(lst + [(PKEY, T.IP[:], T.KC[:])])], rd + ["KC"], [7])

    def key_add(x, high, stop=False):
        src, wt, key = (T.CH, T.TNM, "CH") if high else (T.CL, T.TNP, "CL")
        mm([(PN[:, x], wt[:, 15 - i:143 - i], src[:, x, i:4 * C:16], False, stop and i == 15) for i in range(16)],
           ["%s%d%d" % (key, x, r) for r in range(4)] + ["TNP", "TNM"], [7])

    def drift(t):
        both = (t, 2 + t)
        for a in both:
            v = slice(a * C, (a + 1) * C)
            if t == 1:
                act(wq(3, 1, a), wq(2, 0, a), wk(2, a, "l"), wk(3, a, "h"), bias=WIDE, scale=-1.0)
            add_dma(W[t + 2][:, :, v], W[t + 1][:, :, v], wk(t + 1, a), wk(t + 2, a), ["aW%d" % (t + 1), "bW%d" % (t + 1)])
        for a in both if t == 1 else ():
            add_dma(wq(3, 0, a), wq(2, 1, a), wk(2, a), wk(3, a))
        for a in both:
            send("W%d_%d" % (t + 2, a), wk(t + 2, a))

    def ask(t, m):
        rd = ["M%d_%d" % (t, a) for a in range(4)] + ["Ms%d" % t, "OFH%d" % m]
        ways = [(act, 0, 32)] if t < 2 else [(cp, 0, 32)] if m == 3 else [(cp, 0, 16), (act, 16, 32)]
        for fn, a, b in ways:
            fn(T.GH[:, m, 16 * a:16 * b], M[t][:].indirect(T.OFH[:, m, a:b]), rd, ["GH%d%d" % (m, k) for k in range(a // 16, b // 16)],
               whole=["aM%d" % t] + (["cp%d" % t] if t else []))

    def to_list(m, table, out):
        return [(out, T.TJ[:, table, 15 - i:143 - i], T.GH[:, m, i:512:16]) for i in range(16)]

    def answer(m):
        group(to_list(m, 4, PN[:, 6:8, m, :]), ["GH%d0" % m, "GH%d1" % m, "TJ4"], [7])

    def hop_on(m):
        ts(T.OFH[:, m + 1, :], PN[:, 6:8, m, :], -1.0, Op.mult, (), ["OFH%d" % (m + 1)], float(SENT), Op.add, [7])

    def elect(t):
        ts(T.KS[:], PKEY, 24.0, Op.add, (), ["KS"], bk=[7])
        tt(T.K2[:], T.KS[:, :, 0:2, :], T.KS[:, :, 2:4, :], Op.max, ["KS"], ["K2"])
        tt(T.MXI[:], T.K2[:, :, 0, :], T.K2[:, :, 1, :], Op.max, ["K2"], ["MXI"])
        ts(T.CI[:], T.MXI[:], int(KEY) - 1, Op.bitwise_and, ["MXI"], ["CI"])
        ts(T.OFH[:, 0, :], T.CI[:], float(SENT), Op.min, ["CI"], ["OFH0"])
        ask(t, 0)

    def beside(t):
        act(T.ST[:], T.KS[:], ["KS"], ["ST"], bias=0.5 - 36 * KEY, fn=Fn.Sign)
        ts(T.MXF[:], T.MXI[:], 36 * KEY, Op.max, ["MXI"], ["MXF"])
        ts(T.NS[:], T.MXI[:], 36 * KEY, Op.is_lt, ["MXI"], ["NS"])
        tt(T.EQ[:, :, 3, :], T.CI[:], T.PV[:, t & 1], Op.is_equal, ["CI", "PV"], ["EQ3"])

    def veto(t):
        par = t & 1
        r, rk = T.R[:, :, par], "R%d" % par
        tt(T.EQ[:, :, 0:3, :], PN[:, 6:8, 0:3, :], T.PVN[:, par], Op.is_equal, ["PVN0", "PVN1", "PVN2"], ["EQ"], [7])
        group([(PHOP, T.I8K[:], T.NS[:])] + [(PHOP, T.I8K[:], T.EQ[:, :, m, :]) for m in (3, 0, 1, 2)], ["EQ", "EQ3", "NS", "I8K"], [7])
        tt(T.U1[:], T.CI[:], PHOP, Op.subtract, ["CI"], ["U1"], [7])
        tt(T.U2[:], r, PHOP, Op.min, [rk], ["U2"], [7])
        ts(T.UV[:], PHOP, -128.0, Op.mult, (), ["UV"], 128 * KEY, Op.add, [7])
        tt(r, T.U1[:], T.U2[:], Op.max, ["U1", "U2"], [rk])
        tt(T.UV[:], T.UV[:], T.MXF[:], Op.max, ["UV", "MXF"], ["UV"])
        cp(T.OFH[:, 3, :], r, [rk], ["OFH3"])
        if t < 2:
            ask(t, 3)
        ts(T.F1[:], r, float(M1), Op.is_ge, [rk], ["F1"], 2.0, Op.mult)
        ts(T.F2[:], r, float(M2), Op.is_ge, [rk], ["F2"], 2.0, Op.mult)
        lst = [(PAUX, T.IP[:], T.FL[:, :, par]), (PAUX, T.IP[:], T.SO[:, :, par])]
        for j in range(4):
            lst += [(PN[:, 4:6, j, :], T.I35[:], T.F1[:]), (PN[:, 4:6, j, :], T.IM5[:], T.F2[:])]
        group(lst, ["FL%d" % par, "SO%d" % par, "IP", "I35", "IM5", "F1", "F2"], [7])
        if t < 2:
            act(T.SB[:], PAUX, (), ["SB"], [7], bias=-KEY)
        else:
            ask(t, 3)
            ts(T.SB[:], PAUX, -KEY, Op.add, (), ["SB"], bk=[7])
        for j in range(4):
            tt(T.VE[:, :, j, :], T.KS[:, :, j, :], T.UV[:], Op.is_ge, ["KS", "UV"], ["VE%d" % j])

    def rows_in(t):
        lst = [(PROW, T.I8K[:], T.ST[:])]
        for j in range(4):
            lst += to_list(3, j, PN[:, 2:4, j, :]) + [(PN[:, 2:4, j, :], T.I4K[:], T.F1[:])]
        mm([m + (i == 0, False) for i, m in enumerate(lst)], ["ST", "I8K", "I4K", "F1", "GH30", "GH31"] + ["TJ%d" % j for j in range(4)], [7])
        mm([(PROW, T.IVE[:], T.VE[:], False, True)], ["IVE"] + ["VE%d" % j for j in range(4)], [7])

    def rows_out(t):
        par = t & 1
        sp = "SP%d" % par
        ts(PAUX, PROW, 1024.0, Op.is_lt, (), ["TK"], bk=[7])
        tt(T.DD[:], PROW, T.SB[:], Op.subtract, ["SB"], ["DD"], [7])
        tt(PROW, PAUX, T.DD[:], Op.mult, ["DD", "TK"], ["DT"], [7])
        tt(T.SP[:, :, par], PROW, T.SP[:, :, par], Op.add, [sp, "DT"], [sp], [7])
        cp(T.OFW[:, :, par, :], T.SP[:, :, par], [sp], ["OFW%d" % par])

    def theta_out(par):
        for x in range(2):
            a = 2 * x + par
            v = slice(a * C, (a + 1) * C)
            dma("S", T.SV[:, v], wq(3, 0, a), "sv", wk(3, a, "l"), ["SV%d" % a])
            act(T.YT[:, v], wq(3, 0, a), wk(3, a, "l"), ["YT%d" % a], bias=-0.125, scale=0.5 / F)
            dma("S", T.yt[:, v], T.YT[:, v], "out", ["YT%d" % a])
            act(T.DH[:, v], wq(3, 1, a), wk(3, a, "h") + ["C7"], ["DH%d" % a], bias=0.03125, scale=T.COL[:, 7:8])

    held = []

    def later(fn):
        n = len(ops)
        fn()
        held.extend(ops[n:])
        del ops[n:]

    def drip(n):
        while held and (n > 0 or held[0][0] != "V"):
            n -= held[0][0] == "V"
            ops.append(held.pop(0))

    for t in range(3):
        par = t & 1
        ax, ay = par, 2 + par
        if t == 0:
            first_names([lambda: [lay(0, 0, [2]), first_ends(0, 1, [2]), base(0, 0, 0, [2])], lambda: None,
                         lambda: [first_ends(1, 1, [2]), first_ends(1, 0, [2])], lambda: None, first_drift])
            fetch(0, 0)
            later(lambda: [lay(0, 0, [0]), lows(0, 4), highs(0, lambda at: None, STEPS[:1])])
            to_sbuf, add_d4 = held.pop(1), held.pop()
            drip(99)
            ops.append(to_sbuf)
            lay(0, 0, [1])
            first_ends(0, 1, [0, 1])
            base(0, 0, 0, [0, 1])
            ops.append(add_d4)
            fetch(0, 1)
        else:
            fetch(t, 0, (0,))
            elect(t - 1)
        for s in (3, 4, 1, 2):
            if t or s != 4:
                lows(0, s)
            lows_add(0, s)
            if t and s == 3:
                fetch(t, 0, (1,))
                beside(t - 1)
                carry(t, par)
            if t and s == 4:
                answer(0)
            if t and s == 2:
                hop_on(0)
                ask(t - 1, 1)
                fetch(t, 1, (0,))

        def hook_x(at, t=t):
            if t and at in ("D4", "U1"):
                answer(1 + (at == "U1"))
            if t and at == "D3":
                hop_on(1)
                ask(t - 1, 2)
            if t and at == "U3":
                later(lambda: veto(t - 1))
            if at[0] in "Um":
                drip({"U3": 1, "m1": 3, "m2": 5}.get(at, 0))
            if at == ("U2" if t else "U4"):
                lay(t, 1, [0])
            if at == "m1":
                lay(t, 1, [1])
            if at == ("U4" if t else "m1"):
                base(t, 1, 0, [0, 1, 2], 0)
            if at == "m3":
                if t:
                    fetch(t, 1, (1,))
                    lows(1, 1)
                    drip(99)
                    base(t, 1, 0, [0, 1, 2], 1)
                    lay(t, 1, [2])
                    lows(1, 2)
                    rows_in(t - 1)
                else:
                    first_ends(1, 1, [0, 1])
                    lay(t, 1, [2])
                    for s in (4, 3, 2):
                        lows(1, s)
        highs(0, hook_x, STEPS[t == 0:])
        greatest(t, 0, hook_x)
        under(0, hook_x, t + 1)
        (pa, pk) = pa_of(0)
        if t < 2:
            act(wq(t + 1, 0, ax), pa, [pk], wk(t + 1, ax, "l"), [6])
            send("W%d_%dl" % (t + 1, ax), wk(t + 1, ax, "l"))
        if t == 2:
            act(wq(1, 1, 4), pa, [pk], ["NA0"], [6], scale=-1.0)
            act(wq(1, 1, 5), wq(1, 1, 4), ["NA0"], ["NA1"])
        folded_shift = fold("W%d_%df" % (t + 1, ax) if t < 2 else "AX_0", [T.HI0[:, r * C:(r + 1) * C] for r in range(5)], 3,
                            ["HIP%d" % (t + 1)], wk(t + 1, ax, "h") if t < 2 else ["AX"], keys_of(0)[1])
        for b in range(2) if t == 2 else ():
            add_dma(T.LO0[:, rows(b)], T.W1[:, 1, 4 * C:6 * C], ["NA0", "NA1"], ["LO0%d" % b])
        for s in (3, 4) if t else (1,):
            lows(1, s)
        for s in range(1, 5):
            lows_add(1, s)
        if t:
            later(lambda: [rows_out(t - 1), names([1 - par])])

        def hook_y(at, t=t, par=par):
            if at[0] == "D":
                drip({"D1": 3, "D2": 3, "D3": 2}.get(at, 0))
            if at == "U1":
                drip(99)
            if t == 0 and at == "U2":
                drifts()
            if t == 2 and at == "c0":
                by_scalar(T.CL[:, 0, :], T.LO0[:, 0:4 * C], -1.0, ["LO00", "LO01"], ["CL0%d" % r for r in range(4)])
            if at == "U4":
                base(t, 1, 1, [0, 1, 2])
            if t and at == "U3":
                names_out(1 - par, t)
            if at == "m1":
                key_open(t)
                key_add(0, 1)
            if at == "c2":
                key_add(1, 1)
                if t == 2:
                    key_add(0, 0)
        highs(1, hook_y)
        greatest(t, 1, hook_y)
        under(1, hook_y)
        (pa, pk) = pa_of(1)
        if t < 2:
            folded_shift()
            least(1, wq(t + 1, 1, ay), wk(t + 1, ay, "h"), lambda k: k or low(0, 0))
            send("W%d_%dh" % (t + 1, ay), wk(t + 1, ay, "h"))
            own(t + 1, 0, 0)
            lay(t + 1, 0, [2])
            base(t + 1, 0, 0, [2])
            own(t + 1, 1, 0)
            own(t + 1, 1, 1)
            own(t + 1, 0, 1)
            drift(t)
            for x in range(2):
                for r in range(1 - x, 4):
                    low(x, r)
                key_add(x, 0, x == 1)
        else:
            def first_chunk(k, pa=pa_of(0)[0]):
                if k == 0:
                    low(1, 0)
                elif k == 1:
                    tt(wq(3, 0, 0), pa, T.AX[:], Op.add, ["pa0", "AX"], wk(3, 0, "l"), [6])
                    send("W3_0l", wk(3, 0, "l"))
                else:
                    tt(wq(3, 1, 0), T.AX[:], pa, Op.subtract, ["pa0", "AX"], wk(3, 0, "h"), [6])
            least(1, T.AB[:], ["AB"], first_chunk)
            tt(wq(3, 0, ay), pa, T.AB[:], Op.add, [pk, "AB"], wk(3, ay, "l"), [6])
            send("W3_%dl" % ay, wk(3, ay, "l"))
            for r in range(1, 4):
                low(1, r)
            key_add(1, 0, True)
            tt(wq(3, 1, ay), T.AB[:], pa, Op.subtract, [pk, "AB"], wk(3, ay, "h"), [6])
            send("W3_h", wk(3, ax, "h") + wk(3, ay, "h"))
            theta_out(1)
            theta_out(0)

    Z, D = LO, HI

    def prod(n, j, m=1):
        return T.W1[:, n & 1, 1024 * (1 + n // 2) + j * C:1024 * (1 + n // 2) + (j + m) * C]
    w3 = wkeys(3)

    def sources(n, a):
        act(D[n & 1][:, 0:4 * C], T.W3[:, 1, :].indirect(T.OFW[:, a >> 1, a & 1, :]), w3 + ["OFW%d" % (a & 1)],
            ["D%d" % (n & 1), "HI%d0" % (n & 1), "HI%d1" % (n & 1)], bias=0.0625, scale=0.5 / F, whole=["aW3", "bW3"])

    def diffs(n, a, hs=(0, 1)):
        par, x = a & 1, a >> 1
        ok = "OFW%d" % par
        for j in range(2 * hs[0], 2 * hs[-1] + 2):
            tt(Z[n & 1][:, j * C:(j + 1) * C], T.W3[:, 0, :].indirect(T.OFW[:, x, par, 16 * j:16 * j + 16]), T.SV[:, a * C:(a + 1) * C],
               Op.subtract, w3 + [ok, "SV%d" % a], ["Z%d%d" % (n & 1, j)] + (["LO%d0" % n, "LO%d1" % n] if n < 2 and j == 0 else []), whole=["aW3"])

    def sig(n, hs=(0, 1)):
        ps, b = region(n & 1, 0)
        for h in hs:
            act(ps[:, h * 512:(h + 1) * 512], Z[n & 1][:, h * 512:(h + 1) * 512], ["Z%d%d" % (n & 1, j) for j in (2 * h, 2 * h + 1)], (),
                [b + h], scale=0.5 / F, fn=Fn.Sigmoid)

    def weigh(n, a):
        ps, b = region(n & 1, 0)
        y = ps[:, 4 * C:5 * C]
        for js in ((0, 1), (2, 3)):
            v = slice(js[0] * C, (js[-1] + 1) * C)
            keys = ["P%d%d" % (n, j) for j in js]
            tt(prod(n, js[0], 2), ps[:, v], D[n & 1][:, v], Op.mult, ["D%d" % (n & 1)], keys + ["NA0", "NA1"], [b + js[0] // 2])
            if n:
                mm([(y, T.IF[:], prod(n, j), j == 0, j == 3) for j in js], ["IF"] + keys, [b + 2])
        if n == 0:
            v = slice(a * C, (a + 1) * C)
            fold("YQ_%d" % a, [prod(n, j) for j in range(4)] + [T.DH[:, v]], 1, ["P%d%d" % (n, j) for j in range(4)] + ["DH%d" % a], ["YQ%d" % a])

    def store(a):
        dma("S", T.yq[:, a * C:(a + 1) * C], T.YQ[:, a * C:(a + 1) * C], "out", ["YQ%d" % a])

    def weigh_last(n, a):
        (ps, b), d, dk = region(n & 1, 0), D[n & 1], "D%d" % (n & 1)
        y, v = ps[:, 4 * C:5 * C], slice(a * C, (a + 1) * C)
        row = [slice(j * C, (j + 1) * C) for j in range(4)]
        keys = ["P%d%d" % (n, j) for j in range(4)]
        mm([(y, T.IF[:], T.DH[:, v], True, False)], ["IF", "DH%d" % a], [b + 2])
        for j in range(3):
            tt(prod(n, j), ps[:, row[j]], d[:, row[j]], Op.mult, [dk], [keys[j]], [b + j // 2])
            if j < 2:
                mm([(y, T.IF[:], prod(n, j), False, j == 1)], ["IF", keys[j]], [b + 2])
        tt(ps[:, row[3]], ps[:, row[3]], d[:, row[3]], Op.mult, [dk], ["PL3"], [b + 1])
        tt(prod(n, 3), ps[:, row[3]], prod(n, 2), Op.add, ["PL3", keys[2]], [keys[3]], [b + 1])
        tt(T.YQ[:, v], y, prod(n, 3), Op.add, [keys[3]], ["YQ%d" % a], [b + 2])
        dma("S", T.yq[:, v], T.YQ[:, v], "out", ["YQ%d" % a])

    def y_out(n, a):
        ps, b = region(n & 1, 0)
        v = slice(a * C, (a + 1) * C)
        tt(T.YQ[:, v], ps[:, 4 * C:5 * C], T.DH[:, v], Op.add, ["DH%d" % a], ["YQ%d" % a], [b + 2])
        dma("S", T.yq[:, v], T.YQ[:, v], "out", ["YQ%d" % a])

    def refs_out():
        rk = ["R0", "R1"]
        ts(T.RD[:, 0, 2], T.R[:], -15.5, Op.add, rk, ["RD2"], BIG32, Op.add)
        act(T.FL[:, 0, 2], T.RD[:, 0, 2], ["RD2"], ["FL2"], bias=BIG32 / 2, scale=-0.5)
        act(T.S1[:, 0, 2], T.R[:], rk, ["S12"], bias=M1 - 0.5, scale=-1.0, fn=Fn.Sign)
        act(T.S2[:, 0, 2], T.R[:], rk, ["S22"], bias=M2 - 0.5, scale=-1.0, fn=Fn.Sign)
        out = PA[0:64, 0:128]
        group([(out, T.R[:], T.IF[:]), (out, T.FL[:, 0, 2], T.IP[:]), (out, T.S1[:, 0, 2], T.I8[:]), (out, T.S2[:, 0, 2], T.IC[:])],
              rk + ["FL2", "S12", "S22", "IF", "IP", "IC", "I8"], [6])

    def refs_store():
        ts(T.YR[0:64, :], PA[0:64, 0:128], -16.0, Op.add, (), ["YR"], bk=[6])
        for q in range(8):
            dma("S", T.yr[q, :], T.YR[0:64, 16 * q:16 * q + 16], "out", ["YR"])

    elect(2)
    answer(0)
    beside(2)
    hop_on(0)
    ask(2, 1)
    answer(1)
    hop_on(1)
    ask(2, 2)
    answer(2)
    sources(0, 1)
    diffs(0, 1, (0,))
    later(lambda: veto(2))
    drip(1)
    diffs(0, 1, (1,))
    sig(0)
    drip(99)
    rows_in(2)
    sources(1, 3)
    diffs(1, 3)
    sig(1)
    weigh(0, 1)
    refs_out()
    rows_out(2)
    sources(2, 0)
    weigh(1, 3)
    diffs(2, 0)
    sig(2)
    sources(3, 2)
    diffs(3, 2, (0,))
    y_out(1, 3)
    later(lambda: weigh_last(3, 2))
    drip(0)
    weigh(2, 0)
    sig(3, (0,))
    diffs(3, 2, (1,))
    sig(3, (1,))
    refs_store()
    store(1)
    drip(2)
    y_out(2, 0)
    drip(99)

    writer, readers, bank = {}, {}, {}
    deps = []
    for i, (q, fn, rd, wr, bk, dm, whole) in enumerate(ops):
        d = set()
        for k in rd:
            if k in writer:
                d.add(writer[k])
        for k in wr:
            for j in readers.get(k, []) + ([writer[k]] if k in writer else []):
                d.add(j)
        for b in bk:
            for q2, j in bank.get(b, {}).items():
                if q2 != q or q == "A":
                    d.add(j)
            bank.setdefault(b, {})[q] = i
        for k in rd:
            readers.setdefault(k, []).append(i)
        for k in wr:
            writer[k] = i
            readers[k] = []
        deps.append(d)
    seen = {q: {} for q in "VAPGS"}
    need = []
    for i, d in enumerate(deps):
        if ops[i][0] == "X":
            need.append([])
            continue
        mine, lst = seen[ops[i][0]], []
        newest = {}
        for j in d:
            if ops[j][5]:
                lst.append(ops[j][5][0])
            else:
                newest[ops[j][0]] = max(newest.get(ops[j][0], -1), j)
        keep = []
        for s in sorted(lst) + ops[i][6]:
            if s not in mine:
                mine[s] = 1
                keep.append(s)
        for q2, j in newest.items():
            if mine.get(q2, -1) < j:
                mine[q2] = j
                keep.append(j)
        need.append(keep)
    marked = sorted(set(k for keep in need for k in keep if isinstance(k, int)))
    count, value = {}, {}
    for j in marked:
        count[ops[j][0]] = count.get(ops[j][0], 0) + 1
        value[j] = count[ops[j][0]]
    queue = {"V": g.vector, "A": g.scalar, "P": g.tensor, "G": g, "S": g.sync}
    for i, o in enumerate(ops):
        if o[0] == "X":
            continue
        for k in need[i]:
            if isinstance(k, int):
                queue[o[0]].wait_ge(T.sem[ops[k][0]], value[k])
            else:
                queue[o[0]].wait_ge(T.sem[k], total[k])
        ins = o[1]()
        if i in value:
            ins.then_inc(T.sem[o[0]], 1)
    g.sync.wait_ge(T.sem.out, total["out"])
    g.wait_ge(T.sem.sent, total["sent"])
